import numpy as np
import ml_dtypes


def mxq(x, axis, fmt="e4m3"):
    dtype, down = {"e4m3": (ml_dtypes.float8_e4m3fn, 7), "e5m2": (ml_dtypes.float8_e5m2, 14)}[fmt]
    v = np.moveaxis(np.asarray(x, np.float32).astype(ml_dtypes.bfloat16).astype(np.float64), axis, -1)
    blocks = v.reshape(v.shape[:-1] + (-1, 32))
    amax = np.abs(blocks).max(-1, keepdims=True)
    byte = np.maximum(np.where(amax > 0, np.frexp(amax)[1] - 1 + 127, 0) - down, 1)
    scale = np.exp2(byte - 127.0)
    codes = (blocks / scale).astype(np.float32).astype(dtype).astype(np.float64)
    return np.moveaxis((codes * scale).reshape(v.shape), -1, axis)


WIDE = False


def mx_kscale(k):
    if not WIDE:
        return np.ones(k)
    levels = np.array([10, -10, 5, -5, 0])
    if k % 512:
        return np.exp2(np.random.permutation(np.resize(levels, k // 32))).repeat(32)
    a = np.empty((k // 512, 16))
    for p in range(k // 512):
        a[p, :8] = np.random.permutation(np.resize(levels, 8))
        for g in range(8):
            far = levels[np.abs(levels - a[p, g]) >= 10]
            a[p, g + 8] = far[np.random.randint(len(far))]
    return np.exp2(a.ravel()).repeat(32)


def f64(x):
    return np.asarray(x).astype(np.float64)


def striped(idx):
    return np.tile(idx.reshape(-1, 16).T, (8, 1)).astype(np.uint16)


def unstriped(offs):
    return offs[:16].T.reshape(-1).astype(np.int64)


E2M1 = np.array([0.0, 0.5, 1.0, 1.5, 2.0, 3.0, 4.0, 6.0, -0.0, -0.5, -1.0, -1.5, -2.0, -3.0, -4.0, -6.0])


def pack_weight(w, fmt):
    k, n = w.shape
    w = f64(np.asarray(w, np.float32).astype(ml_dtypes.bfloat16)).reshape(k // 32, 32, n)
    amax = np.abs(w).max(1)
    if fmt == "e4m3":
        byte = np.frexp(amax)[1] - 1 + 127 - 7
    else:
        mant, ex = np.frexp(amax / 6.0)
        byte = np.where(mant > 0.5, ex, ex - 1) + 127
    byte = np.clip(np.where(amax > 0, byte, 1), 1, 254)
    scaled = (w * np.exp2(127.0 - byte)[:, None, :]).reshape(k, n).astype(np.float32)
    by_word = np.ascontiguousarray(scaled.reshape(k // 512, 128, 4, n).transpose(0, 1, 3, 2))
    if fmt == "e4m3":
        words = by_word.astype(ml_dtypes.float8_e4m3fn).view(np.uint8)
    else:
        c = by_word.astype(ml_dtypes.float4_e2m1fn).view(np.uint8) & 0xF
        words = (c[..., 0::2] | (c[..., 1::2] << 4)).reshape(k // 512, 128, 2 * n)
    return np.ascontiguousarray(words), np.ascontiguousarray(byte.astype(np.uint8).reshape(k // 512, 16, n))


def unpack_weight(words, scales, fmt):
    g, _, n = scales.shape
    words = np.ascontiguousarray(words).reshape(g, 128, n, -1)
    if fmt == "e4m3":
        vals = words.view(ml_dtypes.float8_e4m3fn).astype(np.float64)
    else:
        nib = np.empty((g, 128, n, 4), np.uint8)
        nib[..., 0::2] = words & 0xF
        nib[..., 1::2] = words >> 4
        vals = E2M1[nib]
    vals = vals * np.repeat(np.exp2(scales.astype(np.float64) - 127.0), 8, axis=1)[..., None]
    return vals.transpose(0, 1, 3, 2).reshape(g * 512, n)


def gelu(v):
    return 0.5 * v * (1.0 + np.tanh(np.sqrt(2.0 / np.pi) * (v + 0.044715 * v**3)))


def bf(x):
    return np.asarray(x, np.float32).astype(ml_dtypes.bfloat16)


def planes(Y):
    n, m = Y.shape
    b = f64(bf(Y)).reshape(n // 32, 32, m)
    amax = np.abs(b).max(1)
    byte = np.clip(np.where(amax > 0, np.frexp(amax)[1] - 1 + 127 - 7, 1), 1, 254)
    codes = (b * np.exp2(127.0 - byte)[:, None, :]).reshape(n, m).astype(np.float32).astype(ml_dtypes.float8_e4m3fn).view(np.uint8)
    words = codes.reshape(n // 512, 128, 4, m).transpose(0, 1, 3, 2)
    return np.ascontiguousarray(words), np.ascontiguousarray(byte.astype(np.uint8).reshape(n // 512, 16, m))


K, H, N, T, S, T2, P = 1536, 1024, 512, 2048, 512, 1024, 512

def setup_inputs():
    n = np.random.standard_normal
    s = mx_kscale(K)[:, None]
    u = mx_kscale(H)[:, None]
    tab_words, tab_scales = pack_weight(n((K, T)) * s, "e4m3")
    w1 = (0.7 * n((K, H)) / np.sqrt(K) / s).astype(np.float32)
    w2_words, w2_scales = pack_weight(0.7 * n((K, H)) / np.sqrt(K) / s, "e2m1")
    w3 = 1.5 * n((H, N)) / np.sqrt(H) * np.exp(0.8 * n(N))[None, :] / u
    w3_words, w3_scales = pack_weight(w3, "e4m3")
    return {
        "tab_words": tab_words, "tab_scales": tab_scales,
        "offs": striped(np.random.permutation(T)[:S]),
        "w1": w1,
        "w2_words": w2_words, "w2_scales": w2_scales,
        "wgs": np.exp(0.3 * n((128, S))).astype(np.float32),
        "page0": np.square(n((H, T2))).astype(np.float32),
        "offs2": striped(np.random.permutation(T2)[:S]),
        "offs3": striped(np.random.permutation(T2)[:P]),
        "gain": (np.exp(0.3 * n(H)) * u[:, 0]).astype(np.float32),
        "w3_words": w3_words, "w3_scales": w3_scales,
    }

def reference(tab_words, tab_scales, offs, w1, w2_words, w2_scales, wgs, page0, offs2, offs3, gain, w3_words, w3_scales):
    v = unpack_weight(tab_words, tab_scales, "e4m3")[:, unstriped(offs)]
    w2 = unpack_weight(w2_words, w2_scales, "e2m1")
    w3 = unpack_weight(w3_words, w3_scales, "e4m3")
    d = (mxq(f64(w1), 0, "e4m3").T @ v) - (w2.T @ v)
    h = np.square(d)
    page = f64(page0).copy()
    page[:, unstriped(offs2)] = np.tile(f64(wgs), (H // 128, 1)) * h
    x = page[:, unstriped(offs3)]
    z = f64(gain)[:, None] * (1.0 / (1.0 + x))
    y = w3.T @ mxq(z, 0, "e4m3")
    words, scales = planes(y)
    return y, words, scales

@@ -1,0 +1,368 @@
+from contextlib import ExitStack
+
+import concourse.mybir as mybir
+from concourse.masks import make_identity
+
+K, H, N, T, S, T2, M = 1536, 1024, 512, 2048, 512, 1024, 512
+FLOPS = 2 * (2 * K * H * S + H * N * M)
+
+F32 = mybir.dt.float32
+BF16 = mybir.dt.bfloat16
+I32 = mybir.dt.int32
+U32 = mybir.dt.uint32
+U16 = mybir.dt.uint16
+U8 = mybir.dt.uint8
+FP8X4 = mybir.dt.float8_e4m3fn_x4
+FP4X4 = mybir.dt.float4_e2m1fn_x4
+ACT = mybir.ActivationFunctionType
+ALU = mybir.AluOpType
+
+P = 128
+KP = K // 512
+RT = H // P
+MC = M // P
+W1_CHUNKS = (256, 256, 256, 256)
+W2_FIRST = 256
+
+
+def tile_list_substitute_closeness_page_kernel(
+    tc, tab_words, tab_scales, offs, w1, w2_words, w2_scales, wgs, page0, offs2, offs3, gain,
+    w3_words, w3_scales, out_0, out_1, out_2,
+):
+    nc = tc.nc
+    with ExitStack() as ctx:
+        keep = ctx.enter_context(tc.tile_pool(name="keep", bufs=1))
+        ring = ctx.enter_context(tc.tile_pool(name="ring", bufs=3))
+        psum = ctx.enter_context(tc.psum_pool(name="psum", bufs=1))
+
+        def kept(shape, dtype, name, tag=None):
+            return keep.tile(shape, dtype, name=name, tag=tag or name, align_bytes=64)
+
+        def rot(shape, dtype, name, bufs=3):
+            return ring.tile(shape, dtype, name=name, align_bytes=64, bufs=bufs)
+
+        list1 = keep.tile([P, S // 16], U16, name="list1")
+        list2 = keep.tile([P, S // 16], U16, name="list2")
+        list3 = keep.tile([P, M // 16], U16, name="list3")
+
+        tab_sc = kept([P, T], U8, "tab_sc")
+        w2_sc = [kept([P, KP * W2_FIRST], U8, "w2_sca")]
+        v_sc = kept([P, S], U8, "v_sc")
+        v_low = [v_sc] + [kept([P, S], U8, "v_low%d" % a) for a in range(1, KP)]
+        w3_sc = kept([P, N], U8, "w3_sc")
+        gain_rows = kept([P, P], F32, "gain_rows")
+        nc.gpsimd.memset(tab_sc[:].bitcast(I32), 0)
+        for plane in [w2_sc[0], v_low[1], v_low[2]]:
+            nc.vector.memset(plane[:].bitcast(I32), 0)
+        nc.vector.memset(w3_sc[:].bitcast(I32), 0)
+        nc.vector.memset(gain_rows[:], 0.0)
+
+        ident_f = kept([P, P], F32, "ident_f")
+        ident_b = kept([P, P], BF16, "ident_b")
+
+        tab_w = [kept([P, T], I32, "tab_w%d" % a) for a in range(KP)]
+        pages = [kept([P, T2], F32, "page%d" % b) for b in range(RT)]
+        starts = [sum(W1_CHUNKS[:i]) for i in range(len(W1_CHUNKS))]
+        w1_raw = [[kept([P, 4, c], F32, "w1_raw%d_%d" % (i, a)) for a in range(KP)] for i, c in enumerate(W1_CHUNKS)]
+        w2_w = [kept([P, KP, 2 * W2_FIRST], U8, "w2_wa"), kept([P, KP, 2 * (H - W2_FIRST)], U8, "w2_wb")]
+        wgs_sb = kept([P, S], F32, "wgs_sb")
+        w3_w = kept([P, 2, N], I32, "w3_w")
+
+        def load_tab(a):
+            nc.sync.dma_start(out=tab_w[a][:], in_=tab_words[a].rearrange("p t i -> p (t i)").bitcast(I32))
+
+        def load_w1(i, passes=range(KP)):
+            for a in passes:
+                rows = w1[512 * a : 512 * (a + 1), starts[i] : starts[i] + W1_CHUNKS[i]]
+                nc.sync.dma_start(out=w1_raw[i][a][:], in_=rows.rearrange("(p j) c -> p j c", j=4))
+
+        def load_w2(h):
+            lo, hi = (0, 2 * W2_FIRST) if h == 0 else (2 * W2_FIRST, 2 * H)
+            nc.sync.dma_start(out=w2_w[h][:].bitcast(I32),
+                              in_=w2_words.rearrange("a p n -> p a n")[:, :, lo:hi].bitcast(I32))
+
+        def load_page(b):
+            nc.sync.dma_start(out=pages[b][:], in_=page0[P * b : P * (b + 1), :])
+
+        def load_w2_scales(h, queue):
+            lo, hi = (0, W2_FIRST) if h == 0 else (W2_FIRST, H)
+            for r in range(4):
+                queue.dma_start(
+                    out=w2_sc[h][r:P:32, :].bitcast(I32).rearrange("q (a c) -> q a c", a=KP),
+                    in_=w2_scales[:, r:16:4, lo:hi].rearrange("a q c -> q a c").bitcast(I32))
+
+        for q in range(4):
+            nc.gpsimd.dma_start(out=tab_sc[32 * q : 32 * q + 4 * KP, :].bitcast(I32),
+                                in_=tab_scales[:, 4 * q : 4 * q + 4, :].bitcast(I32))
+        load_w2_scales(0, nc.gpsimd)
+        nc.sync.dma_start(list1[:], offs)
+        load_tab(0)
+        load_w1(0, [0])
+        load_tab(1)
+        load_w1(0, [1])
+        warm = kept([P, 1], F32, "warm")
+        nc.scalar.activation(out=warm[:], in_=gain_rows[:, 0:1], func=ACT.Abs_reciprocal_sqrt, bias=1.0)
+        load_w2(0)
+        load_tab(2)
+        load_w1(0, [2])
+        nc.vector.tensor_copy(v_sc[:], tab_sc[:].indirect(list1[:]))
+        for a in range(1, KP):
+            nc.gpsimd.dma_start(out=v_low[a][0:112, :].bitcast(I32), in_=v_sc[4 * a : 4 * a + 112, :].bitcast(I32))
+        make_identity(nc, ident_f[:])
+        make_identity(nc, ident_b[:])
+        nc.sync.dma_start(out=wgs_sb[:], in_=wgs)
+        nc.sync.dma_start(list2[:], offs2)
+        load_page(0)
+        nc.sync.dma_start(list3[:], offs3)
+        nc.sync.dma_start(out=gain_rows[0:RT, :], in_=gain.rearrange("(b p) -> b p", p=P))
+        load_w1(1)
+        load_w2(1)
+        load_page(1)
+        load_w1(2)
+        load_page(2)
+        load_page(3)
+        load_w1(3)
+        load_page(4)
+        nc.sync.dma_start(out=w3_w[:], in_=w3_words.rearrange("a p c i -> p a (c i)").bitcast(I32))
+        for q in range(4):
+            nc.sync.dma_start(out=w3_sc[32 * q : 32 * q + 8, :].bitcast(I32),
+                              in_=w3_scales[:, 4 * q : 4 * q + 4, :].bitcast(I32))
+        load_page(5)
+        load_page(6)
+        load_page(7)
+
+        v_two = kept([P, 2 * S], U32, "v_w01", "tab_sc")
+        v_w = [v_two[:, 0:S], v_two[:, S : 2 * S]]
+
+        chunk_of = [max(n for n in range(len(starts)) if starts[n] <= P * b) for b in range(RT)]
+        grouped, w1_codes, w1_sc, d_tiles, h_tiles = {}, {}, {}, {}, {}
+
+        def h_tag(b):
+            return ("w1_raw0_2", "tab_w2")[b] if b < 2 else "r%d" % (b - 2)
+
+        def x_tag(b):
+            return "tab_w1" if b % 2 else "x0"
+
+        def cast_w1(b, a):
+            if b < 2:
+                grouped[b, a] = kept([P, 1, P, 4], BF16, "grouped%d_%d" % (b, a))[:]
+            elif a == 0:
+                whole = kept([P, KP, P, 4], BF16, "grouped%d" % b, "tab_w2" if b == 2 else x_tag(b))
+                grouped[b, 0], grouped[b, 1], grouped[b, 2] = whole[:], whole[:, 1:], whole[:, 2:]
+            lo = P * b - starts[chunk_of[b]]
+            nc.scalar.activation(
+                out=grouped[b, a][:, 0].rearrange("p (c i) j -> p c j i", i=4),
+                in_=w1_raw[chunk_of[b]][a][:, :, lo : lo + P].rearrange("p j (c i) -> p c j i", i=4),
+                func=ACT.Copy, scale=-1.0)
+
+        def codes_of(b, a, n=1):
+            if b < 2 and a == 2:
+                return w1_codes["late"][:, P * b : P * (b + 1)]
+            return w1_codes[b][:, P * a : P * (a + n)]
+
+        def quantise_w1(b, a, n=1):
+            if a == 0:
+                w1_codes[b] = kept([P, KP * P], U32, "w1_c%d" % b, ("tab_w0", "tab_w1", h_tag(0), h_tag(1))[b] if b < 4 else "zb%d" % (b - 4))
+                w1_sc[b] = kept([P, KP * P], U8, "w1_s%d" % b)
+            cols = slice(P * a, P * (a + n))
+            if (b, a) == (0, 2):
+                w1_codes["late"] = kept([P, 2 * P], U32, "w1_late", "tab_w2")
+            nc.vector.quantize_mx(out=codes_of(b, a, n).bitcast(FP8X4), scales=w1_sc[b][:, cols],
+                                  in_=grouped[b, a][:, 0:n].rearrange("p a c j -> p (a c j)"))
+
+        for a in range(KP):
+            if a == 2:
+                v_w.append(kept([P, S], U32, "v_w2", "grouped1_1")[:])
+            nc.vector.tensor_copy(v_w[a], tab_w[a][:].bitcast(U32).indirect(list1[:]))
+            for b in range(2):
+                cast_w1(b, a)
+                quantise_w1(b, a)
+
+        w2_sc.append(kept([P, KP * (H - W2_FIRST)], U8, "w2_scb", "grouped0_1"))
+        nc.vector.memset(w2_sc[1][:].bitcast(I32), 0)
+        load_w2_scales(1, nc.gpsimd)
+
+        gain_sb = kept([P, RT], F32, "gain_sb")
+
+        def spread_gain():
+            gain_ps = psum.tile([P, P], F32, name="gain_ps", tag="bank_a")
+            nc.tensor.transpose(gain_ps[:], gain_rows[:], ident_f[:])
+            nc.scalar.copy(out=gain_sb[:], in_=gain_ps[:, 0:RT])
+
+        def first_stage(b):
+            col = P * b
+            half = 0 if col < W2_FIRST else 1
+            lo1 = col - half * W2_FIRST
+            lo2 = 2 * lo1
+            wide = (W2_FIRST, H - W2_FIRST)[half]
+            d = psum.tile([P, S], F32, name="d", tag="bank_a")
+            order = ((1, 0), (2, 0), (1, 1), (2, 1), (2, 2), (1, 2)) if b < 2 else [(w, a) for w in (1, 2) for a in range(KP)]
+            for n, (which, a) in enumerate(order):
+                cols = slice(P * a, P * (a + 1))
+                flags = dict(start=(n == 0), stop=(n == len(order) - 1))
+                if which == 2:
+                    nc.tensor.matmul_mx(
+                        out=d[:], lhsT=w2_w[half][:, a, lo2 : lo2 + 2 * P].bitcast(FP4X4),
+                        lhsT_scale=w2_sc[half][:, a * wide + lo1 : a * wide + lo1 + P],
+                        rhs=v_w[a].bitcast(FP8X4), rhs_scale=v_low[a][:], **flags)
+                else:
+                    nc.tensor.matmul_mx(
+                        out=d[:], lhsT=codes_of(b, a).bitcast(FP8X4), lhsT_scale=w1_sc[b][:, cols],
+                        rhs=v_w[a].bitcast(FP8X4), rhs_scale=v_sc[4 * a :, :], **flags)
+            d_tiles[b] = d
+
+        def square(b):
+            h_tiles[b] = kept([P, S], F32, "h%d" % b, h_tag(b))
+            nc.scalar.activation(out=h_tiles[b][:], in_=d_tiles[b][:], func=ACT.Square)
+
+        def scatter(b):
+            nc.vector.tensor_tensor(pages[b][:].indirect(list2[:]), h_tiles[b][:], wgs_sb[:], ALU.mult)
+
+        z_t = [kept([P, MC, 2, P], F32, "z_t%d" % g) for g in range(2)]
+
+        x_tiles, z_tiles = {}, {}
+
+        def gather(b):
+            x_tiles[b] = kept([P, M], F32, "x%d" % b, x_tag(b))
+            nc.vector.tensor_copy(x_tiles[b][:], pages[b][:].indirect(list3[:]))
+
+        def closeness(b):
+            x = x_tiles[b]
+            u = kept([P, M], F32, "u%d" % b, "za%d" % (b - 1) if b else None)
+            nc.scalar.activation(out=u[:], in_=x[:], func=ACT.Abs_reciprocal_sqrt, bias=1.0)
+            r = kept([P, M], F32, "r%d" % b)
+            nc.scalar.activation(out=r[:], in_=u[:], func=ACT.Square)
+            z_tiles[b] = [kept([P, M // 2], BF16, "z%s%d" % (name, b)) for name in "ab"]
+            for i in range(2):
+                nc.scalar.activation(out=z_tiles[b][i][:], in_=r[:, i * M // 2 : (i + 1) * M // 2], func=ACT.Copy,
+                                     scale=gain_sb[:, b : b + 1])
+
+        def turn(b):
+            z = z_tiles[b]
+            turned = psum.tile([P, MC, P], BF16, name="turned", tag="bank_a" if b < 5 else ("bank_b", "bank_c")[b - 5])
+            for c in range(MC):
+                nc.tensor.transpose(turned[:, c, :], z[c // 2][:, P * (c % 2) : P * (c % 2 + 1)], ident_b[:])
+            lo = 32 * (b % 4)
+            nc.scalar.copy(
+                out=z_t[b // 4][:, :, :, lo : lo + 32],
+                in_=turned[:].rearrange("m c r -> m (c r)").bitcast(F32).rearrange("m (c p u) -> m c u p", c=MC, u=2))
+
+        w3_wp = kept([P, 2, N], I32, "w3_wp", "w1_raw3_0")
+        w3_sp = kept([P, N], U8, "w3_sp", "w1_raw3_1")
+
+        def deal_w3():
+            nc.vector.tensor_copy(out=w3_wp[:].rearrange("p a (t m) -> p a t m", t=4),
+                                  in_=w3_w[:].rearrange("p a (m t) -> p a t m", t=4))
+            nc.vector.tensor_copy(out=w3_sp[:].rearrange("p (t m) -> p t m", t=4),
+                                  in_=w3_sc[:].rearrange("p (m t) -> p t m", t=4))
+
+        y_ps = [psum.tile([P, 4, P], F32, name="y%d" % c, tag="y%d" % c) for c in range(MC)]
+
+        def second_stage(g, c, codes, scales):
+            for t in range(4):
+                nc.tensor.matmul_mx(
+                    out=y_ps[c][:, t, :], lhsT=w3_wp[:, g, P * t : P * (t + 1)].bitcast(FP8X4),
+                    lhsT_scale=w3_sp[4 * g :, P * t : P * (t + 1)],
+                    rhs=codes.bitcast(FP8X4), rhs_scale=scales,
+                    start=(g == 0 and t == 0), stop=(g == 1 and t == 3))
+
+        zq = kept([P, M, 2], F32, "zq0")
+
+        def turn_back_first_half():
+            for pair in range(MC // 2):
+                back = psum.tile([P, 2, 2, P], F32, name="back", tag=("bank_b", "bank_c")[pair])
+                for c in range(2):
+                    for u in range(2):
+                        nc.tensor.transpose(back[:, c, u, :], z_t[0][:, 2 * pair + c, u, :], ident_f[:])
+                nc.scalar.copy(
+                    out=zq[:, 2 * P * pair : 2 * P * (pair + 1), :].rearrange("p (c m) u -> p c m u", c=2),
+                    in_=back[:].rearrange("p c u m -> p c m u"))
+
+        def first_half_of_y():
+            codes = kept([P, M], U32, "z_codes0", "zb3")
+            scales = kept([P, M], U8, "z_sc0")
+            nc.vector.quantize_mx(out=codes[:].bitcast(FP8X4), scales=scales[:],
+                                  in_=zq[:].rearrange("p m u -> p (m u)").bitcast(BF16))
+            for c in range(MC):
+                second_stage(0, c, codes[:, P * c : P * (c + 1)], scales[:, P * c : P * (c + 1)])
+
+        first_stage(0)
+        square(0)
+        first_stage(1)
+        for a in range(KP):
+            cast_w1(2, a)
+            cast_w1(3, a)
+        for b in range(RT - 1):
+            scatter(b)
+            if b + 2 < RT:
+                quantise_w1(b + 2, 0, 2)
+                quantise_w1(b + 2, 2)
+            if b == 0:
+                square(1)
+                spread_gain()
+            if b == 4:
+                deal_w3()
+                turn_back_first_half()
+            gather(b)
+            if b + 2 < RT:
+                first_stage(b + 2)
+            if b == 5:
+                first_half_of_y()
+            closeness(b)
+            if b + 2 < RT:
+                square(b + 2)
+            turn(b)
+            if b + 4 < RT:
+                for a in range(KP):
+                    cast_w1(b + 4, a)
+
+        last = RT - 1
+        scatter(last)
+        y_codes = kept([P, M], U32, "y_codes")
+        y_sc = kept([P, M], U8, "y_sc")
+        out_rows = out_0.rearrange("(p t) m -> p t m", t=4)
+        out_words = out_1[0].rearrange("p m t -> p (m t)").bitcast(I32)
+        zs = []
+        u_last = kept([P, M], F32, "u_last", "za%d" % (last - 1))
+        for c in range(MC):
+            x = kept([P, P], F32, "xl%d" % c)
+            nc.vector.tensor_copy(x[:], pages[last][:].indirect(list3[:, 8 * c : 8 * (c + 1)]))
+            u = u_last[:, P * c : P * (c + 1)]
+            nc.scalar.activation(out=u, in_=x[:], func=ACT.Abs_reciprocal_sqrt, bias=1.0)
+            zs.append(u)
+        for c in range(MC):
+            u = zs[c]
+            z = kept([P, P], BF16, "zl%d" % c)
+            nc.vector.scalar_tensor_tensor(out=z[:], in0=u, scalar=gain_sb[:, last : last + 1], in1=u,
+                                           op0=ALU.mult, op1=ALU.mult)
+            turned = psum.tile([P, P], BF16, name="turned_l", tag=("bank_b", "bank_c")[c % 2])
+            nc.tensor.transpose(turned[:], z[:], ident_b[:])
+            nc.scalar.copy(out=z_t[1][:, c, :, 96:128],
+                           in_=turned[:].bitcast(F32).rearrange("m (p u) -> m u p", u=2))
+            back = psum.tile([P, 2, P], F32, name="back_l", tag=("bank_d", "bank_a")[c % 2])
+            for u in range(2):
+                nc.tensor.transpose(back[:, u, :], z_t[1][:, c, u, :], ident_f[:])
+            zq1 = kept([P, P, 2], F32, "zq1_%d" % c)
+            nc.scalar.copy(out=zq1[:], in_=back[:].rearrange("p u m -> p m u"))
+            codes = kept([P, P], U32, "z_codes1_%d" % c)
+            scales = kept([P, P], U8, "z_sc1_%d" % c)
+            nc.vector.quantize_mx(out=codes[:].bitcast(FP8X4), scales=scales[:],
+                                  in_=zq1[:].rearrange("p m u -> p (m u)").bitcast(BF16))
+            second_stage(1, c, codes[:], scales[:])
+        for c in range(MC):
+            cols = slice(P * c, P * (c + 1))
+            y = kept([P, 4, P], F32, "y_sb%d" % c)
+            nc.scalar.copy(out=y[:], in_=y_ps[c][:])
+            nc.sync.dma_start(out=out_rows[:, :, cols], in_=y[:])
+            yb = kept([P, P, 4], BF16, "yb%d" % c)
+            nc.vector.tensor_copy(out=yb[:].rearrange("p (m i) t -> p m t i", i=4),
+                                  in_=y[:].rearrange("p t (m i) -> p m t i", i=4))
+            nc.vector.quantize_mx(out=y_codes[:, cols].bitcast(FP8X4), scales=y_sc[:, cols],
+                                  in_=yb[:].rearrange("p m t -> p (m t)"))
+            if c % 2 == 1:
+                both = slice(P * (c - 1), P * (c + 1))
+                nc.sync.dma_start(out=out_words[:, both], in_=y_codes[:, both].bitcast(I32))
+        for q in range(4):
+            queue = nc.scalar if q % 2 else nc.sync
+            queue.dma_start(out=out_2[0, 4 * q : 4 * q + 4, :].bitcast(I32),
+                            in_=y_sc[32 * q : 32 * q + 4, :].bitcast(I32))

@@ -45,15 +45,15 @@ def tile_list_substitute_closeness_page_kernel(
         list2 = keep.tile([P, S // 16], U16, name="list2")
         list3 = keep.tile([P, M // 16], U16, name="list3")
 
-        tab_sc = kept([P, T], U8, "tab_sc")
-        w2_sc = [kept([P, KP * W2_FIRST], U8, "w2_sca")]
-        v_sc = kept([P, S], U8, "v_sc")
-        v_low = [v_sc] + [kept([P, S], U8, "v_low%d" % a) for a in range(1, KP)]
+        tab_sc = kept([P, KP * T], U8, "tab_sc")
+        w2_sc = [kept([P, KP * W2_FIRST], U8, "w2_sca"), kept([P, KP * (H - W2_FIRST)], U8, "w2_scb")]
+        v_sc = [kept([P, S], U8, "v_sc%d" % a) for a in range(KP)]
         w3_sc = kept([P, N], U8, "w3_sc")
         gain_rows = kept([P, P], F32, "gain_rows")
-        nc.gpsimd.memset(tab_sc[:].bitcast(I32), 0)
-        for plane in [w2_sc[0], v_low[1], v_low[2]]:
-            nc.vector.memset(plane[:].bitcast(I32), 0)
+        nc.gpsimd.memset(tab_sc[:, 0:T].bitcast(I32), 0)
+        nc.vector.memset(tab_sc[:, T:].bitcast(I32), 0)
+        nc.vector.memset(w2_sc[0][:].bitcast(I32), 0)
+        nc.vector.memset(w2_sc[1][:].bitcast(I32), 0)
         nc.vector.memset(w3_sc[:].bitcast(I32), 0)
         nc.vector.memset(gain_rows[:], 0.0)
 
@@ -91,38 +91,34 @@ def tile_list_substitute_closeness_page_kernel(
                     out=w2_sc[h][r:P:32, :].bitcast(I32).rearrange("q (a c) -> q a c", a=KP),
                     in_=w2_scales[:, r:16:4, lo:hi].rearrange("a q c -> q a c").bitcast(I32))
 
-        for q in range(4):
-            nc.gpsimd.dma_start(out=tab_sc[32 * q : 32 * q + 4 * KP, :].bitcast(I32),
-                                in_=tab_scales[:, 4 * q : 4 * q + 4, :].bitcast(I32))
-        load_w2_scales(0, nc.gpsimd)
         nc.sync.dma_start(list1[:], offs)
         load_tab(0)
+        nc.sync.dma_start(list2[:], offs2)
+        for r in range(4):
+            nc.sync.dma_start(out=tab_sc[r:P:32, :].bitcast(I32).rearrange("q (a c) -> q a c", a=KP),
+                              in_=tab_scales[:, r:16:4, :].rearrange("a q c -> q a c").bitcast(I32))
         load_w1(0, [0])
         load_tab(1)
+        load_w2_scales(0, nc.sync)
         load_w1(0, [1])
-        warm = kept([P, 1], F32, "warm")
-        nc.scalar.activation(out=warm[:], in_=gain_rows[:, 0:1], func=ACT.Abs_reciprocal_sqrt, bias=1.0)
         load_w2(0)
         load_tab(2)
         load_w1(0, [2])
-        nc.vector.tensor_copy(v_sc[:], tab_sc[:].indirect(list1[:]))
-        for a in range(1, KP):
-            nc.gpsimd.dma_start(out=v_low[a][0:112, :].bitcast(I32), in_=v_sc[4 * a : 4 * a + 112, :].bitcast(I32))
         make_identity(nc, ident_f[:])
         make_identity(nc, ident_b[:])
         nc.sync.dma_start(out=wgs_sb[:], in_=wgs)
-        nc.sync.dma_start(list2[:], offs2)
         load_page(0)
+        load_w1(1)
         nc.sync.dma_start(list3[:], offs3)
         nc.sync.dma_start(out=gain_rows[0:RT, :], in_=gain.rearrange("(b p) -> b p", p=P))
-        load_w1(1)
         load_w2(1)
         load_page(1)
-        load_w1(2)
+        load_w2_scales(1, nc.sync)
         load_page(2)
+        load_w1(2)
         load_page(3)
-        load_w1(3)
         load_page(4)
+        load_w1(3)
         nc.sync.dma_start(out=w3_w[:], in_=w3_words.rearrange("a p c i -> p a (c i)").bitcast(I32))
         for q in range(4):
             nc.sync.dma_start(out=w3_sc[32 * q : 32 * q + 8, :].bitcast(I32),
@@ -131,24 +127,34 @@ def tile_list_substitute_closeness_page_kernel(
         load_page(6)
         load_page(7)
 
-        v_two = kept([P, 2 * S], U32, "v_w01", "tab_sc")
-        v_w = [v_two[:, 0:S], v_two[:, S : 2 * S]]
+        v_w = [kept([P, S], U32, "v_w%d" % a)[:] for a in range(2)]
 
         chunk_of = [max(n for n in range(len(starts)) if starts[n] <= P * b) for b in range(RT)]
         grouped, w1_codes, w1_sc, d_tiles, h_tiles = {}, {}, {}, {}, {}
 
         def h_tag(b):
-            return ("w1_raw0_2", "tab_w2")[b] if b < 2 else "r%d" % (b - 2)
+            return ("h0", "w1_raw1_2")[b] if b < 2 else "r%d" % (b - 2)
+
+        def u_tag(b):
+            return {0: "u0", 1: "w1_raw2_2", 3: "w1_raw3_2"}.get(b, "z%d" % (b - 1))
+
+        def codes_tag(b):
+            return ("tab_w0", "grouped0_2", h_tag(0), h_tag(1))[b] if b < 4 else (u_tag(b - 3) if b % 2 else h_tag(b - 2))
+
+        def bank(b):
+            return ("bank_a", "bank_b")[b % 2]
 
         def x_tag(b):
-            return "tab_w1" if b % 2 else "x0"
+            return "grouped2_12" if b == 0 else "grouped%d_0" % (b + 2)
 
         def cast_w1(b, a):
             if b < 2:
                 grouped[b, a] = kept([P, 1, P, 4], BF16, "grouped%d_%d" % (b, a))[:]
             elif a == 0:
-                whole = kept([P, KP, P, 4], BF16, "grouped%d" % b, "tab_w2" if b == 2 else x_tag(b))
-                grouped[b, 0], grouped[b, 1], grouped[b, 2] = whole[:], whole[:, 1:], whole[:, 2:]
+                grouped[b, 0] = kept([P, 1, P, 4], BF16, "grouped%d_0" % b, "tab_w2" if b == 2 else None)[:]
+            elif a == 1:
+                both = kept([P, 2, P, 4], BF16, "grouped%d_12" % b)
+                grouped[b, 1], grouped[b, 2] = both[:], both[:, 1:]
             lo = P * b - starts[chunk_of[b]]
             nc.scalar.activation(
                 out=grouped[b, a][:, 0].rearrange("p (c i) j -> p c j i", i=4),
@@ -156,31 +162,31 @@ def tile_list_substitute_closeness_page_kernel(
                 func=ACT.Copy, scale=-1.0)
 
         def codes_of(b, a, n=1):
-            if b < 2 and a == 2:
-                return w1_codes["late"][:, P * b : P * (b + 1)]
+            if (b, a) == (0, 2):
+                return w1_codes["late"][:]
             return w1_codes[b][:, P * a : P * (a + n)]
 
         def quantise_w1(b, a, n=1):
             if a == 0:
-                w1_codes[b] = kept([P, KP * P], U32, "w1_c%d" % b, ("tab_w0", "tab_w1", h_tag(0), h_tag(1))[b] if b < 4 else "zb%d" % (b - 4))
+                w1_codes[b] = kept([P, KP * P], U32, "w1_c%d" % b, codes_tag(b))
                 w1_sc[b] = kept([P, KP * P], U8, "w1_s%d" % b)
             cols = slice(P * a, P * (a + n))
             if (b, a) == (0, 2):
-                w1_codes["late"] = kept([P, 2 * P], U32, "w1_late", "tab_w2")
+                w1_codes["late"] = kept([P, P], U32, "w1_late", "tab_w2")
             nc.vector.quantize_mx(out=codes_of(b, a, n).bitcast(FP8X4), scales=w1_sc[b][:, cols],
                                   in_=grouped[b, a][:, 0:n].rearrange("p a c j -> p (a c j)"))
 
         for a in range(KP):
             if a == 2:
-                v_w.append(kept([P, S], U32, "v_w2", "grouped1_1")[:])
+                v_w.append(kept([P, S], U32, "v_w2", "grouped0_1")[:])
+            nc.vector.tensor_copy(v_sc[a][:], tab_sc[:, a * T : (a + 1) * T].indirect(list1[:]))
             nc.vector.tensor_copy(v_w[a], tab_w[a][:].bitcast(U32).indirect(list1[:]))
-            for b in range(2):
-                cast_w1(b, a)
-                quantise_w1(b, a)
+            cast_w1(0, a)
+            quantise_w1(0, a)
+            cast_w1(1, a)
+        for a in range(KP):
+            quantise_w1(1, a)
 
-        w2_sc.append(kept([P, KP * (H - W2_FIRST)], U8, "w2_scb", "grouped0_1"))
-        nc.vector.memset(w2_sc[1][:].bitcast(I32), 0)
-        load_w2_scales(1, nc.gpsimd)
 
         gain_sb = kept([P, RT], F32, "gain_sb")
 
@@ -195,7 +201,7 @@ def tile_list_substitute_closeness_page_kernel(
             lo1 = col - half * W2_FIRST
             lo2 = 2 * lo1
             wide = (W2_FIRST, H - W2_FIRST)[half]
-            d = psum.tile([P, S], F32, name="d", tag="bank_a")
+            d = psum.tile([P, S], F32, name="d", tag=bank(b))
             order = ((1, 0), (2, 0), (1, 1), (2, 1), (2, 2), (1, 2)) if b < 2 else [(w, a) for w in (1, 2) for a in range(KP)]
             for n, (which, a) in enumerate(order):
                 cols = slice(P * a, P * (a + 1))
@@ -204,11 +210,11 @@ def tile_list_substitute_closeness_page_kernel(
                     nc.tensor.matmul_mx(
                         out=d[:], lhsT=w2_w[half][:, a, lo2 : lo2 + 2 * P].bitcast(FP4X4),
                         lhsT_scale=w2_sc[half][:, a * wide + lo1 : a * wide + lo1 + P],
-                        rhs=v_w[a].bitcast(FP8X4), rhs_scale=v_low[a][:], **flags)
+                        rhs=v_w[a].bitcast(FP8X4), rhs_scale=v_sc[a][:], **flags)
                 else:
                     nc.tensor.matmul_mx(
                         out=d[:], lhsT=codes_of(b, a).bitcast(FP8X4), lhsT_scale=w1_sc[b][:, cols],
-                        rhs=v_w[a].bitcast(FP8X4), rhs_scale=v_sc[4 * a :, :], **flags)
+                        rhs=v_w[a].bitcast(FP8X4), rhs_scale=v_sc[a][:], **flags)
             d_tiles[b] = d
 
         def square(b):
@@ -223,46 +229,57 @@ def tile_list_substitute_closeness_page_kernel(
         x_tiles, z_tiles = {}, {}
 
         def gather(b):
-            x_tiles[b] = kept([P, M], F32, "x%d" % b, x_tag(b))
+            x_tiles[b] = kept([P, M], F32, "x%d" % b, x_tag(b) if b < RT - 2 else "zq0")
             nc.vector.tensor_copy(x_tiles[b][:], pages[b][:].indirect(list3[:]))
 
         def closeness(b):
             x = x_tiles[b]
-            u = kept([P, M], F32, "u%d" % b, "za%d" % (b - 1) if b else None)
+            u = kept([P, M], F32, "u%d" % b, u_tag(b))
             nc.scalar.activation(out=u[:], in_=x[:], func=ACT.Abs_reciprocal_sqrt, bias=1.0)
             r = kept([P, M], F32, "r%d" % b)
             nc.scalar.activation(out=r[:], in_=u[:], func=ACT.Square)
-            z_tiles[b] = [kept([P, M // 2], BF16, "z%s%d" % (name, b)) for name in "ab"]
-            for i in range(2):
-                nc.scalar.activation(out=z_tiles[b][i][:], in_=r[:, i * M // 2 : (i + 1) * M // 2], func=ACT.Copy,
-                                     scale=gain_sb[:, b : b + 1])
+            z_tiles[b] = kept([P, M], BF16, "z%d" % b)
+            nc.scalar.activation(out=z_tiles[b][:], in_=r[:], func=ACT.Copy, scale=gain_sb[:, b : b + 1])
+
+        def turn_chunk(z, c, lo, tag):
+            turned = psum.tile([P, P], BF16, name="turned_c", tag=tag)
+            nc.tensor.transpose(turned[:], z, ident_b[:])
+            nc.scalar.copy(out=z_t[1][:, c, :, lo : lo + 32],
+                           in_=turned[:].bitcast(F32).rearrange("m (p u) -> m u p", u=2))
 
         def turn(b):
             z = z_tiles[b]
-            turned = psum.tile([P, MC, P], BF16, name="turned", tag="bank_a" if b < 5 else ("bank_b", "bank_c")[b - 5])
-            for c in range(MC):
-                nc.tensor.transpose(turned[:, c, :], z[c // 2][:, P * (c % 2) : P * (c % 2 + 1)], ident_b[:])
             lo = 32 * (b % 4)
+            if b == RT - 3:
+                for c in range(MC):
+                    turn_chunk(z[:, P * c : P * (c + 1)], c, lo, "y%d" % c)
+                return
+            turned = psum.tile([P, MC, P], BF16, name="turned", tag=bank(b + 1))
+            for c in range(MC):
+                nc.tensor.transpose(turned[:, c, :], z[:, P * c : P * (c + 1)], ident_b[:])
             nc.scalar.copy(
                 out=z_t[b // 4][:, :, :, lo : lo + 32],
                 in_=turned[:].rearrange("m c r -> m (c r)").bitcast(F32).rearrange("m (c p u) -> m c u p", c=MC, u=2))
 
-        w3_wp = kept([P, 2, N], I32, "w3_wp", "w1_raw3_0")
-        w3_sp = kept([P, N], U8, "w3_sp", "w1_raw3_1")
+        w3_dealt = {}
 
-        def deal_w3():
-            nc.vector.tensor_copy(out=w3_wp[:].rearrange("p a (t m) -> p a t m", t=4),
-                                  in_=w3_w[:].rearrange("p a (m t) -> p a t m", t=4))
-            nc.vector.tensor_copy(out=w3_sp[:].rearrange("p (t m) -> p t m", t=4),
+        def deal_w3_words(g, tag):
+            w3_dealt[g] = kept([P, N], I32, "w3_dealt%d" % g, tag)
+            nc.vector.tensor_copy(out=w3_dealt[g][:].rearrange("p (t m) -> p t m", t=4),
+                                  in_=w3_w[:, g, :].rearrange("p (m t) -> p t m", t=4))
+
+        def deal_w3_scales(tag):
+            w3_dealt["scales"] = kept([P, N], U8, "w3_sp", tag)
+            nc.vector.tensor_copy(out=w3_dealt["scales"][:].rearrange("p (t m) -> p t m", t=4),
                                   in_=w3_sc[:].rearrange("p (m t) -> p t m", t=4))
 
-        y_ps = [psum.tile([P, 4, P], F32, name="y%d" % c, tag="y%d" % c) for c in range(MC)]
+        y_ps = []
 
         def second_stage(g, c, codes, scales):
             for t in range(4):
                 nc.tensor.matmul_mx(
-                    out=y_ps[c][:, t, :], lhsT=w3_wp[:, g, P * t : P * (t + 1)].bitcast(FP8X4),
-                    lhsT_scale=w3_sp[4 * g :, P * t : P * (t + 1)],
+                    out=y_ps[c][:, t, :], lhsT=w3_dealt[g][:, P * t : P * (t + 1)].bitcast(FP8X4),
+                    lhsT_scale=w3_dealt["scales"][4 * g :, P * t : P * (t + 1)],
                     rhs=codes.bitcast(FP8X4), rhs_scale=scales,
                     start=(g == 0 and t == 0), stop=(g == 1 and t == 3))
 
@@ -270,7 +287,7 @@ def tile_list_substitute_closeness_page_kernel(
 
         def turn_back_first_half():
             for pair in range(MC // 2):
-                back = psum.tile([P, 2, 2, P], F32, name="back", tag=("bank_b", "bank_c")[pair])
+                back = psum.tile([P, 2, 2, P], F32, name="back", tag=("bank_c", "bank_d")[pair])
                 for c in range(2):
                     for u in range(2):
                         nc.tensor.transpose(back[:, c, u, :], z_t[0][:, 2 * pair + c, u, :], ident_f[:])
@@ -279,42 +296,45 @@ def tile_list_substitute_closeness_page_kernel(
                     in_=back[:].rearrange("p c u m -> p c m u"))
 
         def first_half_of_y():
-            codes = kept([P, M], U32, "z_codes0", "zb3")
+            codes = kept([P, M], U32, "z_codes0", u_tag(RT - 3))
             scales = kept([P, M], U8, "z_sc0")
             nc.vector.quantize_mx(out=codes[:].bitcast(FP8X4), scales=scales[:],
                                   in_=zq[:].rearrange("p m u -> p (m u)").bitcast(BF16))
             for c in range(MC):
+                y_ps.append(psum.tile([P, 4, P], F32, name="y%d" % c, tag="y%d" % c))
                 second_stage(0, c, codes[:, P * c : P * (c + 1)], scales[:, P * c : P * (c + 1)])
 
         first_stage(0)
         square(0)
         first_stage(1)
-        for a in range(KP):
-            cast_w1(2, a)
-            cast_w1(3, a)
+        for b in (2, 3):
+            for a in range(KP):
+                cast_w1(b, a)
         for b in range(RT - 1):
             scatter(b)
             if b + 2 < RT:
-                quantise_w1(b + 2, 0, 2)
-                quantise_w1(b + 2, 2)
+                quantise_w1(b + 2, 0)
+                quantise_w1(b + 2, 1, 2)
             if b == 0:
                 square(1)
                 spread_gain()
             if b == 4:
-                deal_w3()
+                deal_w3_words(0, "w1_raw3_0")
+                deal_w3_scales("w1_raw3_1")
                 turn_back_first_half()
+            if b == 6:
+                first_half_of_y()
             gather(b)
             if b + 2 < RT:
                 first_stage(b + 2)
-            if b == 5:
-                first_half_of_y()
             closeness(b)
             if b + 2 < RT:
                 square(b + 2)
             turn(b)
-            if b + 4 < RT:
+            if b in (0, 2):
                 for a in range(KP):
                     cast_w1(b + 4, a)
+                    cast_w1(b + 5, a)
 
         last = RT - 1
         scatter(last)
@@ -322,46 +342,42 @@ def tile_list_substitute_closeness_page_kernel(
         y_sc = kept([P, M], U8, "y_sc")
         out_rows = out_0.rearrange("(p t) m -> p t m", t=4)
         out_words = out_1[0].rearrange("p m t -> p (m t)").bitcast(I32)
-        zs = []
-        u_last = kept([P, M], F32, "u_last", "za%d" % (last - 1))
+        u_last = kept([P, M], F32, "u_last", u_tag(last))
+        banks = ("bank_c", "bank_a", "bank_d", "bank_b")
+        xs = [kept([P, P], F32, "xl%d" % c) for c in range(MC)]
+        zs = [kept([P, P], BF16, "zl%d" % c) for c in range(MC)]
+        zq1 = [kept([P, P, 2], F32, "zq1_%d" % c) for c in range(MC)]
+        chunks = [slice(P * c, P * (c + 1)) for c in range(MC)]
         for c in range(MC):
-            x = kept([P, P], F32, "xl%d" % c)
-            nc.vector.tensor_copy(x[:], pages[last][:].indirect(list3[:, 8 * c : 8 * (c + 1)]))
-            u = u_last[:, P * c : P * (c + 1)]
-            nc.scalar.activation(out=u, in_=x[:], func=ACT.Abs_reciprocal_sqrt, bias=1.0)
-            zs.append(u)
+            nc.vector.tensor_copy(xs[c][:], pages[last][:].indirect(list3[:, 8 * c : 8 * (c + 1)]))
+            nc.scalar.activation(out=u_last[:, chunks[c]], in_=xs[c][:], func=ACT.Abs_reciprocal_sqrt, bias=1.0)
         for c in range(MC):
-            u = zs[c]
-            z = kept([P, P], BF16, "zl%d" % c)
-            nc.vector.scalar_tensor_tensor(out=z[:], in0=u, scalar=gain_sb[:, last : last + 1], in1=u,
+            u = u_last[:, chunks[c]]
+            nc.vector.scalar_tensor_tensor(out=zs[c][:], in0=u, scalar=gain_sb[:, last : last + 1], in1=u,
                                            op0=ALU.mult, op1=ALU.mult)
-            turned = psum.tile([P, P], BF16, name="turned_l", tag=("bank_b", "bank_c")[c % 2])
-            nc.tensor.transpose(turned[:], z[:], ident_b[:])
-            nc.scalar.copy(out=z_t[1][:, c, :, 96:128],
-                           in_=turned[:].bitcast(F32).rearrange("m (p u) -> m u p", u=2))
-            back = psum.tile([P, 2, P], F32, name="back_l", tag=("bank_d", "bank_a")[c % 2])
-            for u in range(2):
-                nc.tensor.transpose(back[:, u, :], z_t[1][:, c, u, :], ident_f[:])
-            zq1 = kept([P, P, 2], F32, "zq1_%d" % c)
-            nc.scalar.copy(out=zq1[:], in_=back[:].rearrange("p u m -> p m u"))
+            turn_chunk(zs[c][:], c, 96, banks[c])
+        deal_w3_words(1, "xl%d" % (MC - 1))
+        for c in range(MC):
+            back = psum.tile([P, 2, P], F32, name="back_l", tag=banks[c])
+            for pair in range(2):
+                nc.tensor.transpose(back[:, pair, :], z_t[1][:, c, pair, :], ident_f[:])
+            nc.scalar.copy(out=zq1[c][:], in_=back[:].rearrange("p u m -> p m u"))
             codes = kept([P, P], U32, "z_codes1_%d" % c)
             scales = kept([P, P], U8, "z_sc1_%d" % c)
             nc.vector.quantize_mx(out=codes[:].bitcast(FP8X4), scales=scales[:],
-                                  in_=zq1[:].rearrange("p m u -> p (m u)").bitcast(BF16))
+                                  in_=zq1[c][:].rearrange("p m u -> p (m u)").bitcast(BF16))
             second_stage(1, c, codes[:], scales[:])
         for c in range(MC):
-            cols = slice(P * c, P * (c + 1))
-            y = kept([P, 4, P], F32, "y_sb%d" % c)
-            nc.scalar.copy(out=y[:], in_=y_ps[c][:])
-            nc.sync.dma_start(out=out_rows[:, :, cols], in_=y[:])
+            cols = chunks[c]
+            y = kept([P, 4, P], F32, "y_sb%d" % c)[:]
+            nc.scalar.copy(out=y, in_=y_ps[c][:])
+            nc.sync.dma_start(out=out_rows[:, :, cols], in_=y)
             yb = kept([P, P, 4], BF16, "yb%d" % c)
             nc.vector.tensor_copy(out=yb[:].rearrange("p (m i) t -> p m t i", i=4),
-                                  in_=y[:].rearrange("p t (m i) -> p m t i", i=4))
+                                  in_=y.rearrange("p t (m i) -> p m t i", i=4))
             nc.vector.quantize_mx(out=y_codes[:, cols].bitcast(FP8X4), scales=y_sc[:, cols],
                                   in_=yb[:].rearrange("p m t -> p (m t)"))
-            if c % 2 == 1:
-                both = slice(P * (c - 1), P * (c + 1))
-                nc.sync.dma_start(out=out_words[:, both], in_=y_codes[:, both].bitcast(I32))
+        nc.sync.dma_start(out=out_words, in_=y_codes[:].bitcast(I32))
         for q in range(4):
             queue = nc.scalar if q % 2 else nc.sync
             queue.dma_start(out=out_2[0, 4 * q : 4 * q + 4, :].bitcast(I32),

@@ -21,7 +21,7 @@ P = 128
 KP = K // 512
 RT = H // P
 MC = M // P
-W1_CHUNKS = (256, 256, 256, 256)
+W1_CHUNKS = (256, 256, 128, 128, 128, 128)
 W2_FIRST = 256
 
 
@@ -117,13 +117,15 @@ def tile_list_substitute_closeness_page_kernel(
         load_page(2)
         load_w1(2)
         load_page(3)
-        load_page(4)
         load_w1(3)
+        load_page(4)
+        load_w1(4)
+        load_page(5)
+        load_w1(5)
         nc.sync.dma_start(out=w3_w[:], in_=w3_words.rearrange("a p c i -> p a (c i)").bitcast(I32))
         for q in range(4):
             nc.sync.dma_start(out=w3_sc[32 * q : 32 * q + 8, :].bitcast(I32),
                               in_=w3_scales[:, 4 * q : 4 * q + 4, :].bitcast(I32))
-        load_page(5)
         load_page(6)
         load_page(7)
 
@@ -133,27 +135,27 @@ def tile_list_substitute_closeness_page_kernel(
         grouped, w1_codes, w1_sc, d_tiles, h_tiles = {}, {}, {}, {}, {}
 
         def h_tag(b):
-            return ("h0", "w1_raw1_2")[b] if b < 2 else "r%d" % (b - 2)
+            return ("h0", "w1_raw1_2")[b] if b < 2 else ("z%d" if b < 6 else "r%d") % (b - 2)
 
         def u_tag(b):
-            return {0: "u0", 1: "w1_raw2_2", 3: "w1_raw3_2"}.get(b, "z%d" % (b - 1))
+            return "u0" if b == 0 else ("w1_raw%d_2" % (b + 1) if b <= 4 else "z%d" % (b - 1))
 
         def codes_tag(b):
-            return ("tab_w0", "grouped0_2", h_tag(0), h_tag(1))[b] if b < 4 else (u_tag(b - 3) if b % 2 else h_tag(b - 2))
+            return ("tab_w0", "grouped0_2", h_tag(0), h_tag(1))[b] if b < 4 else None
 
         def bank(b):
             return ("bank_a", "bank_b")[b % 2]
 
         def x_tag(b):
-            return "grouped2_12" if b == 0 else "grouped%d_0" % (b + 2)
+            return ("grouped2_12", "grouped3_0")[b] if b < 2 else "r%d" % (b - 2)
 
         def cast_w1(b, a):
             if b < 2:
                 grouped[b, a] = kept([P, 1, P, 4], BF16, "grouped%d_%d" % (b, a))[:]
             elif a == 0:
-                grouped[b, 0] = kept([P, 1, P, 4], BF16, "grouped%d_0" % b, "tab_w2" if b == 2 else None)[:]
+                grouped[b, 0] = kept([P, 1, P, 4], BF16, "grouped%d_0" % b, ("tab_w2", None)[b - 2] if b < 4 else "r%d" % (b - 4))[:]
             elif a == 1:
-                both = kept([P, 2, P, 4], BF16, "grouped%d_12" % b)
+                both = kept([P, 2, P, 4], BF16, "grouped%d_12" % b, u_tag(b - 4) if b >= 4 else None)
                 grouped[b, 1], grouped[b, 2] = both[:], both[:, 1:]
             lo = P * b - starts[chunk_of[b]]
             nc.scalar.activation(
@@ -169,7 +171,7 @@ def tile_list_substitute_closeness_page_kernel(
         def quantise_w1(b, a, n=1):
             if a == 0:
                 w1_codes[b] = kept([P, KP * P], U32, "w1_c%d" % b, codes_tag(b))
-                w1_sc[b] = kept([P, KP * P], U8, "w1_s%d" % b)
+                w1_sc[b] = kept([P, KP * P], U8, "w1_s%d" % b, "w1_s%d" % min(b, 3))
             cols = slice(P * a, P * (a + n))
             if (b, a) == (0, 2):
                 w1_codes["late"] = kept([P, P], U32, "w1_late", "tab_w2")
@@ -202,7 +204,7 @@ def tile_list_substitute_closeness_page_kernel(
             lo2 = 2 * lo1
             wide = (W2_FIRST, H - W2_FIRST)[half]
             d = psum.tile([P, S], F32, name="d", tag=bank(b))
-            order = ((1, 0), (2, 0), (1, 1), (2, 1), (2, 2), (1, 2)) if b < 2 else [(w, a) for w in (1, 2) for a in range(KP)]
+            order = ((1, 0), (2, 0), (1, 1), (2, 1), (2, 2), (1, 2)) if b < 2 else [(w, a) for w in ((1, 2) if b == 2 else (2, 1)) for a in range(KP)]
             for n, (which, a) in enumerate(order):
                 cols = slice(P * a, P * (a + 1))
                 flags = dict(start=(n == 0), stop=(n == len(order) - 1))
@@ -229,17 +231,22 @@ def tile_list_substitute_closeness_page_kernel(
         x_tiles, z_tiles = {}, {}
 
         def gather(b):
-            x_tiles[b] = kept([P, M], F32, "x%d" % b, x_tag(b) if b < RT - 2 else "zq0")
+            x_tiles[b] = kept([P, M], F32, "x%d" % b, x_tag(b) if b < RT - 2 else x_tag(b - 2))
             nc.vector.tensor_copy(x_tiles[b][:], pages[b][:].indirect(list3[:]))
 
         def closeness(b):
             x = x_tiles[b]
             u = kept([P, M], F32, "u%d" % b, u_tag(b))
-            nc.scalar.activation(out=u[:], in_=x[:], func=ACT.Abs_reciprocal_sqrt, bias=1.0)
             r = kept([P, M], F32, "r%d" % b)
-            nc.scalar.activation(out=r[:], in_=u[:], func=ACT.Square)
             z_tiles[b] = kept([P, M], BF16, "z%d" % b)
-            nc.scalar.activation(out=z_tiles[b][:], in_=r[:], func=ACT.Copy, scale=gain_sb[:, b : b + 1])
+            halves = (slice(0, M // 2), slice(M // 2, M))
+            for half in halves:
+                nc.scalar.activation(out=u[:, half], in_=x[:, half], func=ACT.Abs_reciprocal_sqrt, bias=1.0)
+            for half in halves:
+                nc.scalar.activation(out=r[:, half], in_=u[:, half], func=ACT.Square)
+            for half in halves:
+                nc.scalar.activation(out=z_tiles[b][:, half], in_=r[:, half], func=ACT.Copy,
+                                     scale=gain_sb[:, b : b + 1])
 
         def turn_chunk(z, c, lo, tag):
             turned = psum.tile([P, P], BF16, name="turned_c", tag=tag)
@@ -250,7 +257,7 @@ def tile_list_substitute_closeness_page_kernel(
         def turn(b):
             z = z_tiles[b]
             lo = 32 * (b % 4)
-            if b == RT - 3:
+            if b == RT - 2:
                 for c in range(MC):
                     turn_chunk(z[:, P * c : P * (c + 1)], c, lo, "y%d" % c)
                 return
@@ -295,11 +302,17 @@ def tile_list_substitute_closeness_page_kernel(
                     out=zq[:, 2 * P * pair : 2 * P * (pair + 1), :].rearrange("p (c m) u -> p c m u", c=2),
                     in_=back[:].rearrange("p c u m -> p c m u"))
 
-        def first_half_of_y():
-            codes = kept([P, M], U32, "z_codes0", u_tag(RT - 3))
-            scales = kept([P, M], U8, "z_sc0")
+        first_half = []
+
+        def quantise_first_half():
+            codes = kept([P, M], U32, "z_codes0")
+            scales = kept([P, M], U8, "z_sc0", "w1_s3")
             nc.vector.quantize_mx(out=codes[:].bitcast(FP8X4), scales=scales[:],
                                   in_=zq[:].rearrange("p m u -> p (m u)").bitcast(BF16))
+            first_half.extend([codes, scales])
+
+        def first_half_of_y():
+            codes, scales = first_half
             for c in range(MC):
                 y_ps.append(psum.tile([P, 4, P], F32, name="y%d" % c, tag="y%d" % c))
                 second_stage(0, c, codes[:, P * c : P * (c + 1)], scales[:, P * c : P * (c + 1)])
@@ -319,25 +332,27 @@ def tile_list_substitute_closeness_page_kernel(
                 square(1)
                 spread_gain()
             if b == 4:
-                deal_w3_words(0, "w1_raw3_0")
-                deal_w3_scales("w1_raw3_1")
+                deal_w3_words(0, "w1_raw5_0")
+                deal_w3_scales("w1_raw5_1")
                 turn_back_first_half()
             if b == 6:
-                first_half_of_y()
+                quantise_first_half()
             gather(b)
             if b + 2 < RT:
                 first_stage(b + 2)
             closeness(b)
-            if b + 2 < RT:
+            if b >= 4 and b + 2 < RT:
                 square(b + 2)
             turn(b)
-            if b in (0, 2):
+            if b < 4:
+                square(b + 2)
+            if b + 4 < RT:
                 for a in range(KP):
                     cast_w1(b + 4, a)
-                    cast_w1(b + 5, a)
 
         last = RT - 1
         scatter(last)
+        first_half_of_y()
         y_codes = kept([P, M], U32, "y_codes")
         y_sc = kept([P, M], U8, "y_sc")
         out_rows = out_0.rearrange("(p t) m -> p t m", t=4)
@@ -369,15 +384,20 @@ def tile_list_substitute_closeness_page_kernel(
             second_stage(1, c, codes[:], scales[:])
         for c in range(MC):
             cols = chunks[c]
-            y = kept([P, 4, P], F32, "y_sb%d" % c)[:]
+            if c % 2 == 0:
+                y_pair = kept([P, 4, 2 * P], F32, "y_sb%d" % c)
+            y = y_pair[:, :, P * (c % 2) : P * (c % 2 + 1)]
+            both = slice(P * (c - 1), P * (c + 1))
             nc.scalar.copy(out=y, in_=y_ps[c][:])
-            nc.sync.dma_start(out=out_rows[:, :, cols], in_=y)
+            if c % 2 == 1:
+                nc.sync.dma_start(out=out_rows[:, :, both], in_=y_pair[:])
             yb = kept([P, P, 4], BF16, "yb%d" % c)
             nc.vector.tensor_copy(out=yb[:].rearrange("p (m i) t -> p m t i", i=4),
                                   in_=y.rearrange("p t (m i) -> p m t i", i=4))
             nc.vector.quantize_mx(out=y_codes[:, cols].bitcast(FP8X4), scales=y_sc[:, cols],
                                   in_=yb[:].rearrange("p m t -> p (m t)"))
-        nc.sync.dma_start(out=out_words, in_=y_codes[:].bitcast(I32))
+            if c % 2 == 1:
+                nc.sync.dma_start(out=out_words[:, both], in_=y_codes[:, both].bitcast(I32))
         for q in range(4):
             queue = nc.scalar if q % 2 else nc.sync
             queue.dma_start(out=out_2[0, 4 * q : 4 * q + 4, :].bitcast(I32),

@@ -91,6 +91,8 @@ def tile_list_substitute_closeness_page_kernel(
                     out=w2_sc[h][r:P:32, :].bitcast(I32).rearrange("q (a c) -> q a c", a=KP),
                     in_=w2_scales[:, r:16:4, lo:hi].rearrange("a q c -> q a c").bitcast(I32))
 
+        make_identity(nc, ident_f[:])
+        make_identity(nc, ident_b[:])
         nc.sync.dma_start(list1[:], offs)
         load_tab(0)
         nc.sync.dma_start(list2[:], offs2)
@@ -101,18 +103,18 @@ def tile_list_substitute_closeness_page_kernel(
         load_tab(1)
         load_w2_scales(0, nc.sync)
         load_w1(0, [1])
+        warm = kept([P, 1], F32, "warm")
+        nc.scalar.activation(out=warm[:], in_=ident_f[:, 0:1], func=ACT.Abs_reciprocal_sqrt, bias=1.0)
         load_w2(0)
         load_tab(2)
         load_w1(0, [2])
-        make_identity(nc, ident_f[:])
-        make_identity(nc, ident_b[:])
         nc.sync.dma_start(out=wgs_sb[:], in_=wgs)
         load_page(0)
         load_w1(1)
         nc.sync.dma_start(list3[:], offs3)
         nc.sync.dma_start(out=gain_rows[0:RT, :], in_=gain.rearrange("(b p) -> b p", p=P))
-        load_w2(1)
         load_page(1)
+        load_w2(1)
         load_w2_scales(1, nc.sync)
         load_page(2)
         load_w1(2)

@@ -21,8 +21,9 @@ P = 128
 KP = K // 512
 RT = H // P
 MC = M // P
-W1_CHUNKS = (256, 256, 128, 128, 128, 128)
-W2_FIRST = 256
+HALF = S // 2
+W2_PARTS = (256, 256, 512)
+SPLIT_TILES = 3
 
 
 def tile_list_substitute_closeness_page_kernel(
@@ -32,252 +33,240 @@ def tile_list_substitute_closeness_page_kernel(
     nc = tc.nc
     with ExitStack() as ctx:
         keep = ctx.enter_context(tc.tile_pool(name="keep", bufs=1))
-        ring = ctx.enter_context(tc.tile_pool(name="ring", bufs=3))
         psum = ctx.enter_context(tc.psum_pool(name="psum", bufs=1))
 
         def kept(shape, dtype, name, tag=None):
             return keep.tile(shape, dtype, name=name, tag=tag or name, align_bytes=64)
-
-        def rot(shape, dtype, name, bufs=3):
-            return ring.tile(shape, dtype, name=name, align_bytes=64, bufs=bufs)
 
         list1 = keep.tile([P, S // 16], U16, name="list1")
         list2 = keep.tile([P, S // 16], U16, name="list2")
         list3 = keep.tile([P, M // 16], U16, name="list3")
 
         tab_sc = kept([P, KP * T], U8, "tab_sc")
-        w2_sc = [kept([P, KP * W2_FIRST], U8, "w2_sca"), kept([P, KP * (H - W2_FIRST)], U8, "w2_scb")]
-        v_sc = [kept([P, S], U8, "v_sc%d" % a) for a in range(KP)]
+        v_sc = kept([P, KP * S], U8, "v_sc")
+        w2_lo = [sum(W2_PARTS[:i]) for i in range(len(W2_PARTS))]
+        w2_sc = [kept([P, KP * c], U8, "w2_sc%d" % i) for i, c in enumerate(W2_PARTS)]
+        w2_w = [kept([P, KP, 2 * c], U8, "w2_w%d" % i) for i, c in enumerate(W2_PARTS)]
         w3_sc = kept([P, N], U8, "w3_sc")
         gain_rows = kept([P, P], F32, "gain_rows")
-        nc.gpsimd.memset(tab_sc[:, 0:T].bitcast(I32), 0)
-        nc.vector.memset(tab_sc[:, T:].bitcast(I32), 0)
+        nc.gpsimd.memset(tab_sc[:, 0 : KP * T // 2].bitcast(I32), 0)
+        nc.vector.memset(tab_sc[:, KP * T // 2 :].bitcast(I32), 0)
         nc.vector.memset(w2_sc[0][:].bitcast(I32), 0)
-        nc.vector.memset(w2_sc[1][:].bitcast(I32), 0)
+        for part in w2_sc[1:]:
+            nc.vector.memset(part[:].bitcast(I32), 0)
         nc.vector.memset(w3_sc[:].bitcast(I32), 0)
         nc.vector.memset(gain_rows[:], 0.0)
 
         ident_f = kept([P, P], F32, "ident_f")
         ident_b = kept([P, P], BF16, "ident_b")
+        make_identity(nc, ident_f[:])
+        make_identity(nc, ident_b[:])
 
         tab_w = [kept([P, T], I32, "tab_w%d" % a) for a in range(KP)]
         pages = [kept([P, T2], F32, "page%d" % b) for b in range(RT)]
-        starts = [sum(W1_CHUNKS[:i]) for i in range(len(W1_CHUNKS))]
-        w1_raw = [[kept([P, 4, c], F32, "w1_raw%d_%d" % (i, a)) for a in range(KP)] for i, c in enumerate(W1_CHUNKS)]
-        w2_w = [kept([P, KP, 2 * W2_FIRST], U8, "w2_wa"), kept([P, KP, 2 * (H - W2_FIRST)], U8, "w2_wb")]
+        w1_raw = [[kept([P, S + HALF * (a // 2)], F32, "w1_raw%d_%d" % (b, a)) for a in range(KP)] for b in range(RT)]
         wgs_sb = kept([P, S], F32, "wgs_sb")
         w3_w = kept([P, 2, N], I32, "w3_w")
 
         def load_tab(a):
             nc.sync.dma_start(out=tab_w[a][:], in_=tab_words[a].rearrange("p t i -> p (t i)").bitcast(I32))
 
-        def load_w1(i, passes=range(KP)):
-            for a in passes:
-                rows = w1[512 * a : 512 * (a + 1), starts[i] : starts[i] + W1_CHUNKS[i]]
-                nc.sync.dma_start(out=w1_raw[i][a][:], in_=rows.rearrange("(p j) c -> p j c", j=4))
+        def load_w1(b):
+            for a in range(KP):
+                rows = w1[512 * a : 512 * (a + 1), P * b : P * (b + 1)]
+                nc.sync.dma_start(out=w1_raw[b][a][:, 0:S].rearrange("p (j c) -> p j c", j=4),
+                                  in_=rows.rearrange("(p j) c -> p j c", j=4))
 
-        def load_w2(h):
-            lo, hi = (0, 2 * W2_FIRST) if h == 0 else (2 * W2_FIRST, 2 * H)
-            nc.sync.dma_start(out=w2_w[h][:].bitcast(I32),
-                              in_=w2_words.rearrange("a p n -> p a n")[:, :, lo:hi].bitcast(I32))
+        def load_w2_words(i):
+            cols = slice(2 * w2_lo[i], 2 * (w2_lo[i] + W2_PARTS[i]))
+            nc.sync.dma_start(out=w2_w[i][:].bitcast(I32),
+                              in_=w2_words.rearrange("a p n -> p a n")[:, :, cols].bitcast(I32))
+
+        def load_w2_scales(i, queue):
+            cols = slice(w2_lo[i], w2_lo[i] + W2_PARTS[i])
+            for r in range(4):
+                queue.dma_start(
+                    out=w2_sc[i][r:P:32, :].bitcast(I32).rearrange("q (a c) -> q a c", a=KP),
+                    in_=w2_scales[:, r:16:4, cols].rearrange("a q c -> q a c").bitcast(I32))
 
         def load_page(b):
             nc.sync.dma_start(out=pages[b][:], in_=page0[P * b : P * (b + 1), :])
 
-        def load_w2_scales(h, queue):
-            lo, hi = (0, W2_FIRST) if h == 0 else (W2_FIRST, H)
-            for r in range(4):
-                queue.dma_start(
-                    out=w2_sc[h][r:P:32, :].bitcast(I32).rearrange("q (a c) -> q a c", a=KP),
-                    in_=w2_scales[:, r:16:4, lo:hi].rearrange("a q c -> q a c").bitcast(I32))
-
-        make_identity(nc, ident_f[:])
-        make_identity(nc, ident_b[:])
         nc.sync.dma_start(list1[:], offs)
         load_tab(0)
         nc.sync.dma_start(list2[:], offs2)
         for r in range(4):
             nc.sync.dma_start(out=tab_sc[r:P:32, :].bitcast(I32).rearrange("q (a c) -> q a c", a=KP),
                               in_=tab_scales[:, r:16:4, :].rearrange("a q c -> q a c").bitcast(I32))
-        load_w1(0, [0])
         load_tab(1)
+        load_w1(0)
+        load_w2_words(0)
         load_w2_scales(0, nc.sync)
-        load_w1(0, [1])
+        load_tab(2)
         warm = kept([P, 1], F32, "warm")
         nc.scalar.activation(out=warm[:], in_=ident_f[:, 0:1], func=ACT.Abs_reciprocal_sqrt, bias=1.0)
-        load_w2(0)
-        load_tab(2)
-        load_w1(0, [2])
+        for a in range(KP):
+            nc.vector.tensor_copy(v_sc[:, a * S : (a + 1) * S], tab_sc[:, a * T : (a + 1) * T].indirect(list1[:]))
+        nc.sync.dma_start(list3[:], offs3)
         nc.sync.dma_start(out=wgs_sb[:], in_=wgs)
         load_page(0)
         load_w1(1)
-        nc.sync.dma_start(list3[:], offs3)
-        nc.sync.dma_start(out=gain_rows[0:RT, :], in_=gain.rearrange("(b p) -> b p", p=P))
         load_page(1)
-        load_w2(1)
+        nc.sync.dma_start(out=gain_rows[0:RT, :], in_=gain.rearrange("(b p) -> b p", p=P))
+        load_w2_words(1)
         load_w2_scales(1, nc.sync)
-        load_page(2)
         load_w1(2)
-        load_page(3)
+        load_page(2)
         load_w1(3)
-        load_page(4)
+        load_page(3)
         load_w1(4)
-        load_page(5)
-        load_w1(5)
+        load_w2_words(2)
+        load_w2_scales(2, nc.sync)
+        for b in (5, 6):
+            load_page(b - 1)
+            load_w1(b)
         nc.sync.dma_start(out=w3_w[:], in_=w3_words.rearrange("a p c i -> p a (c i)").bitcast(I32))
         for q in range(4):
             nc.sync.dma_start(out=w3_sc[32 * q : 32 * q + 8, :].bitcast(I32),
                               in_=w3_scales[:, 4 * q : 4 * q + 4, :].bitcast(I32))
+        load_w1(7)
         load_page(6)
         load_page(7)
 
-        v_w = [kept([P, S], U32, "v_w%d" % a)[:] for a in range(2)]
-
-        chunk_of = [max(n for n in range(len(starts)) if starts[n] <= P * b) for b in range(RT)]
+        v_w = [kept([P, S], U32, "v_w%d" % a) for a in range(KP)]
         grouped, w1_codes, w1_sc, d_tiles, h_tiles = {}, {}, {}, {}, {}
+        x_tiles, u_tiles, r_tiles, z_tiles, turned = {}, {}, {}, {}, {}
 
-        def h_tag(b):
-            return ("h0", "w1_raw1_2")[b] if b < 2 else ("z%d" if b < 6 else "r%d") % (b - 2)
-
-        def u_tag(b):
-            return "u0" if b == 0 else ("w1_raw%d_2" % (b + 1) if b <= 4 else "z%d" % (b - 1))
-
-        def codes_tag(b):
-            return ("tab_w0", "grouped0_2", h_tag(0), h_tag(1))[b] if b < 4 else None
-
-        def bank(b):
-            return ("bank_a", "bank_b")[b % 2]
-
-        def x_tag(b):
-            return ("grouped2_12", "grouped3_0")[b] if b < 2 else "r%d" % (b - 2)
+        def gather_table(a, lo, hi):
+            nc.vector.tensor_copy(v_w[a][:, lo:hi], tab_w[a][:].bitcast(U32).indirect(list1[:, lo // 16 : hi // 16]))
 
         def cast_w1(b, a):
-            if b < 2:
-                grouped[b, a] = kept([P, 1, P, 4], BF16, "grouped%d_%d" % (b, a))[:]
-            elif a == 0:
-                grouped[b, 0] = kept([P, 1, P, 4], BF16, "grouped%d_0" % b, ("tab_w2", None)[b - 2] if b < 4 else "r%d" % (b - 4))[:]
+            early = ("w1_c%d" % ((b - 1) % 2), "w1_s%d" % ((b - 1) % 2))
+            late = ("w1_raw%d_1" % (b - 1), "r%d" % (b % 2))
+            tags = (None, None) if b == 0 else early if b < 4 else late
+            if a == 0:
+                grouped[b, 0] = kept([P, 1, P, 4], BF16, "grouped%d_0" % b, tags[0])[:]
             elif a == 1:
-                both = kept([P, 2, P, 4], BF16, "grouped%d_12" % b, u_tag(b - 4) if b >= 4 else None)
+                both = kept([P, 2, P, 4], BF16, "grouped%d_12" % b, tags[1])
                 grouped[b, 1], grouped[b, 2] = both[:], both[:, 1:]
-            lo = P * b - starts[chunk_of[b]]
             nc.scalar.activation(
                 out=grouped[b, a][:, 0].rearrange("p (c i) j -> p c j i", i=4),
-                in_=w1_raw[chunk_of[b]][a][:, :, lo : lo + P].rearrange("p j (c i) -> p c j i", i=4),
+                in_=w1_raw[b][a][:, 0:S].rearrange("p (j c i) -> p c j i", j=4, i=4),
                 func=ACT.Copy, scale=-1.0)
 
-        def codes_of(b, a, n=1):
-            if (b, a) == (0, 2):
-                return w1_codes["late"][:]
-            return w1_codes[b][:, P * a : P * (a + n)]
-
-        def quantise_w1(b, a, n=1):
+        def quantise_w1(b, a, n):
             if a == 0:
-                w1_codes[b] = kept([P, KP * P], U32, "w1_c%d" % b, codes_tag(b))
-                w1_sc[b] = kept([P, KP * P], U8, "w1_s%d" % b, "w1_s%d" % min(b, 3))
+                w1_codes[b] = kept([P, KP * P], U32, "w1_c%d" % b, "w1_c%d" % (b % 2))
+                w1_sc[b] = kept([P, KP * P], U8, "w1_s%d" % b, "w1_s%d" % (b % 2))
             cols = slice(P * a, P * (a + n))
-            if (b, a) == (0, 2):
-                w1_codes["late"] = kept([P, P], U32, "w1_late", "tab_w2")
-            nc.vector.quantize_mx(out=codes_of(b, a, n).bitcast(FP8X4), scales=w1_sc[b][:, cols],
+            nc.vector.quantize_mx(out=w1_codes[b][:, cols].bitcast(FP8X4), scales=w1_sc[b][:, cols],
                                   in_=grouped[b, a][:, 0:n].rearrange("p a c j -> p (a c j)"))
 
-        for a in range(KP):
-            if a == 2:
-                v_w.append(kept([P, S], U32, "v_w2", "grouped0_1")[:])
-            nc.vector.tensor_copy(v_sc[a][:], tab_sc[:, a * T : (a + 1) * T].indirect(list1[:]))
-            nc.vector.tensor_copy(v_w[a], tab_w[a][:].bitcast(U32).indirect(list1[:]))
-            cast_w1(0, a)
-            quantise_w1(0, a)
-            cast_w1(1, a)
-        for a in range(KP):
-            quantise_w1(1, a)
+        def pass_w1(b, a, out, lo, hi, **flags):
+            cols = slice(P * a, P * (a + 1))
+            nc.tensor.matmul_mx(out=out, lhsT=w1_codes[b][:, cols].bitcast(FP8X4), lhsT_scale=w1_sc[b][:, cols],
+                                rhs=v_w[a][:, lo:hi].bitcast(FP8X4), rhs_scale=v_sc[:, a * S + lo : a * S + hi], **flags)
 
+        def pass_w2(b, a, out, lo, hi, **flags):
+            i = max(n for n in range(len(w2_lo)) if w2_lo[n] <= P * b)
+            col = P * b - w2_lo[i]
+            nc.tensor.matmul_mx(out=out, lhsT=w2_w[i][:, a, 2 * col : 2 * (col + P)].bitcast(FP4X4),
+                                lhsT_scale=w2_sc[i][:, a * W2_PARTS[i] + col : a * W2_PARTS[i] + col + P],
+                                rhs=v_w[a][:, lo:hi].bitcast(FP8X4), rhs_scale=v_sc[:, a * S + lo : a * S + hi], **flags)
+
+        def first_stage(b):
+            d = psum.tile([P, S], F32, name="d", tag="d%d" % (b % 2))
+            for a in range(KP):
+                pass_w2(b, a, d[:], 0, S, start=(a == 0), stop=False)
+            for a in (1, 2, 0):
+                pass_w1(b, a, d[:], 0, S, start=False, stop=(a == 0))
+            d_tiles[b] = (d[:, 0:HALF], d[:, HALF:S], d[:])
+
+        def first_stage_in_halves(b):
+            halves = [psum.tile([P, HALF], F32, name="d_half", tag="y%d" % (2 * (b % 2) + k)) for k in range(2)]
+            if b == 0:
+                order = [(which, a) for a in range(KP) for which in (2, 1)]
+            else:
+                order = [(which, a) for which in (2, 1) for a in range(KP)]
+            last_steps = 2
+            steps = [(n, k) for n in range(len(order) - last_steps) for k in range(2)]
+            steps += [(n, k) for k in range(2) for n in range(len(order) - last_steps, len(order))]
+            for n, k in steps:
+                which, a = order[n]
+                lo = k * HALF
+                if which == 1:
+                    pass_w1(b, a, halves[k][:], lo, lo + HALF, start=False, stop=(n == len(order) - 1))
+                else:
+                    for c in range(2):
+                        pass_w2(b, a, halves[k][:, P * c : P * (c + 1)], lo + P * c, lo + P * (c + 1),
+                                start=(n == 0 and c == 0), stop=False)
+            d_tiles[b] = (halves[0][:], halves[1][:])
+
+        def square(b, k):
+            if k == 1 and 1 <= b < RT - 1:
+                h_tiles[b, k] = w1_raw[b + 1][2][:, 0:HALF]
+            else:
+                held = (b, k) == (0, 1) or 3 <= b < RT - 1
+                tag = "w1_raw%d_0" % (b + 1) if held else "r0" if (b, k) == (RT - 1, 1) else None
+                h_tiles[b, k] = kept([P, HALF], F32, "h%d_%d" % (b, k), tag)[:]
+            nc.scalar.activation(out=h_tiles[b, k], in_=d_tiles[b][k], func=ACT.Square)
+
+        def scatter(b, k):
+            nc.vector.tensor_tensor(pages[b][:].indirect(list2[:, 16 * k : 16 * (k + 1)]), h_tiles[b, k],
+                                    wgs_sb[:, k * HALF : (k + 1) * HALF], ALU.mult)
+
+        def gather(b):
+            behind = b + 2 if b else 1
+            x_tiles[b] = w1_raw[behind][2][:, HALF:] if behind < RT else kept([P, M], F32, "x%d" % b, "r0")[:]
+            nc.vector.tensor_copy(x_tiles[b], pages[b][:].indirect(list3[:]))
+
+        def root(b):
+            u_tiles[b] = kept([P, M], F32, "u%d" % b, "w1_raw%d_1" % (b + 3) if b + 3 < RT else ("r1", "z_t0")[b % 2])
+            nc.scalar.activation(out=u_tiles[b][:], in_=x_tiles[b], func=ACT.Abs_reciprocal_sqrt, bias=1.0)
+
+        def closeness(b):
+            r_tiles[b] = kept([P, M], F32, "r%d" % b, "r%d" % (b % 2 if b < RT - 2 else b))
+            nc.scalar.activation(out=r_tiles[b][:], in_=u_tiles[b][:], func=ACT.Square)
 
         gain_sb = kept([P, RT], F32, "gain_sb")
 
         def spread_gain():
-            gain_ps = psum.tile([P, P], F32, name="gain_ps", tag="bank_a")
+            gain_ps = psum.tile([P, P], F32, name="gain_ps", tag="turned")
             nc.tensor.transpose(gain_ps[:], gain_rows[:], ident_f[:])
             nc.scalar.copy(out=gain_sb[:], in_=gain_ps[:, 0:RT])
 
-        def first_stage(b):
-            col = P * b
-            half = 0 if col < W2_FIRST else 1
-            lo1 = col - half * W2_FIRST
-            lo2 = 2 * lo1
-            wide = (W2_FIRST, H - W2_FIRST)[half]
-            d = psum.tile([P, S], F32, name="d", tag=bank(b))
-            order = ((1, 0), (2, 0), (1, 1), (2, 1), (2, 2), (1, 2)) if b < 2 else [(w, a) for w in ((1, 2) if b == 2 else (2, 1)) for a in range(KP)]
-            for n, (which, a) in enumerate(order):
-                cols = slice(P * a, P * (a + 1))
-                flags = dict(start=(n == 0), stop=(n == len(order) - 1))
-                if which == 2:
-                    nc.tensor.matmul_mx(
-                        out=d[:], lhsT=w2_w[half][:, a, lo2 : lo2 + 2 * P].bitcast(FP4X4),
-                        lhsT_scale=w2_sc[half][:, a * wide + lo1 : a * wide + lo1 + P],
-                        rhs=v_w[a].bitcast(FP8X4), rhs_scale=v_sc[a][:], **flags)
-                else:
-                    nc.tensor.matmul_mx(
-                        out=d[:], lhsT=codes_of(b, a).bitcast(FP8X4), lhsT_scale=w1_sc[b][:, cols],
-                        rhs=v_w[a].bitcast(FP8X4), rhs_scale=v_sc[a][:], **flags)
-            d_tiles[b] = d
-
-        def square(b):
-            h_tiles[b] = kept([P, S], F32, "h%d" % b, h_tag(b))
-            nc.scalar.activation(out=h_tiles[b][:], in_=d_tiles[b][:], func=ACT.Square)
-
-        def scatter(b):
-            nc.vector.tensor_tensor(pages[b][:].indirect(list2[:]), h_tiles[b][:], wgs_sb[:], ALU.mult)
+        def weigh(b):
+            z_tiles[b] = kept([P, M], BF16, "z%d" % b, "z%d" % (b % 2))
+            nc.scalar.activation(out=z_tiles[b][:], in_=r_tiles[b][:], func=ACT.Copy, scale=gain_sb[:, b : b + 1])
+            if b == RT - 3:
+                turned[b] = [psum.tile([P, P], BF16, name="turned_c", tag="y%d" % c)[:] for c in range(MC)]
+            else:
+                whole = psum.tile([P, MC, P], BF16, name="turned", tag="d0" if b == RT - 2 else "turned")
+                turned[b] = [whole[:, c, :] for c in range(MC)] + [whole[:]]
+            for c in range(MC):
+                nc.tensor.transpose(turned[b][c], z_tiles[b][:, P * c : P * (c + 1)], ident_b[:])
 
         z_t = [kept([P, MC, 2, P], F32, "z_t%d" % g) for g in range(2)]
 
-        x_tiles, z_tiles = {}, {}
-
-        def gather(b):
-            x_tiles[b] = kept([P, M], F32, "x%d" % b, x_tag(b) if b < RT - 2 else x_tag(b - 2))
-            nc.vector.tensor_copy(x_tiles[b][:], pages[b][:].indirect(list3[:]))
-
-        def closeness(b):
-            x = x_tiles[b]
-            u = kept([P, M], F32, "u%d" % b, u_tag(b))
-            r = kept([P, M], F32, "r%d" % b)
-            z_tiles[b] = kept([P, M], BF16, "z%d" % b)
-            halves = (slice(0, M // 2), slice(M // 2, M))
-            for half in halves:
-                nc.scalar.activation(out=u[:, half], in_=x[:, half], func=ACT.Abs_reciprocal_sqrt, bias=1.0)
-            for half in halves:
-                nc.scalar.activation(out=r[:, half], in_=u[:, half], func=ACT.Square)
-            for half in halves:
-                nc.scalar.activation(out=z_tiles[b][:, half], in_=r[:, half], func=ACT.Copy,
-                                     scale=gain_sb[:, b : b + 1])
-
-        def turn_chunk(z, c, lo, tag):
-            turned = psum.tile([P, P], BF16, name="turned_c", tag=tag)
-            nc.tensor.transpose(turned[:], z, ident_b[:])
-            nc.scalar.copy(out=z_t[1][:, c, :, lo : lo + 32],
-                           in_=turned[:].bitcast(F32).rearrange("m (p u) -> m u p", u=2))
-
-        def turn(b):
-            z = z_tiles[b]
+        def collect(b):
             lo = 32 * (b % 4)
-            if b == RT - 2:
+            if b == RT - 3:
                 for c in range(MC):
-                    turn_chunk(z[:, P * c : P * (c + 1)], c, lo, "y%d" % c)
+                    nc.scalar.copy(out=z_t[1][:, c, :, lo : lo + 32],
+                                   in_=turned[b][c].bitcast(F32).rearrange("m (p u) -> m u p", u=2))
                 return
-            turned = psum.tile([P, MC, P], BF16, name="turned", tag=bank(b + 1))
-            for c in range(MC):
-                nc.tensor.transpose(turned[:, c, :], z[:, P * c : P * (c + 1)], ident_b[:])
             nc.scalar.copy(
                 out=z_t[b // 4][:, :, :, lo : lo + 32],
-                in_=turned[:].rearrange("m c r -> m (c r)").bitcast(F32).rearrange("m (c p u) -> m c u p", c=MC, u=2))
+                in_=turned[b][MC].rearrange("m c r -> m (c r)").bitcast(F32).rearrange("m (c p u) -> m c u p", c=MC, u=2))
 
         w3_dealt = {}
 
-        def deal_w3_words(g, tag):
+        def deal_w3_words(g, tag=None):
             w3_dealt[g] = kept([P, N], I32, "w3_dealt%d" % g, tag)
             nc.vector.tensor_copy(out=w3_dealt[g][:].rearrange("p (t m) -> p t m", t=4),
                                   in_=w3_w[:, g, :].rearrange("p (m t) -> p t m", t=4))
 
-        def deal_w3_scales(tag):
+        def deal_w3_scales(tag=None):
             w3_dealt["scales"] = kept([P, N], U8, "w3_sp", tag)
             nc.vector.tensor_copy(out=w3_dealt["scales"][:].rearrange("p (t m) -> p t m", t=4),
                                   in_=w3_sc[:].rearrange("p (m t) -> p t m", t=4))
@@ -294,85 +283,114 @@ def tile_list_substitute_closeness_page_kernel(
 
         zq = kept([P, M, 2], F32, "zq0")
 
-        def turn_back_first_half():
-            for pair in range(MC // 2):
-                back = psum.tile([P, 2, 2, P], F32, name="back", tag=("bank_c", "bank_d")[pair])
-                for c in range(2):
-                    for u in range(2):
-                        nc.tensor.transpose(back[:, c, u, :], z_t[0][:, 2 * pair + c, u, :], ident_f[:])
-                nc.scalar.copy(
-                    out=zq[:, 2 * P * pair : 2 * P * (pair + 1), :].rearrange("p (c m) u -> p c m u", c=2),
-                    in_=back[:].rearrange("p c u m -> p c m u"))
+        def turn_back_first_half(pair):
+            back = psum.tile([P, 2, 2, P], F32, name="back", tag="y%d" % pair)
+            for c in range(2):
+                for u in range(2):
+                    nc.tensor.transpose(back[:, c, u, :], z_t[0][:, 2 * pair + c, u, :], ident_f[:])
+            nc.scalar.copy(
+                out=zq[:, 2 * P * pair : 2 * P * (pair + 1), :].rearrange("p (c m) u -> p c m u", c=2),
+                in_=back[:].rearrange("p c u m -> p c m u"))
 
-        first_half = []
-
-        def quantise_first_half():
-            codes = kept([P, M], U32, "z_codes0")
-            scales = kept([P, M], U8, "z_sc0", "w1_s3")
-            nc.vector.quantize_mx(out=codes[:].bitcast(FP8X4), scales=scales[:],
-                                  in_=zq[:].rearrange("p m u -> p (m u)").bitcast(BF16))
-            first_half.extend([codes, scales])
-
-        def first_half_of_y():
-            codes, scales = first_half
-            for c in range(MC):
-                y_ps.append(psum.tile([P, 4, P], F32, name="y%d" % c, tag="y%d" % c))
-                second_stage(0, c, codes[:, P * c : P * (c + 1)], scales[:, P * c : P * (c + 1)])
-
-        first_stage(0)
-        square(0)
-        first_stage(1)
-        for b in (2, 3):
-            for a in range(KP):
-                cast_w1(b, a)
-        for b in range(RT - 1):
-            scatter(b)
-            if b + 2 < RT:
-                quantise_w1(b + 2, 0)
-                quantise_w1(b + 2, 1, 2)
-            if b == 0:
-                square(1)
-                spread_gain()
-            if b == 4:
-                deal_w3_words(0, "w1_raw5_0")
-                deal_w3_scales("w1_raw5_1")
-                turn_back_first_half()
-            if b == 6:
-                quantise_first_half()
-            gather(b)
-            if b + 2 < RT:
-                first_stage(b + 2)
-            closeness(b)
-            if b >= 4 and b + 2 < RT:
-                square(b + 2)
-            turn(b)
-            if b < 4:
-                square(b + 2)
-            if b + 4 < RT:
-                for a in range(KP):
-                    cast_w1(b + 4, a)
+        for a in range(KP - 1):
+            gather_table(a, 0, S)
+        for a in range(KP):
+            cast_w1(0, a)
+            quantise_w1(0, a, 1)
+        gather_table(KP - 1, 0, HALF)
+        gather_table(KP - 1, HALF, S)
+        first_stage_in_halves(0)
+        square(0, 0)
+        scatter(0, 0)
+        cast_w1(1, 0)
+        quantise_w1(1, 0, 1)
+        square(0, 1)
+        scatter(0, 1)
+        for a in (1, 2):
+            cast_w1(1, a)
+            quantise_w1(1, a, 1)
+        gather(0)
+        first_stage_in_halves(1)
 
         last = RT - 1
-        scatter(last)
-        first_half_of_y()
+        square(1, 0)
+        for b in range(1, last):
+            scatter(b, 0)
+            for a in range(KP) if b + 1 < 4 else (1, 2):
+                cast_w1(b + 1, a)
+            if b + 1 < 4:
+                quantise_w1(b + 1, 0, 1)
+            quantise_w1(b + 1, 1, 2)
+            if b >= 2:
+                gather(b - 1)
+            if b + 1 < SPLIT_TILES:
+                first_stage_in_halves(b + 1)
+            else:
+                first_stage(b + 1)
+            if b >= 2:
+                root(b - 2)
+            square(b, 1)
+            scatter(b, 1)
+            if b >= 2:
+                closeness(b - 2)
+            if b >= 3:
+                collect(b - 3)
+            if 4 <= b + 2 < RT:
+                cast_w1(b + 2, 0)
+                quantise_w1(b + 2, 0, 1)
+            if b == 2:
+                spread_gain()
+            if b >= 2:
+                weigh(b - 2)
+            if b + 1 < last:
+                square(b + 1, 0)
+
+        deal_w3_words(0, "w1_raw7_1")
+        deal_w3_scales()
+        gather(last - 1)
+        square(last, 0)
+        scatter(last, 0)
+        turn_back_first_half(0)
+        turn_back_first_half(1)
+        root(last - 2)
+        collect(last - 3)
+        closeness(last - 2)
+        weigh(last - 2)
+        collect(last - 2)
+        root(last - 1)
+        square(last, 1)
+        z_codes = kept([P, M], U32, "z_codes0", "h7_0")
+        z_scales = kept([P, M], U8, "z_sc0")
+        nc.vector.quantize_mx(out=z_codes[:].bitcast(FP8X4), scales=z_scales[:],
+                              in_=zq[:].rearrange("p m u -> p (m u)").bitcast(BF16))
+        scatter(last, 1)
+        closeness(last - 1)
+        weigh(last - 1)
+        for c in range(MC):
+            y_ps.append(psum.tile([P, 4, P], F32, name="y%d" % c, tag="y%d" % c))
+            second_stage(0, c, z_codes[:, P * c : P * (c + 1)], z_scales[:, P * c : P * (c + 1)])
+
         y_codes = kept([P, M], U32, "y_codes")
         y_sc = kept([P, M], U8, "y_sc")
         out_rows = out_0.rearrange("(p t) m -> p t m", t=4)
         out_words = out_1[0].rearrange("p m t -> p (m t)").bitcast(I32)
-        u_last = kept([P, M], F32, "u_last", u_tag(last))
-        banks = ("bank_c", "bank_a", "bank_d", "bank_b")
+        banks = ("spare", "d1", "turned", "d0")
         xs = [kept([P, P], F32, "xl%d" % c) for c in range(MC)]
+        u_last = kept([P, M], F32, "u_last", "r6")
+        us = [u_last[:, P * c : P * (c + 1)] for c in range(MC)]
         zs = [kept([P, P], BF16, "zl%d" % c) for c in range(MC)]
         zq1 = [kept([P, P, 2], F32, "zq1_%d" % c) for c in range(MC)]
         chunks = [slice(P * c, P * (c + 1)) for c in range(MC)]
         for c in range(MC):
             nc.vector.tensor_copy(xs[c][:], pages[last][:].indirect(list3[:, 8 * c : 8 * (c + 1)]))
-            nc.scalar.activation(out=u_last[:, chunks[c]], in_=xs[c][:], func=ACT.Abs_reciprocal_sqrt, bias=1.0)
+            nc.scalar.activation(out=us[c], in_=xs[c][:], func=ACT.Abs_reciprocal_sqrt, bias=1.0)
+        collect(last - 1)
         for c in range(MC):
-            u = u_last[:, chunks[c]]
-            nc.vector.scalar_tensor_tensor(out=zs[c][:], in0=u, scalar=gain_sb[:, last : last + 1], in1=u,
+            nc.vector.scalar_tensor_tensor(out=zs[c][:], in0=us[c], scalar=gain_sb[:, last : last + 1], in1=us[c],
                                            op0=ALU.mult, op1=ALU.mult)
-            turn_chunk(zs[c][:], c, 96, banks[c])
+            once = psum.tile([P, P], BF16, name="once", tag=banks[c])
+            nc.tensor.transpose(once[:], zs[c][:], ident_b[:])
+            nc.scalar.copy(out=z_t[1][:, c, :, 96:P], in_=once[:].bitcast(F32).rearrange("m (p u) -> m u p", u=2))
         deal_w3_words(1, "xl%d" % (MC - 1))
         for c in range(MC):
             back = psum.tile([P, 2, P], F32, name="back_l", tag=banks[c])

@@ -22,8 +22,8 @@ KP = K // 512
 RT = H // P
 MC = M // P
 HALF = S // 2
-W2_PARTS = (256, 256, 512)
-SPLIT_TILES = 3
+W2_PARTS = (384, 256, 384)
+SPLIT_TILES = 4
 
 
 def tile_list_substitute_closeness_page_kernel(
@@ -52,10 +52,10 @@ def tile_list_substitute_closeness_page_kernel(
         nc.gpsimd.memset(tab_sc[:, 0 : KP * T // 2].bitcast(I32), 0)
         nc.vector.memset(tab_sc[:, KP * T // 2 :].bitcast(I32), 0)
         nc.vector.memset(w2_sc[0][:].bitcast(I32), 0)
+        nc.vector.memset(gain_rows[:], 0.0)
         for part in w2_sc[1:]:
             nc.vector.memset(part[:].bitcast(I32), 0)
         nc.vector.memset(w3_sc[:].bitcast(I32), 0)
-        nc.vector.memset(gain_rows[:], 0.0)
 
         ident_f = kept([P, P], F32, "ident_f")
         ident_b = kept([P, P], BF16, "ident_b")
@@ -64,15 +64,15 @@ def tile_list_substitute_closeness_page_kernel(
 
         tab_w = [kept([P, T], I32, "tab_w%d" % a) for a in range(KP)]
         pages = [kept([P, T2], F32, "page%d" % b) for b in range(RT)]
-        w1_raw = [[kept([P, S + HALF * (a // 2)], F32, "w1_raw%d_%d" % (b, a)) for a in range(KP)] for b in range(RT)]
+        w1_raw = [[kept([P, S + HALF * (a != 1)], F32, "w1_raw%d_%d" % (b, a)) for a in range(KP)] for b in range(RT)]
         wgs_sb = kept([P, S], F32, "wgs_sb")
         w3_w = kept([P, 2, N], I32, "w3_w")
 
         def load_tab(a):
             nc.sync.dma_start(out=tab_w[a][:], in_=tab_words[a].rearrange("p t i -> p (t i)").bitcast(I32))
 
-        def load_w1(b):
-            for a in range(KP):
+        def load_w1(b, passes=range(KP)):
+            for a in passes:
                 rows = w1[512 * a : 512 * (a + 1), P * b : P * (b + 1)]
                 nc.sync.dma_start(out=w1_raw[b][a][:, 0:S].rearrange("p (j c) -> p j c", j=4),
                                   in_=rows.rearrange("(p j) c -> p j c", j=4))
@@ -100,40 +100,44 @@ def tile_list_substitute_closeness_page_kernel(
                               in_=tab_scales[:, r:16:4, :].rearrange("a q c -> q a c").bitcast(I32))
         load_tab(1)
         load_w1(0)
+        nc.sync.dma_start(out=gain_rows[0:RT, :], in_=gain.rearrange("(b p) -> b p", p=P))
         load_w2_words(0)
         load_w2_scales(0, nc.sync)
-        load_tab(2)
         warm = kept([P, 1], F32, "warm")
         nc.scalar.activation(out=warm[:], in_=ident_f[:, 0:1], func=ACT.Abs_reciprocal_sqrt, bias=1.0)
         for a in range(KP):
             nc.vector.tensor_copy(v_sc[:, a * S : (a + 1) * S], tab_sc[:, a * T : (a + 1) * T].indirect(list1[:]))
-        nc.sync.dma_start(list3[:], offs3)
-        nc.sync.dma_start(out=wgs_sb[:], in_=wgs)
+        load_tab(2)
+        nc.sync.dma_start(out=wgs_sb[:, 0:HALF], in_=wgs[:, 0:HALF])
         load_page(0)
-        load_w1(1)
+        load_w1(1, (0, 1))
+        nc.sync.dma_start(out=wgs_sb[:, HALF:], in_=wgs[:, HALF:])
+        load_w1(1, (2,))
+        nc.sync.dma_start(list3[:], offs3)
         load_page(1)
-        nc.sync.dma_start(out=gain_rows[0:RT, :], in_=gain.rearrange("(b p) -> b p", p=P))
-        load_w2_words(1)
-        load_w2_scales(1, nc.sync)
         load_w1(2)
         load_page(2)
+        load_w2_words(1)
+        load_w2_scales(1, nc.sync)
         load_w1(3)
         load_page(3)
         load_w1(4)
+        load_page(4)
+        load_w1(5)
         load_w2_words(2)
         load_w2_scales(2, nc.sync)
-        for b in (5, 6):
-            load_page(b - 1)
-            load_w1(b)
+        load_page(5)
+        load_w1(6)
+        load_page(6)
+        load_w1(7)
         nc.sync.dma_start(out=w3_w[:], in_=w3_words.rearrange("a p c i -> p a (c i)").bitcast(I32))
         for q in range(4):
             nc.sync.dma_start(out=w3_sc[32 * q : 32 * q + 8, :].bitcast(I32),
                               in_=w3_scales[:, 4 * q : 4 * q + 4, :].bitcast(I32))
-        load_w1(7)
-        load_page(6)
         load_page(7)
 
-        v_w = [kept([P, S], U32, "v_w%d" % a) for a in range(KP)]
+        z_t = [kept([P, MC, 2, P], F32, "z_t%d" % g) for g in range(2)]
+        v_w = [kept([P, S], U32, "v_w%d" % a, None) for a in range(KP)]
         grouped, w1_codes, w1_sc, d_tiles, h_tiles = {}, {}, {}, {}, {}
         x_tiles, u_tiles, r_tiles, z_tiles, turned = {}, {}, {}, {}, {}
 
@@ -142,13 +146,17 @@ def tile_list_substitute_closeness_page_kernel(
 
         def cast_w1(b, a):
             early = ("w1_c%d" % ((b - 1) % 2), "w1_s%d" % ((b - 1) % 2))
-            late = ("w1_raw%d_1" % (b - 1), "r%d" % (b % 2))
-            tags = (None, None) if b == 0 else early if b < 4 else late
-            if a == 0:
+            tags = early if b else (None, None)
+            if a == 0 and b < 4:
                 grouped[b, 0] = kept([P, 1, P, 4], BF16, "grouped%d_0" % b, tags[0])[:]
+            elif a == 0:
+                grouped[b, 0] = u_tiles[b - 4][:, 0:HALF].bitcast(BF16).rearrange("p (a c j) -> p a c j", a=1, j=4)
             elif a == 1:
-                both = kept([P, 2, P, 4], BF16, "grouped%d_12" % b, tags[1])
-                grouped[b, 1], grouped[b, 2] = both[:], both[:, 1:]
+                if b < 4:
+                    both = kept([P, 2, P, 4], BF16, "grouped%d_12" % b, tags[1])[:]
+                else:
+                    both = x_tiles[b - 3].bitcast(BF16).rearrange("p (a c j) -> p a c j", a=2, j=4)
+                grouped[b, 1], grouped[b, 2] = both, both[:, 1:]
             nc.scalar.activation(
                 out=grouped[b, a][:, 0].rearrange("p (c i) j -> p c j i", i=4),
                 in_=w1_raw[b][a][:, 0:S].rearrange("p (j c i) -> p c j i", j=4, i=4),
@@ -186,8 +194,10 @@ def tile_list_substitute_closeness_page_kernel(
             halves = [psum.tile([P, HALF], F32, name="d_half", tag="y%d" % (2 * (b % 2) + k)) for k in range(2)]
             if b == 0:
                 order = [(which, a) for a in range(KP) for which in (2, 1)]
+            elif b == 1:
+                order = [(1, 0), (2, 0), (2, 1), (2, 2), (1, 1), (1, 2)]
             else:
-                order = [(which, a) for which in (2, 1) for a in range(KP)]
+                order = [(2, 0), (2, 1), (2, 2), (1, 0), (1, 1), (1, 2)]
             last_steps = 2
             steps = [(n, k) for n in range(len(order) - last_steps) for k in range(2)]
             steps += [(n, k) for k in range(2) for n in range(len(order) - last_steps, len(order))]
@@ -195,7 +205,7 @@ def tile_list_substitute_closeness_page_kernel(
                 which, a = order[n]
                 lo = k * HALF
                 if which == 1:
-                    pass_w1(b, a, halves[k][:], lo, lo + HALF, start=False, stop=(n == len(order) - 1))
+                    pass_w1(b, a, halves[k][:], lo, lo + HALF, start=(n == 0), stop=(n == len(order) - 1))
                 else:
                     for c in range(2):
                         pass_w2(b, a, halves[k][:, P * c : P * (c + 1)], lo + P * c, lo + P * (c + 1),
@@ -203,12 +213,10 @@ def tile_list_substitute_closeness_page_kernel(
             d_tiles[b] = (halves[0][:], halves[1][:])
 
         def square(b, k):
-            if k == 1 and 1 <= b < RT - 1:
-                h_tiles[b, k] = w1_raw[b + 1][2][:, 0:HALF]
+            if b >= (3, 1)[k]:
+                h_tiles[b, k] = w1_raw[b + 1][2 * k][:, 0:HALF]
             else:
-                held = (b, k) == (0, 1) or 3 <= b < RT - 1
-                tag = "w1_raw%d_0" % (b + 1) if held else "r0" if (b, k) == (RT - 1, 1) else None
-                h_tiles[b, k] = kept([P, HALF], F32, "h%d_%d" % (b, k), tag)[:]
+                h_tiles[b, k] = kept([P, HALF], F32, "h%d_%d" % (b, k))[:]
             nc.scalar.activation(out=h_tiles[b, k], in_=d_tiles[b][k], func=ACT.Square)
 
         def scatter(b, k):
@@ -216,17 +224,26 @@ def tile_list_substitute_closeness_page_kernel(
                                     wgs_sb[:, k * HALF : (k + 1) * HALF], ALU.mult)
 
         def gather(b):
-            behind = b + 2 if b else 1
-            x_tiles[b] = w1_raw[behind][2][:, HALF:] if behind < RT else kept([P, M], F32, "x%d" % b, "r0")[:]
+            if b == 1:
+                x_tiles[b] = w1_raw[3][0][:, HALF:]
+            else:
+                x_tiles[b] = w1_raw[min(b + 2, RT - 1) if b else 1][2][:, HALF:]
             nc.vector.tensor_copy(x_tiles[b], pages[b][:].indirect(list3[:]))
 
         def root(b):
-            u_tiles[b] = kept([P, M], F32, "u%d" % b, "w1_raw%d_1" % (b + 3) if b + 3 < RT else ("r1", "z_t0")[b % 2])
-            nc.scalar.activation(out=u_tiles[b][:], in_=x_tiles[b], func=ACT.Abs_reciprocal_sqrt, bias=1.0)
+            if b == 0:
+                u_tiles[b] = w1_raw[2][2][:, HALF:]
+            elif b + 3 < RT:
+                u_tiles[b] = w1_raw[b + 3][0][:, HALF:]
+            elif b + 2 < RT:
+                u_tiles[b] = z_t[0][:].rearrange("p c u m -> p (c u m)")[:, 0:M]
+            else:
+                u_tiles[b] = kept([P, M], F32, "u%d" % b, "r5")[:]
+            nc.scalar.activation(out=u_tiles[b], in_=x_tiles[b], func=ACT.Abs_reciprocal_sqrt, bias=1.0)
 
         def closeness(b):
-            r_tiles[b] = kept([P, M], F32, "r%d" % b, "r%d" % (b % 2 if b < RT - 2 else b))
-            nc.scalar.activation(out=r_tiles[b][:], in_=u_tiles[b][:], func=ACT.Square)
+            r_tiles[b] = kept([P, M], F32, "r%d" % b, "w1_raw%d_1" % (b + 3) if b + 3 < RT else None)
+            nc.scalar.activation(out=r_tiles[b][:], in_=u_tiles[b], func=ACT.Square)
 
         gain_sb = kept([P, RT], F32, "gain_sb")
 
@@ -241,12 +258,11 @@ def tile_list_substitute_closeness_page_kernel(
             if b == RT - 3:
                 turned[b] = [psum.tile([P, P], BF16, name="turned_c", tag="y%d" % c)[:] for c in range(MC)]
             else:
-                whole = psum.tile([P, MC, P], BF16, name="turned", tag="d0" if b == RT - 2 else "turned")
+                whole = psum.tile([P, MC, P], BF16, name="turned", tag="d%d" % (b % 2))
                 turned[b] = [whole[:, c, :] for c in range(MC)] + [whole[:]]
             for c in range(MC):
                 nc.tensor.transpose(turned[b][c], z_tiles[b][:, P * c : P * (c + 1)], ident_b[:])
 
-        z_t = [kept([P, MC, 2, P], F32, "z_t%d" % g) for g in range(2)]
 
         def collect(b):
             lo = 32 * (b % 4)
@@ -288,10 +304,14 @@ def tile_list_substitute_closeness_page_kernel(
             for c in range(2):
                 for u in range(2):
                     nc.tensor.transpose(back[:, c, u, :], z_t[0][:, 2 * pair + c, u, :], ident_f[:])
+            return back
+
+        def lay_first_half(pair, back):
             nc.scalar.copy(
                 out=zq[:, 2 * P * pair : 2 * P * (pair + 1), :].rearrange("p (c m) u -> p c m u", c=2),
                 in_=back[:].rearrange("p c u m -> p c m u"))
 
+        spread_gain()
         for a in range(KP - 1):
             gather_table(a, 0, S)
         for a in range(KP):
@@ -302,13 +322,13 @@ def tile_list_substitute_closeness_page_kernel(
         first_stage_in_halves(0)
         square(0, 0)
         scatter(0, 0)
+        square(0, 1)
         cast_w1(1, 0)
         quantise_w1(1, 0, 1)
-        square(0, 1)
         scatter(0, 1)
-        for a in (1, 2):
-            cast_w1(1, a)
-            quantise_w1(1, a, 1)
+        cast_w1(1, 1)
+        cast_w1(1, 2)
+        quantise_w1(1, 1, 2)
         gather(0)
         first_stage_in_halves(1)
 
@@ -316,55 +336,56 @@ def tile_list_substitute_closeness_page_kernel(
         square(1, 0)
         for b in range(1, last):
             scatter(b, 0)
-            for a in range(KP) if b + 1 < 4 else (1, 2):
-                cast_w1(b + 1, a)
             if b + 1 < 4:
+                cast_w1(b + 1, 0)
                 quantise_w1(b + 1, 0, 1)
-            quantise_w1(b + 1, 1, 2)
-            if b >= 2:
+            if b == 2:
                 gather(b - 1)
+            cast_w1(b + 1, 1)
+            if b >= 3:
+                collect(b - 3)
+            cast_w1(b + 1, 2)
+            quantise_w1(b + 1, 1, 2)
+            if b > 2:
+                gather(b - 1)
+            if b == last - 1:
+                back = [turn_back_first_half(pair) for pair in range(2)]
             if b + 1 < SPLIT_TILES:
                 first_stage_in_halves(b + 1)
             else:
                 first_stage(b + 1)
             if b >= 2:
-                root(b - 2)
+                closeness(b - 2)
             square(b, 1)
             scatter(b, 1)
-            if b >= 2:
-                closeness(b - 2)
-            if b >= 3:
-                collect(b - 3)
             if 4 <= b + 2 < RT:
                 cast_w1(b + 2, 0)
                 quantise_w1(b + 2, 0, 1)
-            if b == 2:
-                spread_gain()
             if b >= 2:
                 weigh(b - 2)
+            if b == last - 1:
+                for pair in range(2):
+                    lay_first_half(pair, back[pair])
+            root(b - 1)
             if b + 1 < last:
                 square(b + 1, 0)
 
-        deal_w3_words(0, "w1_raw7_1")
+        deal_w3_words(0)
         deal_w3_scales()
-        gather(last - 1)
-        square(last, 0)
-        scatter(last, 0)
-        turn_back_first_half(0)
-        turn_back_first_half(1)
-        root(last - 2)
-        collect(last - 3)
-        closeness(last - 2)
-        weigh(last - 2)
-        collect(last - 2)
-        root(last - 1)
-        square(last, 1)
-        z_codes = kept([P, M], U32, "z_codes0", "h7_0")
+        z_codes = kept([P, M], U32, "z_codes0")
         z_scales = kept([P, M], U8, "z_sc0")
         nc.vector.quantize_mx(out=z_codes[:].bitcast(FP8X4), scales=z_scales[:],
                               in_=zq[:].rearrange("p m u -> p (m u)").bitcast(BF16))
-        scatter(last, 1)
+        gather(last - 1)
+        h_last = z_t[0][:].rearrange("p c u m -> p (c u m)")[:, M:]
+        nc.scalar.activation(out=h_last, in_=d_tiles[last][2], func=ACT.Square)
+        nc.vector.tensor_tensor(pages[last][:].indirect(list2[:]), h_last, wgs_sb[:], ALU.mult)
+        closeness(last - 2)
+        collect(last - 3)
+        weigh(last - 2)
+        root(last - 1)
         closeness(last - 1)
+        collect(last - 2)
         weigh(last - 1)
         for c in range(MC):
             y_ps.append(psum.tile([P, 4, P], F32, name="y%d" % c, tag="y%d" % c))
@@ -374,7 +395,7 @@ def tile_list_substitute_closeness_page_kernel(
         y_sc = kept([P, M], U8, "y_sc")
         out_rows = out_0.rearrange("(p t) m -> p t m", t=4)
         out_words = out_1[0].rearrange("p m t -> p (m t)").bitcast(I32)
-        banks = ("spare", "d1", "turned", "d0")
+        banks = ("spare", "turned", "d1", "d0")
         xs = [kept([P, P], F32, "xl%d" % c) for c in range(MC)]
         u_last = kept([P, M], F32, "u_last", "r6")
         us = [u_last[:, P * c : P * (c + 1)] for c in range(MC)]

@@ -242,38 +242,42 @@ def tile_list_substitute_closeness_page_kernel(
             nc.scalar.activation(out=u_tiles[b], in_=x_tiles[b], func=ACT.Abs_reciprocal_sqrt, bias=1.0)
 
         def closeness(b):
-            r_tiles[b] = kept([P, M], F32, "r%d" % b, "w1_raw%d_1" % (b + 3) if b + 3 < RT else None)
-            nc.scalar.activation(out=r_tiles[b][:], in_=u_tiles[b], func=ACT.Square)
+            if b == 0:
+                r_tiles[b] = w1_raw[3][2][:, HALF:]
+            else:
+                r_tiles[b] = kept([P, M], F32, "r%d" % b, "w1_raw%d_1" % (b + 3) if b + 3 < RT else None)[:]
+            nc.scalar.activation(out=r_tiles[b], in_=u_tiles[b], func=ACT.Square)
 
         gain_sb = kept([P, RT], F32, "gain_sb")
+
+        def gain_of(b):
+            if b in (0, 4, RT - 1):
+                return gain_sb[:, b : b + 1]
+            lo = 32 * ((b - 1) % 4)
+            return z_t[(b - 1) // 4][:, 0, 0, lo : lo + 1]
 
         def spread_gain():
             gain_ps = psum.tile([P, P], F32, name="gain_ps", tag="turned")
             nc.tensor.transpose(gain_ps[:], gain_rows[:], ident_f[:])
             nc.scalar.copy(out=gain_sb[:], in_=gain_ps[:, 0:RT])
+            nc.scalar.copy(out=z_t[0][:, 0, 0, 0:96:32], in_=gain_ps[:, 1:4])
+            nc.scalar.copy(out=z_t[1][:, 0, 0, 0:64:32], in_=gain_ps[:, 5:7])
+
+        def turn(b):
+            turned[b] = psum.tile([P, MC, P], BF16, name="turned", tag=("turned", "spare")[b % 2])
+            for c in range(MC):
+                nc.tensor.transpose(turned[b][:, c, :], z_tiles[b][:, P * c : P * (c + 1)], ident_b[:])
 
         def weigh(b):
             z_tiles[b] = kept([P, M], BF16, "z%d" % b, "z%d" % (b % 2))
-            nc.scalar.activation(out=z_tiles[b][:], in_=r_tiles[b][:], func=ACT.Copy, scale=gain_sb[:, b : b + 1])
-            if b == RT - 3:
-                turned[b] = [psum.tile([P, P], BF16, name="turned_c", tag="y%d" % c)[:] for c in range(MC)]
-            else:
-                whole = psum.tile([P, MC, P], BF16, name="turned", tag="d%d" % (b % 2))
-                turned[b] = [whole[:, c, :] for c in range(MC)] + [whole[:]]
-            for c in range(MC):
-                nc.tensor.transpose(turned[b][c], z_tiles[b][:, P * c : P * (c + 1)], ident_b[:])
-
+            nc.scalar.activation(out=z_tiles[b][:], in_=r_tiles[b], func=ACT.Copy, scale=gain_of(b))
+            turn(b)
 
         def collect(b):
             lo = 32 * (b % 4)
-            if b == RT - 3:
-                for c in range(MC):
-                    nc.scalar.copy(out=z_t[1][:, c, :, lo : lo + 32],
-                                   in_=turned[b][c].bitcast(F32).rearrange("m (p u) -> m u p", u=2))
-                return
             nc.scalar.copy(
                 out=z_t[b // 4][:, :, :, lo : lo + 32],
-                in_=turned[b][MC].rearrange("m c r -> m (c r)").bitcast(F32).rearrange("m (c p u) -> m c u p", c=MC, u=2))
+                in_=turned[b][:].rearrange("m c r -> m (c r)").bitcast(F32).rearrange("m (c p u) -> m c u p", c=MC, u=2))
 
         w3_dealt = {}
 
@@ -342,22 +346,23 @@ def tile_list_substitute_closeness_page_kernel(
             if b == 2:
                 gather(b - 1)
             cast_w1(b + 1, 1)
-            if b >= 3:
-                collect(b - 3)
             cast_w1(b + 1, 2)
             quantise_w1(b + 1, 1, 2)
             if b > 2:
                 gather(b - 1)
             if b == last - 1:
+                collect(b - 3)
                 back = [turn_back_first_half(pair) for pair in range(2)]
             if b + 1 < SPLIT_TILES:
                 first_stage_in_halves(b + 1)
             else:
                 first_stage(b + 1)
-            if b >= 2:
+            if b > 2:
                 closeness(b - 2)
             square(b, 1)
             scatter(b, 1)
+            if b == 2:
+                closeness(b - 2)
             if 4 <= b + 2 < RT:
                 cast_w1(b + 2, 0)
                 quantise_w1(b + 2, 0, 1)
@@ -367,6 +372,8 @@ def tile_list_substitute_closeness_page_kernel(
                 for pair in range(2):
                     lay_first_half(pair, back[pair])
             root(b - 1)
+            if 3 <= b < last - 1:
+                collect(b - 3)
             if b + 1 < last:
                 square(b + 1, 0)
 
@@ -381,21 +388,21 @@ def tile_list_substitute_closeness_page_kernel(
         nc.scalar.activation(out=h_last, in_=d_tiles[last][2], func=ACT.Square)
         nc.vector.tensor_tensor(pages[last][:].indirect(list2[:]), h_last, wgs_sb[:], ALU.mult)
         closeness(last - 2)
-        collect(last - 3)
         weigh(last - 2)
-        root(last - 1)
-        closeness(last - 1)
-        collect(last - 2)
-        weigh(last - 1)
+        collect(last - 3)
         for c in range(MC):
             y_ps.append(psum.tile([P, 4, P], F32, name="y%d" % c, tag="y%d" % c))
             second_stage(0, c, z_codes[:, P * c : P * (c + 1)], z_scales[:, P * c : P * (c + 1)])
+        root(last - 1)
+        closeness(last - 1)
+        weigh(last - 1)
+        collect(last - 2)
 
         y_codes = kept([P, M], U32, "y_codes")
         y_sc = kept([P, M], U8, "y_sc")
         out_rows = out_0.rearrange("(p t) m -> p t m", t=4)
         out_words = out_1[0].rearrange("p m t -> p (m t)").bitcast(I32)
-        banks = ("spare", "turned", "d1", "d0")
+        banks = ("d0", "d1", "spare", "turned")
         xs = [kept([P, P], F32, "xl%d" % c) for c in range(MC)]
         u_last = kept([P, M], F32, "u_last", "r6")
         us = [u_last[:, P * c : P * (c + 1)] for c in range(MC)]
@@ -407,7 +414,7 @@ def tile_list_substitute_closeness_page_kernel(
             nc.scalar.activation(out=us[c], in_=xs[c][:], func=ACT.Abs_reciprocal_sqrt, bias=1.0)
         collect(last - 1)
         for c in range(MC):
-            nc.vector.scalar_tensor_tensor(out=zs[c][:], in0=us[c], scalar=gain_sb[:, last : last + 1], in1=us[c],
+            nc.vector.scalar_tensor_tensor(out=zs[c][:], in0=us[c], scalar=gain_of(last), in1=us[c],
                                            op0=ALU.mult, op1=ALU.mult)
             once = psum.tile([P, P], BF16, name="once", tag=banks[c])
             nc.tensor.transpose(once[:], zs[c][:], ident_b[:])

@@ -45,16 +45,13 @@ def tile_list_substitute_closeness_page_kernel(
         tab_sc = kept([P, KP * T], U8, "tab_sc")
         v_sc = kept([P, KP * S], U8, "v_sc")
         w2_lo = [sum(W2_PARTS[:i]) for i in range(len(W2_PARTS))]
-        w2_sc = [kept([P, KP * c], U8, "w2_sc%d" % i) for i, c in enumerate(W2_PARTS)]
+        w2_sc = kept([P, KP * H], U8, "w2_sc")
         w2_w = [kept([P, KP, 2 * c], U8, "w2_w%d" % i) for i, c in enumerate(W2_PARTS)]
         w3_sc = kept([P, N], U8, "w3_sc")
         gain_rows = kept([P, P], F32, "gain_rows")
-        nc.gpsimd.memset(tab_sc[:, 0 : KP * T // 2].bitcast(I32), 0)
-        nc.vector.memset(tab_sc[:, KP * T // 2 :].bitcast(I32), 0)
-        nc.vector.memset(w2_sc[0][:].bitcast(I32), 0)
+        nc.gpsimd.memset(w2_sc[:].bitcast(I32), 0)
+        nc.vector.memset(tab_sc[:].bitcast(I32), 0)
         nc.vector.memset(gain_rows[:], 0.0)
-        for part in w2_sc[1:]:
-            nc.vector.memset(part[:].bitcast(I32), 0)
         nc.vector.memset(w3_sc[:].bitcast(I32), 0)
 
         ident_f = kept([P, P], F32, "ident_f")
@@ -82,12 +79,10 @@ def tile_list_substitute_closeness_page_kernel(
             nc.sync.dma_start(out=w2_w[i][:].bitcast(I32),
                               in_=w2_words.rearrange("a p n -> p a n")[:, :, cols].bitcast(I32))
 
-        def load_w2_scales(i, queue):
-            cols = slice(w2_lo[i], w2_lo[i] + W2_PARTS[i])
+        def load_scale_rows(planes, scales):
             for r in range(4):
-                queue.dma_start(
-                    out=w2_sc[i][r:P:32, :].bitcast(I32).rearrange("q (a c) -> q a c", a=KP),
-                    in_=w2_scales[:, r:16:4, cols].rearrange("a q c -> q a c").bitcast(I32))
+                nc.sync.dma_start(out=planes[r:P:32, :].bitcast(I32).rearrange("q (a c) -> q a c", a=KP),
+                                  in_=scales[:, r:16:4, :].rearrange("a q c -> q a c").bitcast(I32))
 
         def load_page(b):
             nc.sync.dma_start(out=pages[b][:], in_=page0[P * b : P * (b + 1), :])
@@ -95,14 +90,13 @@ def tile_list_substitute_closeness_page_kernel(
         nc.sync.dma_start(list1[:], offs)
         load_tab(0)
         nc.sync.dma_start(list2[:], offs2)
-        for r in range(4):
-            nc.sync.dma_start(out=tab_sc[r:P:32, :].bitcast(I32).rearrange("q (a c) -> q a c", a=KP),
-                              in_=tab_scales[:, r:16:4, :].rearrange("a q c -> q a c").bitcast(I32))
+        nc.sync.dma_start(list3[:], offs3)
+        load_scale_rows(tab_sc, tab_scales)
+        load_scale_rows(w2_sc, w2_scales)
         load_tab(1)
         load_w1(0)
         nc.sync.dma_start(out=gain_rows[0:RT, :], in_=gain.rearrange("(b p) -> b p", p=P))
         load_w2_words(0)
-        load_w2_scales(0, nc.sync)
         warm = kept([P, 1], F32, "warm")
         nc.scalar.activation(out=warm[:], in_=ident_f[:, 0:1], func=ACT.Abs_reciprocal_sqrt, bias=1.0)
         for a in range(KP):
@@ -113,19 +107,16 @@ def tile_list_substitute_closeness_page_kernel(
         load_w1(1, (0, 1))
         nc.sync.dma_start(out=wgs_sb[:, HALF:], in_=wgs[:, HALF:])
         load_w1(1, (2,))
-        nc.sync.dma_start(list3[:], offs3)
         load_page(1)
         load_w1(2)
         load_page(2)
         load_w2_words(1)
-        load_w2_scales(1, nc.sync)
         load_w1(3)
         load_page(3)
         load_w1(4)
         load_page(4)
         load_w1(5)
         load_w2_words(2)
-        load_w2_scales(2, nc.sync)
         load_page(5)
         load_w1(6)
         load_page(6)
@@ -179,7 +170,7 @@ def tile_list_substitute_closeness_page_kernel(
             i = max(n for n in range(len(w2_lo)) if w2_lo[n] <= P * b)
             col = P * b - w2_lo[i]
             nc.tensor.matmul_mx(out=out, lhsT=w2_w[i][:, a, 2 * col : 2 * (col + P)].bitcast(FP4X4),
-                                lhsT_scale=w2_sc[i][:, a * W2_PARTS[i] + col : a * W2_PARTS[i] + col + P],
+                                lhsT_scale=w2_sc[:, a * H + P * b : a * H + P * (b + 1)],
                                 rhs=v_w[a][:, lo:hi].bitcast(FP8X4), rhs_scale=v_sc[:, a * S + lo : a * S + hi], **flags)
 
         def first_stage(b):

@@ -50,8 +50,8 @@ def tile_list_substitute_closeness_page_kernel(
         w3_sc = kept([P, N], U8, "w3_sc")
         gain_rows = kept([P, P], F32, "gain_rows")
         nc.gpsimd.memset(w2_sc[:].bitcast(I32), 0)
-        nc.vector.memset(tab_sc[:].bitcast(I32), 0)
         nc.vector.memset(gain_rows[:], 0.0)
+        nc.vector.memset(tab_sc[:].bitcast(I32), 0)
         nc.vector.memset(w3_sc[:].bitcast(I32), 0)
 
         ident_f = kept([P, P], F32, "ident_f")
@@ -91,11 +91,11 @@ def tile_list_substitute_closeness_page_kernel(
         load_tab(0)
         nc.sync.dma_start(list2[:], offs2)
         nc.sync.dma_start(list3[:], offs3)
+        nc.sync.dma_start(out=gain_rows[0:RT, :], in_=gain.rearrange("(b p) -> b p", p=P))
         load_scale_rows(tab_sc, tab_scales)
         load_scale_rows(w2_sc, w2_scales)
         load_tab(1)
         load_w1(0)
-        nc.sync.dma_start(out=gain_rows[0:RT, :], in_=gain.rearrange("(b p) -> b p", p=P))
         load_w2_words(0)
         warm = kept([P, 1], F32, "warm")
         nc.scalar.activation(out=warm[:], in_=ident_f[:, 0:1], func=ACT.Abs_reciprocal_sqrt, bias=1.0)
@@ -177,8 +177,9 @@ def tile_list_substitute_closeness_page_kernel(
             d = psum.tile([P, S], F32, name="d", tag="d%d" % (b % 2))
             for a in range(KP):
                 pass_w2(b, a, d[:], 0, S, start=(a == 0), stop=False)
-            for a in (1, 2, 0):
-                pass_w1(b, a, d[:], 0, S, start=False, stop=(a == 0))
+            order = (1, 2, 0) if b == RT - 1 else (0, 1, 2)
+            for a in order:
+                pass_w1(b, a, d[:], 0, S, start=False, stop=(a == order[-1]))
             d_tiles[b] = (d[:, 0:HALF], d[:, HALF:S], d[:])
 
         def first_stage_in_halves(b):
@@ -438,6 +439,5 @@ def tile_list_substitute_closeness_page_kernel(
             if c % 2 == 1:
                 nc.sync.dma_start(out=out_words[:, both], in_=y_codes[:, both].bitcast(I32))
         for q in range(4):
-            queue = nc.scalar if q % 2 else nc.sync
-            queue.dma_start(out=out_2[0, 4 * q : 4 * q + 4, :].bitcast(I32),
-                            in_=y_sc[32 * q : 32 * q + 4, :].bitcast(I32))
+            nc.sync.dma_start(out=out_2[0, 4 * q : 4 * q + 4, :].bitcast(I32),
+                              in_=y_sc[32 * q : 32 * q + 4, :].bitcast(I32))

@@ -186,11 +186,9 @@ def tile_list_substitute_closeness_page_kernel(
             halves = [psum.tile([P, HALF], F32, name="d_half", tag="y%d" % (2 * (b % 2) + k)) for k in range(2)]
             if b == 0:
                 order = [(which, a) for a in range(KP) for which in (2, 1)]
-            elif b == 1:
-                order = [(1, 0), (2, 0), (2, 1), (2, 2), (1, 1), (1, 2)]
             else:
-                order = [(2, 0), (2, 1), (2, 2), (1, 0), (1, 1), (1, 2)]
-            last_steps = 2
+                order = [(2, 2), (2, 1), (2, 0), (1, 0), (1, 1), (1, 2)]
+            last_steps = 3 if b == 2 else 2
             steps = [(n, k) for n in range(len(order) - last_steps) for k in range(2)]
             steps += [(n, k) for k in range(2) for n in range(len(order) - last_steps, len(order))]
             for n, k in steps:
@@ -234,10 +232,7 @@ def tile_list_substitute_closeness_page_kernel(
             nc.scalar.activation(out=u_tiles[b], in_=x_tiles[b], func=ACT.Abs_reciprocal_sqrt, bias=1.0)
 
         def closeness(b):
-            if b == 0:
-                r_tiles[b] = w1_raw[3][2][:, HALF:]
-            else:
-                r_tiles[b] = kept([P, M], F32, "r%d" % b, "w1_raw%d_1" % (b + 3) if b + 3 < RT else None)[:]
+            r_tiles[b] = kept([P, M], F32, "r%d" % b, "w1_raw%d_1" % (b + 3) if 3 < b + 3 < RT else None)[:]
             nc.scalar.activation(out=r_tiles[b], in_=u_tiles[b], func=ACT.Square)
 
         gain_sb = kept([P, RT], F32, "gain_sb")
@@ -261,7 +256,7 @@ def tile_list_substitute_closeness_page_kernel(
                 nc.tensor.transpose(turned[b][:, c, :], z_tiles[b][:, P * c : P * (c + 1)], ident_b[:])
 
         def weigh(b):
-            z_tiles[b] = kept([P, M], BF16, "z%d" % b, "z%d" % (b % 2))
+            z_tiles[b] = kept([P, M], BF16, "z%d" % b, "z%d" % (b % 2) if b else "w1_raw3_1")
             nc.scalar.activation(out=z_tiles[b][:], in_=r_tiles[b], func=ACT.Copy, scale=gain_of(b))
             turn(b)
 
@@ -318,13 +313,17 @@ def tile_list_substitute_closeness_page_kernel(
         first_stage_in_halves(0)
         square(0, 0)
         scatter(0, 0)
-        square(0, 1)
+        third = kept([P, P], F32, "h0_third")[:]
+        nc.scalar.activation(out=third, in_=d_tiles[0][1][:, 0:P], func=ACT.Square)
         cast_w1(1, 0)
         quantise_w1(1, 0, 1)
-        scatter(0, 1)
+        nc.vector.tensor_tensor(pages[0][:].indirect(list2[:, 16:24]), third, wgs_sb[:, HALF : HALF + P], ALU.mult)
         cast_w1(1, 1)
         cast_w1(1, 2)
         quantise_w1(1, 1, 2)
+        fourth = w1_raw[1][2][:, 0:P]
+        nc.scalar.activation(out=fourth, in_=d_tiles[0][1][:, P:], func=ACT.Square)
+        nc.vector.tensor_tensor(pages[0][:].indirect(list2[:, 24:32]), fourth, wgs_sb[:, HALF + P :], ALU.mult)
         gather(0)
         first_stage_in_halves(1)
 
@@ -354,11 +353,11 @@ def tile_list_substitute_closeness_page_kernel(
             square(b, 1)
             scatter(b, 1)
             if b == 2:
-                closeness(b - 2)
+                weigh(b - 2)
             if 4 <= b + 2 < RT:
                 cast_w1(b + 2, 0)
                 quantise_w1(b + 2, 0, 1)
-            if b >= 2:
+            if b > 2:
                 weigh(b - 2)
             if b == last - 1:
                 for pair in range(2):
@@ -368,9 +367,11 @@ def tile_list_substitute_closeness_page_kernel(
                 collect(b - 3)
             if b + 1 < last:
                 square(b + 1, 0)
+            if b == 1:
+                closeness(0)
 
-        deal_w3_words(0)
-        deal_w3_scales()
+        deal_w3_words(0, "w1_raw7_1")
+        deal_w3_scales("w1_s1")
         z_codes = kept([P, M], U32, "z_codes0")
         z_scales = kept([P, M], U8, "z_sc0")
         nc.vector.quantize_mx(out=z_codes[:].bitcast(FP8X4), scales=z_scales[:],

@@ -256,8 +256,11 @@ def tile_list_substitute_closeness_page_kernel(
                 nc.tensor.transpose(turned[b][:, c, :], z_tiles[b][:, P * c : P * (c + 1)], ident_b[:])
 
         def weigh(b):
-            z_tiles[b] = kept([P, M], BF16, "z%d" % b, "z%d" % (b % 2) if b else "w1_raw3_1")
-            nc.scalar.activation(out=z_tiles[b][:], in_=r_tiles[b], func=ACT.Copy, scale=gain_of(b))
+            if b == 0:
+                z_tiles[b] = w1_raw[3][2][:, HALF:S].bitcast(BF16)
+            else:
+                z_tiles[b] = kept([P, M], BF16, "z%d" % b, "z%d" % (b % 2))[:]
+            nc.scalar.activation(out=z_tiles[b], in_=r_tiles[b], func=ACT.Copy, scale=gain_of(b))
             turn(b)
 
         def collect(b):

@@ -238,7 +238,7 @@ def tile_list_substitute_closeness_page_kernel(
         gain_sb = kept([P, RT], F32, "gain_sb")
 
         def gain_of(b):
-            if b in (0, 4, RT - 1):
+            if b in (0, 4, RT - 2, RT - 1):
                 return gain_sb[:, b : b + 1]
             lo = 32 * ((b - 1) % 4)
             return z_t[(b - 1) // 4][:, 0, 0, lo : lo + 1]
@@ -248,12 +248,14 @@ def tile_list_substitute_closeness_page_kernel(
             nc.tensor.transpose(gain_ps[:], gain_rows[:], ident_f[:])
             nc.scalar.copy(out=gain_sb[:], in_=gain_ps[:, 0:RT])
             nc.scalar.copy(out=z_t[0][:, 0, 0, 0:96:32], in_=gain_ps[:, 1:4])
-            nc.scalar.copy(out=z_t[1][:, 0, 0, 0:64:32], in_=gain_ps[:, 5:7])
+            nc.scalar.copy(out=z_t[1][:, 0, 0, 0:1], in_=gain_ps[:, 5:6])
 
         def turn(b):
-            turned[b] = psum.tile([P, MC, P], BF16, name="turned", tag=("turned", "spare")[b % 2])
+            tags = ["y%d" % (2 * (b - RT + 3) + i) for i in range(2)] if b >= RT - 3 else [("turned", "spare")[b % 2]]
+            n = MC // len(tags)
+            turned[b] = [psum.tile([P, n, P], BF16, name="turned", tag=tag) for tag in tags]
             for c in range(MC):
-                nc.tensor.transpose(turned[b][:, c, :], z_tiles[b][:, P * c : P * (c + 1)], ident_b[:])
+                nc.tensor.transpose(turned[b][c // n][:, c % n, :], z_tiles[b][:, P * c : P * (c + 1)], ident_b[:])
 
         def weigh(b):
             if b == 0:
@@ -265,9 +267,11 @@ def tile_list_substitute_closeness_page_kernel(
 
         def collect(b):
             lo = 32 * (b % 4)
-            nc.scalar.copy(
-                out=z_t[b // 4][:, :, :, lo : lo + 32],
-                in_=turned[b][:].rearrange("m c r -> m (c r)").bitcast(F32).rearrange("m (c p u) -> m c u p", c=MC, u=2))
+            n = MC // len(turned[b])
+            for i, bank in enumerate(turned[b]):
+                nc.scalar.copy(
+                    out=z_t[b // 4][:, n * i : n * (i + 1), :, lo : lo + 32],
+                    in_=bank[:].rearrange("m c r -> m (c r)").bitcast(F32).rearrange("m (c p u) -> m c u p", c=n, u=2))
 
         w3_dealt = {}
 
@@ -386,36 +390,37 @@ def tile_list_substitute_closeness_page_kernel(
         closeness(last - 2)
         weigh(last - 2)
         collect(last - 3)
+        root(last - 1)
+        collect(last - 2)
+        closeness(last - 1)
+        weigh(last - 1)
+        collect(last - 1)
         for c in range(MC):
             y_ps.append(psum.tile([P, 4, P], F32, name="y%d" % c, tag="y%d" % c))
             second_stage(0, c, z_codes[:, P * c : P * (c + 1)], z_scales[:, P * c : P * (c + 1)])
-        root(last - 1)
-        closeness(last - 1)
-        weigh(last - 1)
-        collect(last - 2)
 
         y_codes = kept([P, M], U32, "y_codes")
         y_sc = kept([P, M], U8, "y_sc")
         out_rows = out_0.rearrange("(p t) m -> p t m", t=4)
         out_words = out_1[0].rearrange("p m t -> p (m t)").bitcast(I32)
         banks = ("d0", "d1", "spare", "turned")
-        xs = [kept([P, P], F32, "xl%d" % c) for c in range(MC)]
+        x_last = kept([P, M], F32, "x_last", "z%d" % ((last - 1) % 2))
+        xs = [x_last[:, P * c : P * (c + 1)] for c in range(MC)]
         u_last = kept([P, M], F32, "u_last", "r6")
         us = [u_last[:, P * c : P * (c + 1)] for c in range(MC)]
         zs = [kept([P, P], BF16, "zl%d" % c) for c in range(MC)]
         zq1 = [kept([P, P, 2], F32, "zq1_%d" % c) for c in range(MC)]
         chunks = [slice(P * c, P * (c + 1)) for c in range(MC)]
         for c in range(MC):
-            nc.vector.tensor_copy(xs[c][:], pages[last][:].indirect(list3[:, 8 * c : 8 * (c + 1)]))
-            nc.scalar.activation(out=us[c], in_=xs[c][:], func=ACT.Abs_reciprocal_sqrt, bias=1.0)
-        collect(last - 1)
+            nc.vector.tensor_copy(xs[c], pages[last][:].indirect(list3[:, 8 * c : 8 * (c + 1)]))
+            nc.scalar.activation(out=us[c], in_=xs[c], func=ACT.Abs_reciprocal_sqrt, bias=1.0)
         for c in range(MC):
             nc.vector.scalar_tensor_tensor(out=zs[c][:], in0=us[c], scalar=gain_of(last), in1=us[c],
                                            op0=ALU.mult, op1=ALU.mult)
             once = psum.tile([P, P], BF16, name="once", tag=banks[c])
             nc.tensor.transpose(once[:], zs[c][:], ident_b[:])
             nc.scalar.copy(out=z_t[1][:, c, :, 96:P], in_=once[:].bitcast(F32).rearrange("m (p u) -> m u p", u=2))
-        deal_w3_words(1, "xl%d" % (MC - 1))
+        deal_w3_words(1, "z%d" % ((last - 1) % 2))
         for c in range(MC):
             back = psum.tile([P, 2, P], F32, name="back_l", tag=banks[c])
             for pair in range(2):

@@ -45,11 +45,12 @@ def tile_list_substitute_closeness_page_kernel(
         tab_sc = kept([P, KP * T], U8, "tab_sc")
         v_sc = kept([P, KP * S], U8, "v_sc")
         w2_lo = [sum(W2_PARTS[:i]) for i in range(len(W2_PARTS))]
-        w2_sc = kept([P, KP * H], U8, "w2_sc")
+        w2_sc = [kept([P, KP * H // 2], U8, "w2_sc%d" % i) for i in range(2)]
         w2_w = [kept([P, KP, 2 * c], U8, "w2_w%d" % i) for i, c in enumerate(W2_PARTS)]
         w3_sc = kept([P, N], U8, "w3_sc")
         gain_rows = kept([P, P], F32, "gain_rows")
-        nc.gpsimd.memset(w2_sc[:].bitcast(I32), 0)
+        for planes in w2_sc:
+            nc.gpsimd.memset(planes[:].bitcast(I32), 0)
         nc.vector.memset(gain_rows[:], 0.0)
         nc.vector.memset(tab_sc[:].bitcast(I32), 0)
         nc.vector.memset(w3_sc[:].bitcast(I32), 0)
@@ -93,7 +94,7 @@ def tile_list_substitute_closeness_page_kernel(
         nc.sync.dma_start(list3[:], offs3)
         nc.sync.dma_start(out=gain_rows[0:RT, :], in_=gain.rearrange("(b p) -> b p", p=P))
         load_scale_rows(tab_sc, tab_scales)
-        load_scale_rows(w2_sc, w2_scales)
+        load_scale_rows(w2_sc[0], w2_scales[:, :, 0 : H // 2])
         load_tab(1)
         load_w1(0)
         load_w2_words(0)
@@ -113,6 +114,7 @@ def tile_list_substitute_closeness_page_kernel(
         load_w2_words(1)
         load_w1(3)
         load_page(3)
+        load_scale_rows(w2_sc[1], w2_scales[:, :, H // 2 :])
         load_w1(4)
         load_page(4)
         load_w1(5)
@@ -170,7 +172,7 @@ def tile_list_substitute_closeness_page_kernel(
             i = max(n for n in range(len(w2_lo)) if w2_lo[n] <= P * b)
             col = P * b - w2_lo[i]
             nc.tensor.matmul_mx(out=out, lhsT=w2_w[i][:, a, 2 * col : 2 * (col + P)].bitcast(FP4X4),
-                                lhsT_scale=w2_sc[:, a * H + P * b : a * H + P * (b + 1)],
+                                lhsT_scale=w2_sc[b // 4][:, a * H // 2 + P * (b % 4) : a * H // 2 + P * (b % 4 + 1)],
                                 rhs=v_w[a][:, lo:hi].bitcast(FP8X4), rhs_scale=v_sc[:, a * S + lo : a * S + hi], **flags)
 
         def first_stage(b):
@@ -404,17 +406,23 @@ def tile_list_substitute_closeness_page_kernel(
         out_rows = out_0.rearrange("(p t) m -> p t m", t=4)
         out_words = out_1[0].rearrange("p m t -> p (m t)").bitcast(I32)
         banks = ("d0", "d1", "spare", "turned")
-        x_last = kept([P, M], F32, "x_last", "z%d" % ((last - 1) % 2))
-        xs = [x_last[:, P * c : P * (c + 1)] for c in range(MC)]
+        x_last = kept([P, (MC - 1) * P], F32, "x_last", "z%d" % ((last - 1) % 2))
+        xs = [x_last[:, P * (c % (MC - 1)) : P * (c % (MC - 1) + 1)] for c in range(MC)]
         u_last = kept([P, M], F32, "u_last", "r6")
         us = [u_last[:, P * c : P * (c + 1)] for c in range(MC)]
         zs = [kept([P, P], BF16, "zl%d" % c) for c in range(MC)]
         zq1 = [kept([P, P, 2], F32, "zq1_%d" % c) for c in range(MC)]
         chunks = [slice(P * c, P * (c + 1)) for c in range(MC)]
-        for c in range(MC):
+
+        def last_root(c):
             nc.vector.tensor_copy(xs[c], pages[last][:].indirect(list3[:, 8 * c : 8 * (c + 1)]))
             nc.scalar.activation(out=us[c], in_=xs[c], func=ACT.Abs_reciprocal_sqrt, bias=1.0)
+
+        for c in range(MC - 1):
+            last_root(c)
         for c in range(MC):
+            if c == 1:
+                last_root(MC - 1)
             nc.vector.scalar_tensor_tensor(out=zs[c][:], in0=us[c], scalar=gain_of(last), in1=us[c],
                                            op0=ALU.mult, op1=ALU.mult)
             once = psum.tile([P, P], BF16, name="once", tag=banks[c])
@@ -437,7 +445,10 @@ def tile_list_substitute_closeness_page_kernel(
                 y_pair = kept([P, 4, 2 * P], F32, "y_sb%d" % c)
             y = y_pair[:, :, P * (c % 2) : P * (c % 2 + 1)]
             both = slice(P * (c - 1), P * (c + 1))
-            nc.scalar.copy(out=y, in_=y_ps[c][:])
+            if c == 1:
+                nc.vector.tensor_copy(out=y, in_=y_ps[c][:])
+            else:
+                nc.scalar.copy(out=y, in_=y_ps[c][:])
             if c % 2 == 1:
                 nc.sync.dma_start(out=out_rows[:, :, both], in_=y_pair[:])
             yb = kept([P, P, 4], BF16, "yb%d" % c)

@@ -279,8 +279,8 @@ def tile_list_substitute_closeness_page_kernel(
 
         def deal_w3_words(g, tag=None):
             w3_dealt[g] = kept([P, N], I32, "w3_dealt%d" % g, tag)
-            nc.vector.tensor_copy(out=w3_dealt[g][:].rearrange("p (t m) -> p t m", t=4),
-                                  in_=w3_w[:, g, :].rearrange("p (m t) -> p t m", t=4))
+            nc.vector.tensor_copy(out=w3_dealt[g][:].rearrange("p (t m) -> p m t", t=4),
+                                  in_=w3_w[:, g, :].rearrange("p (m t) -> p m t", t=4))
 
         def deal_w3_scales(tag=None):
             w3_dealt["scales"] = kept([P, N], U8, "w3_sp", tag)
@@ -300,7 +300,7 @@ def tile_list_substitute_closeness_page_kernel(
         zq = kept([P, M, 2], F32, "zq0")
 
         def turn_back_first_half(pair):
-            back = psum.tile([P, 2, 2, P], F32, name="back", tag="y%d" % pair)
+            back = psum.tile([P, 2, 2, P], F32, name="back", tag=("y0", "d1")[pair])
             for c in range(2):
                 for u in range(2):
                     nc.tensor.transpose(back[:, c, u, :], z_t[0][:, 2 * pair + c, u, :], ident_f[:])
@@ -352,7 +352,7 @@ def tile_list_substitute_closeness_page_kernel(
                 gather(b - 1)
             if b == last - 1:
                 collect(b - 3)
-                back = [turn_back_first_half(pair) for pair in range(2)]
+                back = turn_back_first_half(0)
             if b + 1 < SPLIT_TILES:
                 first_stage_in_halves(b + 1)
             else:
@@ -369,8 +369,7 @@ def tile_list_substitute_closeness_page_kernel(
             if b > 2:
                 weigh(b - 2)
             if b == last - 1:
-                for pair in range(2):
-                    lay_first_half(pair, back[pair])
+                lay_first_half(0, back)
             root(b - 1)
             if 3 <= b < last - 1:
                 collect(b - 3)
@@ -383,15 +382,23 @@ def tile_list_substitute_closeness_page_kernel(
         deal_w3_scales("w1_s1")
         z_codes = kept([P, M], U32, "z_codes0")
         z_scales = kept([P, M], U8, "z_sc0")
-        nc.vector.quantize_mx(out=z_codes[:].bitcast(FP8X4), scales=z_scales[:],
-                              in_=zq[:].rearrange("p m u -> p (m u)").bitcast(BF16))
+
+        def quantise_first_half(pair):
+            cols = slice(2 * P * pair, 2 * P * (pair + 1))
+            nc.vector.quantize_mx(out=z_codes[:, cols].bitcast(FP8X4), scales=z_scales[:, cols],
+                                  in_=zq[:, cols, :].rearrange("p m u -> p (m u)").bitcast(BF16))
+
+        quantise_first_half(0)
         gather(last - 1)
-        h_last = z_t[0][:].rearrange("p c u m -> p (c u m)")[:, M:]
+        h_last = kept([P, S], F32, "h_last", "w1_raw7_0")[:]
         nc.scalar.activation(out=h_last, in_=d_tiles[last][2], func=ACT.Square)
         nc.vector.tensor_tensor(pages[last][:].indirect(list2[:]), h_last, wgs_sb[:], ALU.mult)
         closeness(last - 2)
+        back = turn_back_first_half(1)
         weigh(last - 2)
         collect(last - 3)
+        lay_first_half(1, back)
+        quantise_first_half(1)
         root(last - 1)
         collect(last - 2)
         closeness(last - 1)

@@ -456,15 +456,16 @@ def tile_list_substitute_closeness_page_kernel(
                 nc.vector.tensor_copy(out=y, in_=y_ps[c][:])
             else:
                 nc.scalar.copy(out=y, in_=y_ps[c][:])
-            if c % 2 == 1:
+            if c < 2:
+                nc.sync.dma_start(out=out_rows[:, :, cols], in_=y)
+            elif c == MC - 1:
                 nc.sync.dma_start(out=out_rows[:, :, both], in_=y_pair[:])
             yb = kept([P, P, 4], BF16, "yb%d" % c)
             nc.vector.tensor_copy(out=yb[:].rearrange("p (m i) t -> p m t i", i=4),
                                   in_=y.rearrange("p t (m i) -> p m t i", i=4))
             nc.vector.quantize_mx(out=y_codes[:, cols].bitcast(FP8X4), scales=y_sc[:, cols],
                                   in_=yb[:].rearrange("p m t -> p (m t)"))
-            if c % 2 == 1:
-                nc.sync.dma_start(out=out_words[:, both], in_=y_codes[:, both].bitcast(I32))
+        nc.sync.dma_start(out=out_words, in_=y_codes[:].bitcast(I32))
         for q in range(4):
             nc.sync.dma_start(out=out_2[0, 4 * q : 4 * q + 4, :].bitcast(I32),
                               in_=y_sc[32 * q : 32 * q + 4, :].bitcast(I32))

@@ -22,7 +22,7 @@ KP = K // 512
 RT = H // P
 MC = M // P
 HALF = S // 2
-W2_PARTS = (384, 256, 384)
+W2_PARTS = (256, 384, 384)
 SPLIT_TILES = 4
 
 
@@ -43,22 +43,24 @@ def tile_list_substitute_closeness_page_kernel(
         list3 = keep.tile([P, M // 16], U16, name="list3")
 
         tab_sc = kept([P, KP * T], U8, "tab_sc")
-        v_sc = kept([P, KP * S], U8, "v_sc")
+        picked_sc = kept([P, KP * S], U8, "picked_sc")
+        staged = kept([P, 2 * KP * S], U8, "staged")
+        planes0 = kept([P, 2 * KP * S], U8, "planes0")
+        v_sc = planes0[:, 0 : KP * S]
         w2_lo = [sum(W2_PARTS[:i]) for i in range(len(W2_PARTS))]
-        w2_sc = [kept([P, KP * H // 2], U8, "w2_sc%d" % i) for i in range(2)]
+        w2_sc = [planes0[:, KP * S :], kept([P, KP * H // 2], U8, "w2_sc1")[:]]
         w2_w = [kept([P, KP, 2 * c], U8, "w2_w%d" % i) for i, c in enumerate(W2_PARTS)]
         w3_sc = kept([P, N], U8, "w3_sc")
         gain_rows = kept([P, P], F32, "gain_rows")
-        for planes in w2_sc:
-            nc.gpsimd.memset(planes[:].bitcast(I32), 0)
+        nc.vector.memset(tab_sc[0 : P - 16, :].bitcast(I32), 0)
+        nc.vector.memset(planes0[:].bitcast(I32), 0)
+        nc.vector.memset(w2_sc[1].bitcast(I32), 0)
         nc.vector.memset(gain_rows[:], 0.0)
-        nc.vector.memset(tab_sc[:].bitcast(I32), 0)
         nc.vector.memset(w3_sc[:].bitcast(I32), 0)
 
         ident_f = kept([P, P], F32, "ident_f")
         ident_b = kept([P, P], BF16, "ident_b")
         make_identity(nc, ident_f[:])
-        make_identity(nc, ident_b[:])
 
         tab_w = [kept([P, T], I32, "tab_w%d" % a) for a in range(KP)]
         pages = [kept([P, T2], F32, "page%d" % b) for b in range(RT)]
@@ -66,8 +68,9 @@ def tile_list_substitute_closeness_page_kernel(
         wgs_sb = kept([P, S], F32, "wgs_sb")
         w3_w = kept([P, 2, N], I32, "w3_w")
 
-        def load_tab(a):
-            nc.sync.dma_start(out=tab_w[a][:], in_=tab_words[a].rearrange("p t i -> p (t i)").bitcast(I32))
+        def load_tab(a, lo=0, hi=T):
+            nc.sync.dma_start(out=tab_w[a][:, lo:hi],
+                              in_=tab_words[a].rearrange("p t i -> p (t i)").bitcast(I32)[:, lo:hi])
 
         def load_w1(b, passes=range(KP)):
             for a in passes:
@@ -89,29 +92,36 @@ def tile_list_substitute_closeness_page_kernel(
             nc.sync.dma_start(out=pages[b][:], in_=page0[P * b : P * (b + 1), :])
 
         nc.sync.dma_start(list1[:], offs)
+        nc.sync.dma_start(out=tab_sc[P - 16 :, :].bitcast(I32).rearrange("q (a c) -> q a c", a=KP),
+                          in_=tab_scales.rearrange("a q c -> q a c").bitcast(I32))
+        nc.sync.dma_start(out=staged[P - 16 :, KP * S :].bitcast(I32).rearrange("q (a c) -> q a c", a=KP),
+                          in_=w2_scales[:, :, 0 : H // 2].rearrange("a q c -> q a c").bitcast(I32))
         load_tab(0)
         nc.sync.dma_start(list2[:], offs2)
-        nc.sync.dma_start(list3[:], offs3)
-        nc.sync.dma_start(out=gain_rows[0:RT, :], in_=gain.rearrange("(b p) -> b p", p=P))
-        load_scale_rows(tab_sc, tab_scales)
-        load_scale_rows(w2_sc[0], w2_scales[:, :, 0 : H // 2])
-        load_tab(1)
         load_w1(0)
+        load_tab(1)
         load_w2_words(0)
+        load_tab(2, 0, T // 2)
         warm = kept([P, 1], F32, "warm")
-        nc.scalar.activation(out=warm[:], in_=ident_f[:, 0:1], func=ACT.Abs_reciprocal_sqrt, bias=1.0)
+        nc.scalar.activation(out=warm[:], in_=gain_rows[:, 0:1], func=ACT.Abs_reciprocal_sqrt, bias=1.0)
+        nc.vector.tensor_copy(out=ident_b[:], in_=ident_f[:])
         for a in range(KP):
-            nc.vector.tensor_copy(v_sc[:, a * S : (a + 1) * S], tab_sc[:, a * T : (a + 1) * T].indirect(list1[:]))
-        load_tab(2)
-        nc.sync.dma_start(out=wgs_sb[:, 0:HALF], in_=wgs[:, 0:HALF])
+            nc.vector.tensor_copy(picked_sc[:, a * S : (a + 1) * S], tab_sc[:, a * T : (a + 1) * T].indirect(list1[:]))
+        nc.vector.tensor_copy(out=staged[96:, 0 : KP * S].bitcast(I32), in_=picked_sc[96:, :].bitcast(I32))
+        for r in range(4):
+            nc.sync.dma_start(out=planes0[r:P:32, :].bitcast(I32), in_=staged[P - 16 + r : P : 4, :].bitcast(I32))
+        load_tab(2, T // 2, T)
         load_page(0)
+        nc.sync.dma_start(out=wgs_sb[:, 0:HALF], in_=wgs[:, 0:HALF])
         load_w1(1, (0, 1))
         nc.sync.dma_start(out=wgs_sb[:, HALF:], in_=wgs[:, HALF:])
         load_w1(1, (2,))
+        nc.sync.dma_start(list3[:], offs3)
+        nc.sync.dma_start(out=gain_rows[0:RT, :], in_=gain.rearrange("(b p) -> b p", p=P))
         load_page(1)
         load_w1(2)
-        load_page(2)
         load_w2_words(1)
+        load_page(2)
         load_w1(3)
         load_page(3)
         load_scale_rows(w2_sc[1], w2_scales[:, :, H // 2 :])
@@ -130,7 +140,7 @@ def tile_list_substitute_closeness_page_kernel(
         load_page(7)
 
         z_t = [kept([P, MC, 2, P], F32, "z_t%d" % g) for g in range(2)]
-        v_w = [kept([P, S], U32, "v_w%d" % a, None) for a in range(KP)]
+        v_w = [kept([P, S], U32, "v_w%d" % a, None if a else "picked_sc") for a in range(KP)]
         grouped, w1_codes, w1_sc, d_tiles, h_tiles = {}, {}, {}, {}, {}
         x_tiles, u_tiles, r_tiles, z_tiles, turned = {}, {}, {}, {}, {}
 
@@ -184,12 +194,19 @@ def tile_list_substitute_closeness_page_kernel(
                 pass_w1(b, a, d[:], 0, S, start=False, stop=(a == order[-1]))
             d_tiles[b] = (d[:, 0:HALF], d[:, HALF:S], d[:])
 
+        def first_stage_of_tile_0():
+            quarters = [psum.tile([P, P], F32, name="d_quarter", tag=tag) for tag in ("y0", "d0", "y1", "d1")]
+            steps = [(q, a) for q in range(2) for a in range(KP - 1)] + [(q, KP - 1) for q in range(2)]
+            steps += [(q, a) for q in range(2, 4) for a in reversed(range(KP))]
+            for q, a in steps:
+                first, final = (0, KP - 1) if q < 2 else (KP - 1, 0)
+                pass_w2(0, a, quarters[q][:], P * q, P * (q + 1), start=(a == first), stop=False)
+                pass_w1(0, a, quarters[q][:], P * q, P * (q + 1), start=False, stop=(a == final))
+            d_tiles[0] = [bank[:] for bank in quarters]
+
         def first_stage_in_halves(b):
             halves = [psum.tile([P, HALF], F32, name="d_half", tag="y%d" % (2 * (b % 2) + k)) for k in range(2)]
-            if b == 0:
-                order = [(which, a) for a in range(KP) for which in (2, 1)]
-            else:
-                order = [(2, 2), (2, 1), (2, 0), (1, 0), (1, 1), (1, 2)]
+            order = [(2, 2), (2, 1), (2, 0), (1, 0), (1, 1), (1, 2)]
             last_steps = 3 if b == 2 else 2
             steps = [(n, k) for n in range(len(order) - last_steps) for k in range(2)]
             steps += [(n, k) for k in range(2) for n in range(len(order) - last_steps, len(order))]
@@ -199,9 +216,7 @@ def tile_list_substitute_closeness_page_kernel(
                 if which == 1:
                     pass_w1(b, a, halves[k][:], lo, lo + HALF, start=(n == 0), stop=(n == len(order) - 1))
                 else:
-                    for c in range(2):
-                        pass_w2(b, a, halves[k][:, P * c : P * (c + 1)], lo + P * c, lo + P * (c + 1),
-                                start=(n == 0 and c == 0), stop=False)
+                    pass_w2(b, a, halves[k][:], lo, lo + HALF, start=(n == 0), stop=False)
             d_tiles[b] = (halves[0][:], halves[1][:])
 
         def square(b, k):
@@ -311,19 +326,21 @@ def tile_list_substitute_closeness_page_kernel(
                 out=zq[:, 2 * P * pair : 2 * P * (pair + 1), :].rearrange("p (c m) u -> p c m u", c=2),
                 in_=back[:].rearrange("p c u m -> p c m u"))
 
-        spread_gain()
         for a in range(KP - 1):
             gather_table(a, 0, S)
         for a in range(KP):
             cast_w1(0, a)
             quantise_w1(0, a, 1)
-        gather_table(KP - 1, 0, HALF)
-        gather_table(KP - 1, HALF, S)
-        first_stage_in_halves(0)
-        square(0, 0)
-        scatter(0, 0)
+        for q in range(4):
+            gather_table(KP - 1, P * q, P * (q + 1))
+        first_stage_of_tile_0()
+        for q in range(2):
+            quarter = kept([P, P], F32, "h0_q%d" % q)[:]
+            nc.scalar.activation(out=quarter, in_=d_tiles[0][q], func=ACT.Square)
+            nc.vector.tensor_tensor(pages[0][:].indirect(list2[:, 8 * q : 8 * (q + 1)]), quarter,
+                                    wgs_sb[:, P * q : P * (q + 1)], ALU.mult)
         third = kept([P, P], F32, "h0_third")[:]
-        nc.scalar.activation(out=third, in_=d_tiles[0][1][:, 0:P], func=ACT.Square)
+        nc.scalar.activation(out=third, in_=d_tiles[0][2], func=ACT.Square)
         cast_w1(1, 0)
         quantise_w1(1, 0, 1)
         nc.vector.tensor_tensor(pages[0][:].indirect(list2[:, 16:24]), third, wgs_sb[:, HALF : HALF + P], ALU.mult)
@@ -331,10 +348,11 @@ def tile_list_substitute_closeness_page_kernel(
         cast_w1(1, 2)
         quantise_w1(1, 1, 2)
         fourth = w1_raw[1][2][:, 0:P]
-        nc.scalar.activation(out=fourth, in_=d_tiles[0][1][:, P:], func=ACT.Square)
+        nc.scalar.activation(out=fourth, in_=d_tiles[0][3], func=ACT.Square)
         nc.vector.tensor_tensor(pages[0][:].indirect(list2[:, 24:32]), fourth, wgs_sb[:, HALF + P :], ALU.mult)
         gather(0)
         first_stage_in_halves(1)
+        spread_gain()
 
         last = RT - 1
         square(1, 0)

@@ -189,7 +189,7 @@ def tile_list_substitute_closeness_page_kernel(
             d = psum.tile([P, S], F32, name="d", tag="d%d" % (b % 2))
             for a in range(KP):
                 pass_w2(b, a, d[:], 0, S, start=(a == 0), stop=False)
-            order = (1, 2, 0) if b == RT - 1 else (0, 1, 2)
+            order = (1, 2, 0)
             for a in order:
                 pass_w1(b, a, d[:], 0, S, start=False, stop=(a == order[-1]))
             d_tiles[b] = (d[:, 0:HALF], d[:, HALF:S], d[:])
@@ -233,6 +233,8 @@ def tile_list_substitute_closeness_page_kernel(
         def gather(b):
             if b == 1:
                 x_tiles[b] = w1_raw[3][0][:, HALF:]
+            elif b == RT - 2:
+                x_tiles[b] = kept([P, M], F32, "x6", "u5")[:]
             else:
                 x_tiles[b] = w1_raw[min(b + 2, RT - 1) if b else 1][2][:, HALF:]
             nc.vector.tensor_copy(x_tiles[b], pages[b][:].indirect(list3[:]))
@@ -243,9 +245,9 @@ def tile_list_substitute_closeness_page_kernel(
             elif b + 3 < RT:
                 u_tiles[b] = w1_raw[b + 3][0][:, HALF:]
             elif b + 2 < RT:
-                u_tiles[b] = z_t[0][:].rearrange("p c u m -> p (c u m)")[:, 0:M]
+                u_tiles[b] = kept([P, M], F32, "u%d" % b)[:]
             else:
-                u_tiles[b] = kept([P, M], F32, "u%d" % b, "r5")[:]
+                u_tiles[b] = x_tiles[b - 1]
             nc.scalar.activation(out=u_tiles[b], in_=x_tiles[b], func=ACT.Abs_reciprocal_sqrt, bias=1.0)
 
         def closeness(b):
@@ -255,20 +257,16 @@ def tile_list_substitute_closeness_page_kernel(
         gain_sb = kept([P, RT], F32, "gain_sb")
 
         def gain_of(b):
-            if b in (0, 4, RT - 2, RT - 1):
-                return gain_sb[:, b : b + 1]
-            lo = 32 * ((b - 1) % 4)
-            return z_t[(b - 1) // 4][:, 0, 0, lo : lo + 1]
+            return z_t[0][:, 0, 0, 0:1] if b == 1 else gain_sb[:, b : b + 1]
 
         def spread_gain():
             gain_ps = psum.tile([P, P], F32, name="gain_ps", tag="turned")
             nc.tensor.transpose(gain_ps[:], gain_rows[:], ident_f[:])
             nc.scalar.copy(out=gain_sb[:], in_=gain_ps[:, 0:RT])
-            nc.scalar.copy(out=z_t[0][:, 0, 0, 0:96:32], in_=gain_ps[:, 1:4])
-            nc.scalar.copy(out=z_t[1][:, 0, 0, 0:1], in_=gain_ps[:, 5:6])
+            nc.scalar.copy(out=z_t[0][:, 0, 0, 0:1], in_=gain_ps[:, 1:2])
 
         def turn(b):
-            tags = ["y%d" % (2 * (b - RT + 3) + i) for i in range(2)] if b >= RT - 3 else [("turned", "spare")[b % 2]]
+            tags = ["y2", "y3"] if b == RT - 2 else [("turned", "spare")[b % 2]]
             n = MC // len(tags)
             turned[b] = [psum.tile([P, n, P], BF16, name="turned", tag=tag) for tag in tags]
             for c in range(MC):
@@ -292,9 +290,9 @@ def tile_list_substitute_closeness_page_kernel(
 
         w3_dealt = {}
 
-        def deal_w3_words(g, tag=None):
-            w3_dealt[g] = kept([P, N], I32, "w3_dealt%d" % g, tag)
-            nc.vector.tensor_copy(out=w3_dealt[g][:].rearrange("p (t m) -> p m t", t=4),
+        def deal_w3_words(g, into):
+            w3_dealt[g] = into
+            nc.vector.tensor_copy(out=into.rearrange("p (t m) -> p m t", t=4),
                                   in_=w3_w[:, g, :].rearrange("p (m t) -> p m t", t=4))
 
         def deal_w3_scales(tag=None):
@@ -315,7 +313,7 @@ def tile_list_substitute_closeness_page_kernel(
         zq = kept([P, M, 2], F32, "zq0")
 
         def turn_back_first_half(pair):
-            back = psum.tile([P, 2, 2, P], F32, name="back", tag=("y0", "d1")[pair])
+            back = psum.tile([P, 2, 2, P], F32, name="back", tag=("y0", "y1")[pair])
             for c in range(2):
                 for u in range(2):
                     nc.tensor.transpose(back[:, c, u, :], z_t[0][:, 2 * pair + c, u, :], ident_f[:])
@@ -369,8 +367,7 @@ def tile_list_substitute_closeness_page_kernel(
             if b > 2:
                 gather(b - 1)
             if b == last - 1:
-                collect(b - 3)
-                back = turn_back_first_half(0)
+                backs = [turn_back_first_half(pair) for pair in range(2)]
             if b + 1 < SPLIT_TILES:
                 first_stage_in_halves(b + 1)
             else:
@@ -387,40 +384,44 @@ def tile_list_substitute_closeness_page_kernel(
             if b > 2:
                 weigh(b - 2)
             if b == last - 1:
-                lay_first_half(0, back)
+                lay_first_half(0, backs[0])
             root(b - 1)
-            if 3 <= b < last - 1:
-                collect(b - 3)
+            if b == last - 1:
+                lay_first_half(1, backs[1])
+                closeness(b - 1)
+                h_last = kept([P, S], F32, "h_last", "w1_raw7_0")[:]
+                nc.scalar.activation(out=h_last, in_=d_tiles[last][2], func=ACT.Square)
+                weigh(b - 1)
+            if b == 3:
+                collect(0)
             if b + 1 < last:
                 square(b + 1, 0)
+            if 3 <= b < last - 1:
+                collect(b - 2)
             if b == 1:
                 closeness(0)
 
-        deal_w3_words(0, "w1_raw7_1")
+        deal_w3_words(0, kept([P, N], I32, "w3_dealt0", "w1_raw7_1")[:])
         deal_w3_scales("w1_s1")
         z_codes = kept([P, M], U32, "z_codes0")
         z_scales = kept([P, M], U8, "z_sc0")
 
-        def quantise_first_half(pair):
-            cols = slice(2 * P * pair, 2 * P * (pair + 1))
-            nc.vector.quantize_mx(out=z_codes[:, cols].bitcast(FP8X4), scales=z_scales[:, cols],
-                                  in_=zq[:, cols, :].rearrange("p m u -> p (m u)").bitcast(BF16))
-
-        quantise_first_half(0)
+        nc.vector.quantize_mx(out=z_codes[:].bitcast(FP8X4), scales=z_scales[:],
+                              in_=zq[:].rearrange("p m u -> p (m u)").bitcast(BF16))
         gather(last - 1)
-        h_last = kept([P, S], F32, "h_last", "w1_raw7_0")[:]
-        nc.scalar.activation(out=h_last, in_=d_tiles[last][2], func=ACT.Square)
         nc.vector.tensor_tensor(pages[last][:].indirect(list2[:]), h_last, wgs_sb[:], ALU.mult)
-        closeness(last - 2)
-        back = turn_back_first_half(1)
-        weigh(last - 2)
-        collect(last - 3)
-        lay_first_half(1, back)
-        quantise_first_half(1)
         root(last - 1)
+        deal_w3_words(1, kept([P, N], I32, "w3_dealt1", "u5")[:])
+        collect(last - 3)
+        r_tiles[last - 1] = kept([P, M], F32, "r6")[:]
+        z_tiles[last - 1] = kept([P, M], BF16, "z6", "z0")[:]
+        for half in (slice(0, HALF), slice(HALF, M)):
+            nc.scalar.activation(out=r_tiles[last - 1][:, half], in_=u_tiles[last - 1][:, half], func=ACT.Square)
+        for half in (slice(0, HALF), slice(HALF, M)):
+            nc.scalar.activation(out=z_tiles[last - 1][:, half], in_=r_tiles[last - 1][:, half], func=ACT.Copy,
+                                 scale=gain_of(last - 1))
+        turn(last - 1)
         collect(last - 2)
-        closeness(last - 1)
-        weigh(last - 1)
         collect(last - 1)
         for c in range(MC):
             y_ps.append(psum.tile([P, 4, P], F32, name="y%d" % c, tag="y%d" % c))
@@ -453,7 +454,6 @@ def tile_list_substitute_closeness_page_kernel(
             once = psum.tile([P, P], BF16, name="once", tag=banks[c])
             nc.tensor.transpose(once[:], zs[c][:], ident_b[:])
             nc.scalar.copy(out=z_t[1][:, c, :, 96:P], in_=once[:].bitcast(F32).rearrange("m (p u) -> m u p", u=2))
-        deal_w3_words(1, "z%d" % ((last - 1) % 2))
         for c in range(MC):
             back = psum.tile([P, 2, P], F32, name="back_l", tag=banks[c])
             for pair in range(2):
@@ -477,7 +477,7 @@ def tile_list_substitute_closeness_page_kernel(
             if c < 2:
                 nc.sync.dma_start(out=out_rows[:, :, cols], in_=y)
             elif c == MC - 1:
-                nc.sync.dma_start(out=out_rows[:, :, both], in_=y_pair[:])
+                nc.scalar.dma_start(out=out_rows[:, :, both], in_=y_pair[:])
             yb = kept([P, P, 4], BF16, "yb%d" % c)
             nc.vector.tensor_copy(out=yb[:].rearrange("p (m i) t -> p m t i", i=4),
                                   in_=y.rearrange("p t (m i) -> p m t i", i=4))
@@ -485,5 +485,5 @@ def tile_list_substitute_closeness_page_kernel(
                                   in_=yb[:].rearrange("p m t -> p (m t)"))
         nc.sync.dma_start(out=out_words, in_=y_codes[:].bitcast(I32))
         for q in range(4):
-            nc.sync.dma_start(out=out_2[0, 4 * q : 4 * q + 4, :].bitcast(I32),
-                              in_=y_sc[32 * q : 32 * q + 4, :].bitcast(I32))
+            (nc.scalar if q % 2 else nc.sync).dma_start(out=out_2[0, 4 * q : 4 * q + 4, :].bitcast(I32),
+                                                        in_=y_sc[32 * q : 32 * q + 4, :].bitcast(I32))

@@ -161,8 +161,8 @@ def tile_list_substitute_closeness_page_kernel(
                     both = x_tiles[b - 3].bitcast(BF16).rearrange("p (a c j) -> p a c j", a=2, j=4)
                 grouped[b, 1], grouped[b, 2] = both, both[:, 1:]
             nc.scalar.activation(
-                out=grouped[b, a][:, 0].rearrange("p (c i) j -> p c j i", i=4),
-                in_=w1_raw[b][a][:, 0:S].rearrange("p (j c i) -> p c j i", j=4, i=4),
+                out=grouped[b, a][:, 0].rearrange("p (c i) j -> p c j i", i=2),
+                in_=w1_raw[b][a][:, 0:S].rearrange("p (j c i) -> p c j i", j=4, i=2),
                 func=ACT.Copy, scale=-1.0)
 
         def quantise_w1(b, a, n):

@@ -149,7 +149,7 @@ def tile_list_substitute_closeness_page_kernel(
 
         def cast_w1(b, a):
             early = ("w1_c%d" % ((b - 1) % 2), "w1_s%d" % ((b - 1) % 2))
-            tags = early if b else (None, None)
+            tags = (early[0] if b == 3 else None, early[1]) if b else (None, None)
             if a == 0 and b < 4:
                 grouped[b, 0] = kept([P, 1, P, 4], BF16, "grouped%d_0" % b, tags[0])[:]
             elif a == 0:
@@ -292,8 +292,12 @@ def tile_list_substitute_closeness_page_kernel(
 
         def deal_w3_words(g, into):
             w3_dealt[g] = into
-            nc.vector.tensor_copy(out=into.rearrange("p (t m) -> p m t", t=4),
-                                  in_=w3_w[:, g, :].rearrange("p (m t) -> p m t", t=4))
+            dealt = into.rearrange("p (t m) -> p m t", t=4)
+            words = w3_w[:, g, :].rearrange("p (m t) -> p m t", t=4)
+            if g == 0:
+                nc.scalar.copy(out=dealt.bitcast(U32), in_=words.bitcast(U32))
+            else:
+                nc.vector.tensor_copy(out=dealt, in_=words)
 
         def deal_w3_scales(tag=None):
             w3_dealt["scales"] = kept([P, N], U8, "w3_sp", tag)
@@ -401,7 +405,6 @@ def tile_list_substitute_closeness_page_kernel(
             if b == 1:
                 closeness(0)
 
-        deal_w3_words(0, kept([P, N], I32, "w3_dealt0", "w1_raw7_1")[:])
         deal_w3_scales("w1_s1")
         z_codes = kept([P, M], U32, "z_codes0")
         z_scales = kept([P, M], U8, "z_sc0")
@@ -410,6 +413,7 @@ def tile_list_substitute_closeness_page_kernel(
                               in_=zq[:].rearrange("p m u -> p (m u)").bitcast(BF16))
         gather(last - 1)
         nc.vector.tensor_tensor(pages[last][:].indirect(list2[:]), h_last, wgs_sb[:], ALU.mult)
+        deal_w3_words(0, kept([P, N], I32, "w3_dealt0", "w1_raw7_1")[:])
         root(last - 1)
         deal_w3_words(1, kept([P, N], I32, "w3_dealt1", "u5")[:])
         collect(last - 3)

@@ -294,10 +294,7 @@ def tile_list_substitute_closeness_page_kernel(
             w3_dealt[g] = into
             dealt = into.rearrange("p (t m) -> p m t", t=4)
             words = w3_w[:, g, :].rearrange("p (m t) -> p m t", t=4)
-            if g == 0:
-                nc.scalar.copy(out=dealt.bitcast(U32), in_=words.bitcast(U32))
-            else:
-                nc.vector.tensor_copy(out=dealt, in_=words)
+            nc.scalar.copy(out=dealt.bitcast(U32), in_=words.bitcast(U32))
 
         def deal_w3_scales(tag=None):
             w3_dealt["scales"] = kept([P, N], U8, "w3_sp", tag)
@@ -406,16 +403,20 @@ def tile_list_substitute_closeness_page_kernel(
                 closeness(0)
 
         deal_w3_scales("w1_s1")
-        z_codes = kept([P, M], U32, "z_codes0")
-        z_scales = kept([P, M], U8, "z_sc0")
+        z_codes, z_scales = {}, {}
 
-        nc.vector.quantize_mx(out=z_codes[:].bitcast(FP8X4), scales=z_scales[:],
-                              in_=zq[:].rearrange("p m u -> p (m u)").bitcast(BF16))
+        def quantise_first_half(pair, tag=None):
+            z_codes[pair] = kept([P, HALF], U32, "z_codes0_%d" % pair, tag)
+            z_scales[pair] = kept([P, HALF], U8, "z_sc0_%d" % pair)
+            nc.vector.quantize_mx(out=z_codes[pair][:].bitcast(FP8X4), scales=z_scales[pair][:],
+                                  in_=zq[:, HALF * pair : HALF * (pair + 1), :].rearrange("p m u -> p (m u)").bitcast(BF16))
+
+        quantise_first_half(0)
         gather(last - 1)
         nc.vector.tensor_tensor(pages[last][:].indirect(list2[:]), h_last, wgs_sb[:], ALU.mult)
         deal_w3_words(0, kept([P, N], I32, "w3_dealt0", "w1_raw7_1")[:])
         root(last - 1)
-        deal_w3_words(1, kept([P, N], I32, "w3_dealt1", "u5")[:])
+        quantise_first_half(1, "u5")
         collect(last - 3)
         r_tiles[last - 1] = kept([P, M], F32, "r6")[:]
         z_tiles[last - 1] = kept([P, M], BF16, "z6", "z0")[:]
@@ -427,9 +428,11 @@ def tile_list_substitute_closeness_page_kernel(
         turn(last - 1)
         collect(last - 2)
         collect(last - 1)
+        deal_w3_words(1, kept([P, N], I32, "w3_dealt1", "r5")[:])
         for c in range(MC):
             y_ps.append(psum.tile([P, 4, P], F32, name="y%d" % c, tag="y%d" % c))
-            second_stage(0, c, z_codes[:, P * c : P * (c + 1)], z_scales[:, P * c : P * (c + 1)])
+            cols = slice(P * (c % 2), P * (c % 2 + 1))
+            second_stage(0, c, z_codes[c // 2][:, cols], z_scales[c // 2][:, cols])
 
         y_codes = kept([P, M], U32, "y_codes")
         y_sc = kept([P, M], U8, "y_sc")

@@ -471,6 +471,12 @@ def tile_list_substitute_closeness_page_kernel(
             nc.vector.quantize_mx(out=codes[:].bitcast(FP8X4), scales=scales[:],
                                   in_=zq1[c][:].rearrange("p m u -> p (m u)").bitcast(BF16))
             second_stage(1, c, codes[:], scales[:])
+        yb = kept([P, 4 * M], BF16, "yb")
+
+        def quantise_y(lo, hi):
+            nc.vector.quantize_mx(out=y_codes[:, P * lo : P * hi].bitcast(FP8X4), scales=y_sc[:, P * lo : P * hi],
+                                  in_=yb[:, 4 * P * lo : 4 * P * hi])
+
         for c in range(MC):
             cols = chunks[c]
             if c % 2 == 0:
@@ -485,11 +491,12 @@ def tile_list_substitute_closeness_page_kernel(
                 nc.sync.dma_start(out=out_rows[:, :, cols], in_=y)
             elif c == MC - 1:
                 nc.scalar.dma_start(out=out_rows[:, :, both], in_=y_pair[:])
-            yb = kept([P, P, 4], BF16, "yb%d" % c)
-            nc.vector.tensor_copy(out=yb[:].rearrange("p (m i) t -> p m t i", i=4),
-                                  in_=y.rearrange("p t (m i) -> p m t i", i=4))
-            nc.vector.quantize_mx(out=y_codes[:, cols].bitcast(FP8X4), scales=y_sc[:, cols],
-                                  in_=yb[:].rearrange("p m t -> p (m t)"))
+            rounded = yb[:, 4 * P * c : 4 * P * (c + 1)].rearrange("p (m i t) -> p m t i", i=4, t=4)
+            nc.vector.tensor_copy(out=rounded, in_=y.rearrange("p t (m i) -> p m t i", i=4))
+            if c == 1:
+                quantise_y(0, 2)
+        quantise_y(2, 3)
+        quantise_y(3, 4)
         nc.sync.dma_start(out=out_words, in_=y_codes[:].bitcast(I32))
         for q in range(4):
             (nc.scalar if q % 2 else nc.sync).dma_start(out=out_2[0, 4 * q : 4 * q + 4, :].bitcast(I32),

@@ -189,7 +189,7 @@ def tile_list_substitute_closeness_page_kernel(
             d = psum.tile([P, S], F32, name="d", tag="d%d" % (b % 2))
             for a in range(KP):
                 pass_w2(b, a, d[:], 0, S, start=(a == 0), stop=False)
-            order = (1, 2, 0)
+            order = (0, 1, 2)
             for a in order:
                 pass_w1(b, a, d[:], 0, S, start=False, stop=(a == order[-1]))
             d_tiles[b] = (d[:, 0:HALF], d[:, HALF:S], d[:])
@@ -377,13 +377,11 @@ def tile_list_substitute_closeness_page_kernel(
                 closeness(b - 2)
             square(b, 1)
             scatter(b, 1)
-            if b == 2:
+            if b >= 2:
                 weigh(b - 2)
             if 4 <= b + 2 < RT:
                 cast_w1(b + 2, 0)
                 quantise_w1(b + 2, 0, 1)
-            if b > 2:
-                weigh(b - 2)
             if b == last - 1:
                 lay_first_half(0, backs[0])
             root(b - 1)
@@ -493,7 +491,7 @@ def tile_list_substitute_closeness_page_kernel(
                 nc.scalar.dma_start(out=out_rows[:, :, both], in_=y_pair[:])
             rounded = yb[:, 4 * P * c : 4 * P * (c + 1)].rearrange("p (m i t) -> p m t i", i=4, t=4)
             nc.vector.tensor_copy(out=rounded, in_=y.rearrange("p t (m i) -> p m t i", i=4))
-            if c == 1:
+            if c == 2:
                 quantise_y(0, 2)
         quantise_y(2, 3)
         quantise_y(3, 4)

@@ -117,10 +117,10 @@ def tile_list_substitute_closeness_page_kernel(
         nc.sync.dma_start(out=wgs_sb[:, HALF:], in_=wgs[:, HALF:])
         load_w1(1, (2,))
         nc.sync.dma_start(list3[:], offs3)
-        nc.sync.dma_start(out=gain_rows[0:RT, :], in_=gain.rearrange("(b p) -> b p", p=P))
         load_page(1)
         load_w1(2)
         load_w2_words(1)
+        nc.sync.dma_start(out=gain_rows[0:RT, :], in_=gain.rearrange("(b p) -> b p", p=P))
         load_page(2)
         load_w1(3)
         load_page(3)
@@ -260,7 +260,7 @@ def tile_list_substitute_closeness_page_kernel(
             return z_t[0][:, 0, 0, 0:1] if b == 1 else gain_sb[:, b : b + 1]
 
         def spread_gain():
-            gain_ps = psum.tile([P, P], F32, name="gain_ps", tag="turned")
+            gain_ps = psum.tile([P, P], F32, name="gain_ps", tag="y3")
             nc.tensor.transpose(gain_ps[:], gain_rows[:], ident_f[:])
             nc.scalar.copy(out=gain_sb[:], in_=gain_ps[:, 0:RT])
             nc.scalar.copy(out=z_t[0][:, 0, 0, 0:1], in_=gain_ps[:, 1:2])
@@ -351,7 +351,6 @@ def tile_list_substitute_closeness_page_kernel(
         nc.vector.tensor_tensor(pages[0][:].indirect(list2[:, 24:32]), fourth, wgs_sb[:, HALF + P :], ALU.mult)
         gather(0)
         first_stage_in_halves(1)
-        spread_gain()
 
         last = RT - 1
         square(1, 0)
@@ -391,6 +390,8 @@ def tile_list_substitute_closeness_page_kernel(
                 h_last = kept([P, S], F32, "h_last", "w1_raw7_0")[:]
                 nc.scalar.activation(out=h_last, in_=d_tiles[last][2], func=ACT.Square)
                 weigh(b - 1)
+            if b == 1:
+                spread_gain()
             if b == 3:
                 collect(0)
             if b + 1 < last:

from contextlib import ExitStack

import concourse.mybir as mybir
from concourse.masks import make_identity

K, H, N, T, S, T2, M = 1536, 1024, 512, 2048, 512, 1024, 512
FLOPS = 2 * (2 * K * H * S + H * N * M)

F32 = mybir.dt.float32
BF16 = mybir.dt.bfloat16
I32 = mybir.dt.int32
U32 = mybir.dt.uint32
U16 = mybir.dt.uint16
U8 = mybir.dt.uint8
FP8X4 = mybir.dt.float8_e4m3fn_x4
FP4X4 = mybir.dt.float4_e2m1fn_x4
ACT = mybir.ActivationFunctionType
ALU = mybir.AluOpType

P = 128
KP = K // 512
RT = H // P
MC = M // P
HALF = S // 2
W2_PARTS = (256, 384, 384)
SPLIT_TILES = 4


def tile_list_substitute_closeness_page_kernel(
    tc, tab_words, tab_scales, offs, w1, w2_words, w2_scales, wgs, page0, offs2, offs3, gain,
    w3_words, w3_scales, out_0, out_1, out_2,
):
    nc = tc.nc
    with ExitStack() as ctx:
        keep = ctx.enter_context(tc.tile_pool(name="keep", bufs=1))
        psum = ctx.enter_context(tc.psum_pool(name="psum", bufs=1))

        def kept(shape, dtype, name, tag=None):
            return keep.tile(shape, dtype, name=name, tag=tag or name, align_bytes=64)

        list1 = keep.tile([P, S // 16], U16, name="list1")
        list2 = keep.tile([P, S // 16], U16, name="list2")
        list3 = keep.tile([P, M // 16], U16, name="list3")

        tab_sc = kept([P, KP * T], U8, "tab_sc")
        picked_sc = kept([P, KP * S], U8, "picked_sc")
        staged = kept([P, 2 * KP * S], U8, "staged")
        planes0 = kept([P, 2 * KP * S], U8, "planes0")
        v_sc = planes0[:, 0 : KP * S]
        w2_lo = [sum(W2_PARTS[:i]) for i in range(len(W2_PARTS))]
        w2_sc = [planes0[:, KP * S :], kept([P, KP * H // 2], U8, "w2_sc1")[:]]
        w2_w = [kept([P, KP, 2 * c], U8, "w2_w%d" % i) for i, c in enumerate(W2_PARTS)]
        w3_sc = kept([P, N], U8, "w3_sc")
        gain_rows = kept([P, P], F32, "gain_rows")
        nc.vector.memset(tab_sc[0 : P - 16, :].bitcast(I32), 0)
        nc.vector.memset(planes0[:].bitcast(I32), 0)
        nc.vector.memset(w2_sc[1].bitcast(I32), 0)
        nc.vector.memset(gain_rows[:], 0.0)
        nc.vector.memset(w3_sc[:].bitcast(I32), 0)

        ident_f = kept([P, P], F32, "ident_f")
        ident_b = kept([P, P], BF16, "ident_b")
        make_identity(nc, ident_f[:])

        tab_w = [kept([P, T], I32, "tab_w%d" % a) for a in range(KP)]
        pages = [kept([P, T2], F32, "page%d" % b) for b in range(RT)]
        w1_raw = [[kept([P, S + HALF * (a != 1)], F32, "w1_raw%d_%d" % (b, a)) for a in range(KP)] for b in range(RT)]
        wgs_sb = kept([P, S], F32, "wgs_sb")
        w3_w = kept([P, 2, N], I32, "w3_w")

        def load_tab(a, lo=0, hi=T):
            nc.sync.dma_start(out=tab_w[a][:, lo:hi],
                              in_=tab_words[a].rearrange("p t i -> p (t i)").bitcast(I32)[:, lo:hi])

        def load_w1(b, passes=range(KP)):
            for a in passes:
                rows = w1[512 * a : 512 * (a + 1), P * b : P * (b + 1)]
                nc.sync.dma_start(out=w1_raw[b][a][:, 0:S].rearrange("p (j c) -> p j c", j=4),
                                  in_=rows.rearrange("(p j) c -> p j c", j=4))

        def load_w2_words(i):
            cols = slice(2 * w2_lo[i], 2 * (w2_lo[i] + W2_PARTS[i]))
            nc.sync.dma_start(out=w2_w[i][:].bitcast(I32),
                              in_=w2_words.rearrange("a p n -> p a n")[:, :, cols].bitcast(I32))

        def load_scale_rows(planes, scales):
            for r in range(4):
                nc.sync.dma_start(out=planes[r:P:32, :].bitcast(I32).rearrange("q (a c) -> q a c", a=KP),
                                  in_=scales[:, r:16:4, :].rearrange("a q c -> q a c").bitcast(I32))

        def load_page(b):
            nc.sync.dma_start(out=pages[b][:], in_=page0[P * b : P * (b + 1), :])

        nc.sync.dma_start(list1[:], offs)
        nc.sync.dma_start(out=tab_sc[P - 16 :, :].bitcast(I32).rearrange("q (a c) -> q a c", a=KP),
                          in_=tab_scales.rearrange("a q c -> q a c").bitcast(I32))
        nc.sync.dma_start(out=staged[P - 16 :, KP * S :].bitcast(I32).rearrange("q (a c) -> q a c", a=KP),
                          in_=w2_scales[:, :, 0 : H // 2].rearrange("a q c -> q a c").bitcast(I32))
        load_tab(0)
        nc.sync.dma_start(list2[:], offs2)
        load_w1(0)
        load_tab(1)
        load_w2_words(0)
        load_tab(2, 0, T // 2)
        warm = kept([P, 1], F32, "warm")
        nc.scalar.activation(out=warm[:], in_=gain_rows[:, 0:1], func=ACT.Abs_reciprocal_sqrt, bias=1.0)
        nc.vector.tensor_copy(out=ident_b[:], in_=ident_f[:])
        for a in range(KP):
            nc.vector.tensor_copy(picked_sc[:, a * S : (a + 1) * S], tab_sc[:, a * T : (a + 1) * T].indirect(list1[:]))
        nc.vector.tensor_copy(out=staged[96:, 0 : KP * S].bitcast(I32), in_=picked_sc[96:, :].bitcast(I32))
        for r in range(4):
            nc.sync.dma_start(out=planes0[r:P:32, :].bitcast(I32), in_=staged[P - 16 + r : P : 4, :].bitcast(I32))
        load_tab(2, T // 2, T)
        load_page(0)
        nc.sync.dma_start(out=wgs_sb[:, 0:HALF], in_=wgs[:, 0:HALF])
        load_w1(1, (0, 1))
        nc.sync.dma_start(out=wgs_sb[:, HALF:], in_=wgs[:, HALF:])
        load_w1(1, (2,))
        nc.sync.dma_start(list3[:], offs3)
        load_page(1)
        load_w1(2)
        load_w2_words(1)
        nc.sync.dma_start(out=gain_rows[0:RT, :], in_=gain.rearrange("(b p) -> b p", p=P))
        load_page(2)
        load_w1(3)
        load_page(3)
        load_scale_rows(w2_sc[1], w2_scales[:, :, H // 2 :])
        load_w1(4)
        load_page(4)
        load_w1(5)
        load_w2_words(2)
        load_page(5)
        load_w1(6)
        load_page(6)
        load_w1(7)
        nc.sync.dma_start(out=w3_w[:], in_=w3_words.rearrange("a p c i -> p a (c i)").bitcast(I32))
        for q in range(4):
            nc.sync.dma_start(out=w3_sc[32 * q : 32 * q + 8, :].bitcast(I32),
                              in_=w3_scales[:, 4 * q : 4 * q + 4, :].bitcast(I32))
        load_page(7)

        z_t = [kept([P, MC, 2, P], F32, "z_t%d" % g) for g in range(2)]
        v_w = [kept([P, S], U32, "v_w%d" % a, None if a else "picked_sc") for a in range(KP)]
        grouped, w1_codes, w1_sc, d_tiles, h_tiles = {}, {}, {}, {}, {}
        x_tiles, u_tiles, r_tiles, z_tiles, turned = {}, {}, {}, {}, {}

        def gather_table(a, lo, hi):
            nc.vector.tensor_copy(v_w[a][:, lo:hi], tab_w[a][:].bitcast(U32).indirect(list1[:, lo // 16 : hi // 16]))

        def cast_w1(b, a):
            early = ("w1_c%d" % ((b - 1) % 2), "w1_s%d" % ((b - 1) % 2))
            tags = (early[0] if b == 3 else None, early[1]) if b else (None, None)
            if a == 0 and b < 4:
                grouped[b, 0] = kept([P, 1, P, 4], BF16, "grouped%d_0" % b, tags[0])[:]
            elif a == 0:
                grouped[b, 0] = u_tiles[b - 4][:, 0:HALF].bitcast(BF16).rearrange("p (a c j) -> p a c j", a=1, j=4)
            elif a == 1:
                if b < 4:
                    both = kept([P, 2, P, 4], BF16, "grouped%d_12" % b, tags[1])[:]
                else:
                    both = x_tiles[b - 3].bitcast(BF16).rearrange("p (a c j) -> p a c j", a=2, j=4)
                grouped[b, 1], grouped[b, 2] = both, both[:, 1:]
            nc.scalar.activation(
                out=grouped[b, a][:, 0].rearrange("p (c i) j -> p c j i", i=2),
                in_=w1_raw[b][a][:, 0:S].rearrange("p (j c i) -> p c j i", j=4, i=2),
                func=ACT.Copy, scale=-1.0)

        def quantise_w1(b, a, n):
            if a == 0:
                w1_codes[b] = kept([P, KP * P], U32, "w1_c%d" % b, "w1_c%d" % (b % 2))
                w1_sc[b] = kept([P, KP * P], U8, "w1_s%d" % b, "w1_s%d" % (b % 2))
            cols = slice(P * a, P * (a + n))
            nc.vector.quantize_mx(out=w1_codes[b][:, cols].bitcast(FP8X4), scales=w1_sc[b][:, cols],
                                  in_=grouped[b, a][:, 0:n].rearrange("p a c j -> p (a c j)"))

        def pass_w1(b, a, out, lo, hi, **flags):
            cols = slice(P * a, P * (a + 1))
            nc.tensor.matmul_mx(out=out, lhsT=w1_codes[b][:, cols].bitcast(FP8X4), lhsT_scale=w1_sc[b][:, cols],
                                rhs=v_w[a][:, lo:hi].bitcast(FP8X4), rhs_scale=v_sc[:, a * S + lo : a * S + hi], **flags)

        def pass_w2(b, a, out, lo, hi, **flags):
            i = max(n for n in range(len(w2_lo)) if w2_lo[n] <= P * b)
            col = P * b - w2_lo[i]
            nc.tensor.matmul_mx(out=out, lhsT=w2_w[i][:, a, 2 * col : 2 * (col + P)].bitcast(FP4X4),
                                lhsT_scale=w2_sc[b // 4][:, a * H // 2 + P * (b % 4) : a * H // 2 + P * (b % 4 + 1)],
                                rhs=v_w[a][:, lo:hi].bitcast(FP8X4), rhs_scale=v_sc[:, a * S + lo : a * S + hi], **flags)

        def first_stage(b):
            d = psum.tile([P, S], F32, name="d", tag="d%d" % (b % 2))
            for a in range(KP):
                pass_w2(b, a, d[:], 0, S, start=(a == 0), stop=False)
            order = (0, 1, 2)
            for a in order:
                pass_w1(b, a, d[:], 0, S, start=False, stop=(a == order[-1]))
            d_tiles[b] = (d[:, 0:HALF], d[:, HALF:S], d[:])

        def first_stage_of_tile_0():
            quarters = [psum.tile([P, P], F32, name="d_quarter", tag=tag) for tag in ("y0", "d0", "y1", "d1")]
            steps = [(q, a) for q in range(2) for a in range(KP - 1)] + [(q, KP - 1) for q in range(2)]
            steps += [(q, a) for q in range(2, 4) for a in reversed(range(KP))]
            for q, a in steps:
                first, final = (0, KP - 1) if q < 2 else (KP - 1, 0)
                pass_w2(0, a, quarters[q][:], P * q, P * (q + 1), start=(a == first), stop=False)
                pass_w1(0, a, quarters[q][:], P * q, P * (q + 1), start=False, stop=(a == final))
            d_tiles[0] = [bank[:] for bank in quarters]

        def first_stage_in_halves(b):
            halves = [psum.tile([P, HALF], F32, name="d_half", tag="y%d" % (2 * (b % 2) + k)) for k in range(2)]
            order = [(2, 2), (2, 1), (2, 0), (1, 0), (1, 1), (1, 2)]
            last_steps = 3 if b == 2 else 2
            steps = [(n, k) for n in range(len(order) - last_steps) for k in range(2)]
            steps += [(n, k) for k in range(2) for n in range(len(order) - last_steps, len(order))]
            for n, k in steps:
                which, a = order[n]
                lo = k * HALF
                if which == 1:
                    pass_w1(b, a, halves[k][:], lo, lo + HALF, start=(n == 0), stop=(n == len(order) - 1))
                else:
                    pass_w2(b, a, halves[k][:], lo, lo + HALF, start=(n == 0), stop=False)
            d_tiles[b] = (halves[0][:], halves[1][:])

        def square(b, k):
            if b >= (3, 1)[k]:
                h_tiles[b, k] = w1_raw[b + 1][2 * k][:, 0:HALF]
            else:
                h_tiles[b, k] = kept([P, HALF], F32, "h%d_%d" % (b, k))[:]
            nc.scalar.activation(out=h_tiles[b, k], in_=d_tiles[b][k], func=ACT.Square)

        def scatter(b, k):
            nc.vector.tensor_tensor(pages[b][:].indirect(list2[:, 16 * k : 16 * (k + 1)]), h_tiles[b, k],
                                    wgs_sb[:, k * HALF : (k + 1) * HALF], ALU.mult)

        def gather(b):
            if b == 1:
                x_tiles[b] = w1_raw[3][0][:, HALF:]
            elif b == RT - 2:
                x_tiles[b] = kept([P, M], F32, "x6", "u5")[:]
            else:
                x_tiles[b] = w1_raw[min(b + 2, RT - 1) if b else 1][2][:, HALF:]
            nc.vector.tensor_copy(x_tiles[b], pages[b][:].indirect(list3[:]))

        def root(b):
            if b == 0:
                u_tiles[b] = w1_raw[2][2][:, HALF:]
            elif b + 3 < RT:
                u_tiles[b] = w1_raw[b + 3][0][:, HALF:]
            elif b + 2 < RT:
                u_tiles[b] = kept([P, M], F32, "u%d" % b)[:]
            else:
                u_tiles[b] = x_tiles[b - 1]
            nc.scalar.activation(out=u_tiles[b], in_=x_tiles[b], func=ACT.Abs_reciprocal_sqrt, bias=1.0)

        def closeness(b):
            r_tiles[b] = kept([P, M], F32, "r%d" % b, "w1_raw%d_1" % (b + 3) if 3 < b + 3 < RT else None)[:]
            nc.scalar.activation(out=r_tiles[b], in_=u_tiles[b], func=ACT.Square)

        gain_sb = kept([P, RT], F32, "gain_sb")

        def gain_of(b):
            return z_t[0][:, 0, 0, 0:1] if b == 1 else gain_sb[:, b : b + 1]

        def spread_gain():
            gain_ps = psum.tile([P, P], F32, name="gain_ps", tag="y3")
            nc.tensor.transpose(gain_ps[:], gain_rows[:], ident_f[:])
            nc.scalar.copy(out=gain_sb[:], in_=gain_ps[:, 0:RT])
            nc.scalar.copy(out=z_t[0][:, 0, 0, 0:1], in_=gain_ps[:, 1:2])

        def turn(b):
            tags = ["y2", "y3"] if b == RT - 2 else [("turned", "spare")[b % 2]]
            n = MC // len(tags)
            turned[b] = [psum.tile([P, n, P], BF16, name="turned", tag=tag) for tag in tags]
            for c in range(MC):
                nc.tensor.transpose(turned[b][c // n][:, c % n, :], z_tiles[b][:, P * c : P * (c + 1)], ident_b[:])

        def weigh(b):
            if b == 0:
                z_tiles[b] = w1_raw[3][2][:, HALF:S].bitcast(BF16)
            else:
                z_tiles[b] = kept([P, M], BF16, "z%d" % b, "z%d" % (b % 2))[:]
            nc.scalar.activation(out=z_tiles[b], in_=r_tiles[b], func=ACT.Copy, scale=gain_of(b))
            turn(b)

        def collect(b):
            lo = 32 * (b % 4)
            n = MC // len(turned[b])
            for i, bank in enumerate(turned[b]):
                nc.scalar.copy(
                    out=z_t[b // 4][:, n * i : n * (i + 1), :, lo : lo + 32],
                    in_=bank[:].rearrange("m c r -> m (c r)").bitcast(F32).rearrange("m (c p u) -> m c u p", c=n, u=2))

        w3_dealt = {}

        def deal_w3_words(g, into):
            w3_dealt[g] = into
            dealt = into.rearrange("p (t m) -> p m t", t=4)
            words = w3_w[:, g, :].rearrange("p (m t) -> p m t", t=4)
            nc.scalar.copy(out=dealt.bitcast(U32), in_=words.bitcast(U32))

        def deal_w3_scales(tag=None):
            w3_dealt["scales"] = kept([P, N], U8, "w3_sp", tag)
            nc.vector.tensor_copy(out=w3_dealt["scales"][:].rearrange("p (t m) -> p t m", t=4),
                                  in_=w3_sc[:].rearrange("p (m t) -> p t m", t=4))

        y_ps = []

        def second_stage(g, c, codes, scales):
            for t in range(4):
                nc.tensor.matmul_mx(
                    out=y_ps[c][:, t, :], lhsT=w3_dealt[g][:, P * t : P * (t + 1)].bitcast(FP8X4),
                    lhsT_scale=w3_dealt["scales"][4 * g :, P * t : P * (t + 1)],
                    rhs=codes.bitcast(FP8X4), rhs_scale=scales,
                    start=(g == 0 and t == 0), stop=(g == 1 and t == 3))

        zq = kept([P, M, 2], F32, "zq0")

        def turn_back_first_half(pair):
            back = psum.tile([P, 2, 2, P], F32, name="back", tag=("y0", "y1")[pair])
            for c in range(2):
                for u in range(2):
                    nc.tensor.transpose(back[:, c, u, :], z_t[0][:, 2 * pair + c, u, :], ident_f[:])
            return back

        def lay_first_half(pair, back):
            nc.scalar.copy(
                out=zq[:, 2 * P * pair : 2 * P * (pair + 1), :].rearrange("p (c m) u -> p c m u", c=2),
                in_=back[:].rearrange("p c u m -> p c m u"))

        for a in range(KP - 1):
            gather_table(a, 0, S)
        for a in range(KP):
            cast_w1(0, a)
            quantise_w1(0, a, 1)
        for q in range(4):
            gather_table(KP - 1, P * q, P * (q + 1))
        first_stage_of_tile_0()
        for q in range(2):
            quarter = kept([P, P], F32, "h0_q%d" % q)[:]
            nc.scalar.activation(out=quarter, in_=d_tiles[0][q], func=ACT.Square)
            nc.vector.tensor_tensor(pages[0][:].indirect(list2[:, 8 * q : 8 * (q + 1)]), quarter,
                                    wgs_sb[:, P * q : P * (q + 1)], ALU.mult)
        third = kept([P, P], F32, "h0_third")[:]
        nc.scalar.activation(out=third, in_=d_tiles[0][2], func=ACT.Square)
        cast_w1(1, 0)
        quantise_w1(1, 0, 1)
        nc.vector.tensor_tensor(pages[0][:].indirect(list2[:, 16:24]), third, wgs_sb[:, HALF : HALF + P], ALU.mult)
        cast_w1(1, 1)
        cast_w1(1, 2)
        quantise_w1(1, 1, 2)
        fourth = w1_raw[1][2][:, 0:P]
        nc.scalar.activation(out=fourth, in_=d_tiles[0][3], func=ACT.Square)
        nc.vector.tensor_tensor(pages[0][:].indirect(list2[:, 24:32]), fourth, wgs_sb[:, HALF + P :], ALU.mult)
        gather(0)
        first_stage_in_halves(1)

        last = RT - 1
        square(1, 0)
        for b in range(1, last):
            scatter(b, 0)
            if b + 1 < 4:
                cast_w1(b + 1, 0)
                quantise_w1(b + 1, 0, 1)
            if b == 2:
                gather(b - 1)
            cast_w1(b + 1, 1)
            cast_w1(b + 1, 2)
            quantise_w1(b + 1, 1, 2)
            if b > 2:
                gather(b - 1)
            if b == last - 1:
                backs = [turn_back_first_half(pair) for pair in range(2)]
            if b + 1 < SPLIT_TILES:
                first_stage_in_halves(b + 1)
            else:
                first_stage(b + 1)
            if b > 2:
                closeness(b - 2)
            square(b, 1)
            scatter(b, 1)
            if b >= 2:
                weigh(b - 2)
            if 4 <= b + 2 < RT:
                cast_w1(b + 2, 0)
                quantise_w1(b + 2, 0, 1)
            if b == last - 1:
                lay_first_half(0, backs[0])
            root(b - 1)
            if b == last - 1:
                lay_first_half(1, backs[1])
                closeness(b - 1)
                h_last = kept([P, S], F32, "h_last", "w1_raw7_0")[:]
                nc.scalar.activation(out=h_last, in_=d_tiles[last][2], func=ACT.Square)
                weigh(b - 1)
            if b == 1:
                spread_gain()
            if b == 3:
                collect(0)
            if b + 1 < last:
                square(b + 1, 0)
            if 3 <= b < last - 1:
                collect(b - 2)
            if b == 1:
                closeness(0)

        deal_w3_scales("w1_s1")
        z_codes, z_scales = {}, {}

        def quantise_first_half(pair, tag=None):
            z_codes[pair] = kept([P, HALF], U32, "z_codes0_%d" % pair, tag)
            z_scales[pair] = kept([P, HALF], U8, "z_sc0_%d" % pair)
            nc.vector.quantize_mx(out=z_codes[pair][:].bitcast(FP8X4), scales=z_scales[pair][:],
                                  in_=zq[:, HALF * pair : HALF * (pair + 1), :].rearrange("p m u -> p (m u)").bitcast(BF16))

        quantise_first_half(0)
        gather(last - 1)
        nc.vector.tensor_tensor(pages[last][:].indirect(list2[:]), h_last, wgs_sb[:], ALU.mult)
        deal_w3_words(0, kept([P, N], I32, "w3_dealt0", "w1_raw7_1")[:])
        root(last - 1)
        quantise_first_half(1, "u5")
        collect(last - 3)
        r_tiles[last - 1] = kept([P, M], F32, "r6")[:]
        z_tiles[last - 1] = kept([P, M], BF16, "z6", "z0")[:]
        for half in (slice(0, HALF), slice(HALF, M)):
            nc.scalar.activation(out=r_tiles[last - 1][:, half], in_=u_tiles[last - 1][:, half], func=ACT.Square)
        for half in (slice(0, HALF), slice(HALF, M)):
            nc.scalar.activation(out=z_tiles[last - 1][:, half], in_=r_tiles[last - 1][:, half], func=ACT.Copy,
                                 scale=gain_of(last - 1))
        turn(last - 1)
        collect(last - 2)
        collect(last - 1)
        deal_w3_words(1, kept([P, N], I32, "w3_dealt1", "r5")[:])
        for c in range(MC):
            y_ps.append(psum.tile([P, 4, P], F32, name="y%d" % c, tag="y%d" % c))
            cols = slice(P * (c % 2), P * (c % 2 + 1))
            second_stage(0, c, z_codes[c // 2][:, cols], z_scales[c // 2][:, cols])

        y_codes = kept([P, M], U32, "y_codes")
        y_sc = kept([P, M], U8, "y_sc")
        out_rows = out_0.rearrange("(p t) m -> p t m", t=4)
        out_words = out_1[0].rearrange("p m t -> p (m t)").bitcast(I32)
        banks = ("d0", "d1", "spare", "turned")
        x_last = kept([P, (MC - 1) * P], F32, "x_last", "z%d" % ((last - 1) % 2))
        xs = [x_last[:, P * (c % (MC - 1)) : P * (c % (MC - 1) + 1)] for c in range(MC)]
        u_last = kept([P, M], F32, "u_last", "r6")
        us = [u_last[:, P * c : P * (c + 1)] for c in range(MC)]
        zs = [kept([P, P], BF16, "zl%d" % c) for c in range(MC)]
        zq1 = [kept([P, P, 2], F32, "zq1_%d" % c) for c in range(MC)]
        chunks = [slice(P * c, P * (c + 1)) for c in range(MC)]

        def last_root(c):
            nc.vector.tensor_copy(xs[c], pages[last][:].indirect(list3[:, 8 * c : 8 * (c + 1)]))
            nc.scalar.activation(out=us[c], in_=xs[c], func=ACT.Abs_reciprocal_sqrt, bias=1.0)

        for c in range(MC - 1):
            last_root(c)
        for c in range(MC):
            if c == 1:
                last_root(MC - 1)
            nc.vector.scalar_tensor_tensor(out=zs[c][:], in0=us[c], scalar=gain_of(last), in1=us[c],
                                           op0=ALU.mult, op1=ALU.mult)
            once = psum.tile([P, P], BF16, name="once", tag=banks[c])
            nc.tensor.transpose(once[:], zs[c][:], ident_b[:])
            nc.scalar.copy(out=z_t[1][:, c, :, 96:P], in_=once[:].bitcast(F32).rearrange("m (p u) -> m u p", u=2))
        for c in range(MC):
            back = psum.tile([P, 2, P], F32, name="back_l", tag=banks[c])
            for pair in range(2):
                nc.tensor.transpose(back[:, pair, :], z_t[1][:, c, pair, :], ident_f[:])
            nc.scalar.copy(out=zq1[c][:], in_=back[:].rearrange("p u m -> p m u"))
            codes = kept([P, P], U32, "z_codes1_%d" % c)
            scales = kept([P, P], U8, "z_sc1_%d" % c)
            nc.vector.quantize_mx(out=codes[:].bitcast(FP8X4), scales=scales[:],
                                  in_=zq1[c][:].rearrange("p m u -> p (m u)").bitcast(BF16))
            second_stage(1, c, codes[:], scales[:])
        yb = kept([P, 4 * M], BF16, "yb")

        def quantise_y(lo, hi):
            nc.vector.quantize_mx(out=y_codes[:, P * lo : P * hi].bitcast(FP8X4), scales=y_sc[:, P * lo : P * hi],
                                  in_=yb[:, 4 * P * lo : 4 * P * hi])

        for c in range(MC):
            cols = chunks[c]
            if c % 2 == 0:
                y_pair = kept([P, 4, 2 * P], F32, "y_sb%d" % c)
            y = y_pair[:, :, P * (c % 2) : P * (c % 2 + 1)]
            both = slice(P * (c - 1), P * (c + 1))
            if c == 1:
                nc.vector.tensor_copy(out=y, in_=y_ps[c][:])
            else:
                nc.scalar.copy(out=y, in_=y_ps[c][:])
            if c < 2:
                nc.sync.dma_start(out=out_rows[:, :, cols], in_=y)
            elif c == MC - 1:
                nc.scalar.dma_start(out=out_rows[:, :, both], in_=y_pair[:])
            rounded = yb[:, 4 * P * c : 4 * P * (c + 1)].rearrange("p (m i t) -> p m t i", i=4, t=4)
            nc.vector.tensor_copy(out=rounded, in_=y.rearrange("p t (m i) -> p m t i", i=4))
            if c == 2:
                quantise_y(0, 2)
        quantise_y(2, 3)
        quantise_y(3, 4)
        nc.sync.dma_start(out=out_words, in_=y_codes[:].bitcast(I32))
        for q in range(4):
            (nc.scalar if q % 2 else nc.sync).dma_start(out=out_2[0, 4 * q : 4 * q + 4, :].bitcast(I32),
                                                        in_=y_sc[32 * q : 32 * q + 4, :].bitcast(I32))
